import numpy as np
import ml_dtypes


def mxq(x, axis, fmt="e4m3"):
    dtype, down = {"e4m3": (ml_dtypes.float8_e4m3fn, 7), "e5m2": (ml_dtypes.float8_e5m2, 14)}[fmt]
    v = np.moveaxis(np.asarray(x, np.float32).astype(ml_dtypes.bfloat16).astype(np.float64), axis, -1)
    blocks = v.reshape(v.shape[:-1] + (-1, 32))
    amax = np.abs(blocks).max(-1, keepdims=True)
    byte = np.maximum(np.where(amax > 0, np.frexp(amax)[1] - 1 + 127, 0) - down, 1)
    scale = np.exp2(byte - 127.0)
    codes = (blocks / scale).astype(np.float32).astype(dtype).astype(np.float64)
    return np.moveaxis((codes * scale).reshape(v.shape), -1, axis)


WIDE = False


def mx_kscale(k):
    if not WIDE:
        return np.ones(k)
    levels = np.array([10, -10, 5, -5, 0])
    if k % 512:
        return np.exp2(np.random.permutation(np.resize(levels, k // 32))).repeat(32)
    a = np.empty((k // 512, 16))
    for p in range(k // 512):
        a[p, :8] = np.random.permutation(np.resize(levels, 8))
        for g in range(8):
            far = levels[np.abs(levels - a[p, g]) >= 10]
            a[p, g + 8] = far[np.random.randint(len(far))]
    return np.exp2(a.ravel()).repeat(32)


def f64(x):
    return np.asarray(x).astype(np.float64)


def striped(idx):
    return np.tile(idx.reshape(-1, 16).T, (8, 1)).astype(np.uint16)


def unstriped(offs):
    return offs[:16].T.reshape(-1).astype(np.int64)


E2M1 = np.array([0.0, 0.5, 1.0, 1.5, 2.0, 3.0, 4.0, 6.0, -0.0, -0.5, -1.0, -1.5, -2.0, -3.0, -4.0, -6.0])


def pack_weight(w, fmt):
    k, n = w.shape
    w = f64(np.asarray(w, np.float32).astype(ml_dtypes.bfloat16)).reshape(k // 32, 32, n)
    amax = np.abs(w).max(1)
    if fmt == "e4m3":
        byte = np.frexp(amax)[1] - 1 + 127 - 7
    else:
        mant, ex = np.frexp(amax / 6.0)
        byte = np.where(mant > 0.5, ex, ex - 1) + 127
    byte = np.clip(np.where(amax > 0, byte, 1), 1, 254)
    scaled = (w * np.exp2(127.0 - byte)[:, None, :]).reshape(k, n).astype(np.float32)
    by_word = np.ascontiguousarray(scaled.reshape(k // 512, 128, 4, n).transpose(0, 1, 3, 2))
    if fmt == "e4m3":
        words = by_word.astype(ml_dtypes.float8_e4m3fn).view(np.uint8)
    else:
        c = by_word.astype(ml_dtypes.float4_e2m1fn).view(np.uint8) & 0xF
        words = (c[..., 0::2] | (c[..., 1::2] << 4)).reshape(k // 512, 128, 2 * n)
    return np.ascontiguousarray(words), np.ascontiguousarray(byte.astype(np.uint8).reshape(k // 512, 16, n))


def unpack_weight(words, scales, fmt):
    g, _, n = scales.shape
    words = np.ascontiguousarray(words).reshape(g, 128, n, -1)
    if fmt == "e4m3":
        vals = words.view(ml_dtypes.float8_e4m3fn).astype(np.float64)
    else:
        nib = np.empty((g, 128, n, 4), np.uint8)
        nib[..., 0::2] = words & 0xF
        nib[..., 1::2] = words >> 4
        vals = E2M1[nib]
    vals = vals * np.repeat(np.exp2(scales.astype(np.float64) - 127.0), 8, axis=1)[..., None]
    return vals.transpose(0, 1, 3, 2).reshape(g * 512, n)


def gelu(v):
    return 0.5 * v * (1.0 + np.tanh(np.sqrt(2.0 / np.pi) * (v + 0.044715 * v**3)))


K, T, S, H, N = 1024, 2048, 1024, 1024, 512

def setup_inputs():
    n = np.random.standard_normal
    s = mx_kscale(K)[:, None]
    u = mx_kscale(H)[:, None]
    tab_words, tab_scales = pack_weight(n((K, T)) * s, "e4m3")
    w2_words, w2_scales = pack_weight(1.3 * n((H, N)) / np.sqrt(H) / u, "e2m1")
    w3_words, w3_scales = pack_weight(n((K, N)) / np.sqrt(K) / s, "e4m3")
    return {
        "tab_words": tab_words, "tab_scales": tab_scales,
        "offs": striped(np.random.permutation(T)[:S]),
        "gT": n((N, T)).astype(np.float32),
        "w1": (n((K, H)) / np.sqrt(K) / s).astype(np.float32),
        "gain": (np.random.uniform(0.5, 1.5, H) * u[:, 0]).astype(np.float32),
        "w2_words": w2_words, "w2_scales": w2_scales,
        "w3_words": w3_words, "w3_scales": w3_scales,
    }

def reference(tab_words, tab_scales, offs, gT, w1, gain, w2_words, w2_scales, w3_words, w3_scales):
    v = unpack_weight(tab_words, tab_scales, "e4m3")[:, unstriped(offs)]
    g = f64(gT)[:, unstriped(offs)]
    a = mxq(f64(w1), 0, "e4m3").T @ v
    h = f64(gain)[:, None] * np.tanh(a)
    w2 = unpack_weight(w2_words, w2_scales, "e2m1")
    y = w2.T @ mxq(h, 0, "e4m3")
    w3 = unpack_weight(w3_words, w3_scales, "e4m3")
    d = w3.T @ v
    new = g + y * d
    out = f64(gT).copy()
    out[:, unstriped(offs)] = new
    return out

@@ -1,0 +1,226 @@
+from contextlib import ExitStack
+
+import concourse.mybir as mybir
+
+K, T, S, H, N = 1024, 2048, 1024, 1024, 512
+FLOPS = 2 * S * (K * H + H * N + K * N)
+
+F32 = mybir.dt.float32
+BF16 = mybir.dt.bfloat16
+I32 = mybir.dt.int32
+U32 = mybir.dt.uint32
+U16 = mybir.dt.uint16
+U8 = mybir.dt.uint8
+E4M3 = mybir.dt.float8_e4m3fn_x4
+E2M1 = mybir.dt.float4_e2m1fn_x4
+MULT = mybir.AluOpType.mult
+ADD = mybir.AluOpType.add
+TANH = mybir.ActivationFunctionType.Tanh
+COPY = mybir.ActivationFunctionType.Copy
+
+P = 128
+PACK = 4
+PASS = P * PACK
+PASSES = K // PASS
+BANK = 512
+ROW_TILES = N // P
+PER_COLUMN = 16
+GATHER = 256
+SLICES = (128, 128, 256, 256, 256)
+CAST_ON_VECTOR = (0, 64, 128, 128)
+
+
+def tile_list_sense_drift_rewrite_kernel(
+    tc, tab_words, tab_scales, offs, gT, w1, gain, w2_words, w2_scales, w3_words, w3_scales, out
+):
+    nc = tc.nc
+    with ExitStack() as ctx:
+        keep = ctx.enter_context(tc.tile_pool(name="keep", bufs=1))
+        ring = ctx.enter_context(tc.tile_pool(name="ring", bufs=3))
+        psum = ctx.enter_context(tc.psum_pool(name="psum", bufs=2))
+
+        offsets = keep.tile([P, S // PER_COLUMN], U16, name="offsets")
+        nc.sync.dma_start(offsets[:], offs)
+
+        def listed(first, count):
+            return offsets[:, first // PER_COLUMN : (first + count) // PER_COLUMN]
+
+        tab_plane = keep.tile([P, T], U8, name="tab_plane", align_bytes=64)
+        nc.gpsimd.memset(tab_plane[:].bitcast(I32), 0)
+        tab = [keep.tile([P, T], U32, name="tab%d" % a, align_bytes=64) for a in range(PASSES)]
+        nc.sync.dma_start(tab[0][:].bitcast(I32), tab_words[0].rearrange("p t i -> p (t i)").bitcast(I32))
+        for q in range(4):
+            nc.sync.dma_start(
+                tab_plane[32 * q : 32 * q + 4 * PASSES, :].bitcast(I32),
+                tab_scales[:, 4 * q : 4 * q + 4, :].bitcast(I32),
+            )
+        nc.sync.dma_start(tab[1][:].bitcast(I32), tab_words[1].rearrange("p t i -> p (t i)").bitcast(I32))
+
+        def load_plane(scales, name):
+            plane = keep.tile([P, PASSES, N], U8, name=name, align_bytes=64)
+            nc.gpsimd.memset(plane[:].bitcast(I32), 0)
+            for q in range(4):
+                nc.sync.dma_start(
+                    plane[32 * q : 32 * q + 4, :, :].bitcast(I32),
+                    scales[:, 4 * q : 4 * q + 4, :].rearrange("a q c -> q a c").bitcast(I32),
+                )
+            return plane
+
+        def load_w1(b, a):
+            raw = keep.tile([P, PACK, PASS], F32, name="w1_raw%d%d" % (b, a))
+            nc.sync.dma_start(
+                raw[:],
+                w1[a * PASS : (a + 1) * PASS, b * PASS : (b + 1) * PASS].rearrange("(p j) c -> p j c", j=PACK),
+            )
+            return raw
+
+        w1_raw = {}
+        gains = keep.tile([P, PASSES, PACK], F32, name="gains")
+        nc.sync.dma_start(gains[:], gain.rearrange("(b p t) -> p b t", b=PASSES, t=PACK))
+        w3_plane = load_plane(w3_scales, "w3_plane")
+        w1_raw[0, 0] = load_w1(0, 0)
+        w2_plane = load_plane(w2_scales, "w2_plane")
+        w1_raw[0, 1] = load_w1(0, 1)
+        w1_raw[1, 0] = load_w1(1, 0)
+        w1_raw[1, 1] = load_w1(1, 1)
+        state = [keep.tile([P, T], F32, name="state%d" % n) for n in range(ROW_TILES)]
+        w3_codes = keep.tile([P, PASSES, N], U32, name="w3_codes", align_bytes=64)
+        nc.sync.dma_start(w3_codes[:].bitcast(I32), w3_words.rearrange("a p c i -> p a (c i)").bitcast(I32))
+        w2_codes = keep.tile([P, PASSES, 2 * N], U8, name="w2_codes", align_bytes=64)
+        nc.sync.dma_start(w2_codes[:].bitcast(I32), w2_words.rearrange("a p c -> p a c").bitcast(I32))
+        for n in range(ROW_TILES):
+            nc.sync.dma_start(state[n][:], gT[n * P : (n + 1) * P, :])
+
+        v_plane = keep.tile([P, S], U8, name="v_plane", align_bytes=64)
+        nc.vector.tensor_copy(v_plane[:], tab_plane[:].indirect(offsets[:]))
+        v_codes = [keep.tile([P, S], U32, name="v_codes%d" % a, align_bytes=64) for a in range(PASSES)]
+        for a in range(PASSES):
+            nc.vector.tensor_copy(v_codes[a][:], tab[a][:].indirect(offsets[:]))
+
+        w1_codes, w1_plane = {}, {}
+        for b in range(PASSES):
+            for a in range(PASSES):
+                grouped = keep.tile([P, PACK * PASS], BF16, name="w1_grouped%d%d" % (b, a), align_bytes=64)
+                dst = grouped[:].rearrange("p (t m j) -> p m j t", t=PACK, j=PACK)
+                src = w1_raw[b, a][:].rearrange("p j (m t) -> p m j t", t=PACK)
+                split = CAST_ON_VECTOR[PASSES * b + a]
+                if split > 0:
+                    nc.vector.tensor_copy(dst[:, :split], src[:, :split])
+                if split < P:
+                    nc.scalar.copy(dst[:, split:], src[:, split:])
+                w1_codes[b, a] = keep.tile([P, PASS], U32, name="w1_codes%d%d" % (b, a), align_bytes=64)
+                w1_plane[b, a] = keep.tile([P, PASS], U8, name="w1_plane%d%d" % (b, a), align_bytes=64)
+                nc.vector.quantize_mx(w1_codes[b, a][:].bitcast(E4M3), w1_plane[b, a][:], grouped[:])
+
+        def times_table(acc, codes, planes, cols):
+            for a in range(PASSES):
+                nc.tensor.matmul_mx(
+                    acc,
+                    lhsT=codes[a].bitcast(E4M3),
+                    lhsT_scale=planes[a],
+                    rhs=v_codes[a][:, cols].bitcast(E4M3),
+                    rhs_scale=v_plane[4 * a :, cols],
+                    start=(a == 0),
+                    stop=(a == PASSES - 1),
+                )
+
+        first = 0
+        for s, width in enumerate(SLICES):
+            cols = slice(first, first + width)
+            per_bank = BANK // width
+            h_grouped = keep.tile([P, PASSES, width * PACK], BF16, name="h_grouped", tag="slice%d" % s, align_bytes=64)
+            h_codes = keep.tile([P, PASSES * width], U32, name="h_codes%d" % s, align_bytes=64)
+            h_plane = keep.tile([P, PASSES * width], U8, name="h_plane%d" % s, align_bytes=64)
+            for b in range(PASSES):
+                short_way = s == 0 and b == PASSES - 1
+                if not short_way:
+                    h_rows = ring.tile([P, PACK, width], BF16, name="h_rows")
+                for t0 in range(0, PACK, per_bank):
+                    pre = psum.tile([P, per_bank, width], F32, name="pre", bufs=4)
+                    for i in range(per_bank):
+                        m = slice((t0 + i) * P, (t0 + i + 1) * P)
+                        times_table(
+                            pre[:, i, :],
+                            [w1_codes[b, a][:, m] for a in range(PASSES)],
+                            [w1_plane[b, a][:, m] for a in range(PASSES)],
+                            cols,
+                        )
+                    act = ring.tile([P, BANK], F32, name="act")
+                    if short_way:
+                        act3 = act[:].rearrange("p (c t) -> p c t", t=PACK)
+                        nc.scalar.activation(act3, pre[:].rearrange("p t c -> p c t"), TANH)
+                        nc.vector.tensor_tensor(
+                            h_grouped[:, b, :].rearrange("p (c t) -> p c t", t=PACK),
+                            act3,
+                            gains[:, b : b + 1, :].to_broadcast([P, width, PACK]),
+                            MULT,
+                        )
+                    else:
+                        nc.scalar.activation(act[:], pre[:].rearrange("p t c -> p (t c)"), TANH)
+                        for i in range(per_bank):
+                            nc.scalar.activation(
+                                h_rows[:, t0 + i, :],
+                                act[:, i * width : (i + 1) * width],
+                                COPY,
+                                scale=gains[:, b, t0 + i : t0 + i + 1],
+                            )
+                if not short_way:
+                    nc.scalar.copy(
+                        h_grouped[:, b, :].rearrange("p (c i t) -> p c t i", i=4, t=PACK),
+                        h_rows[:].rearrange("p t (c i) -> p c t i", i=4),
+                    )
+            nc.vector.quantize_mx(h_codes[:].bitcast(E4M3), h_plane[:], h_grouped[:].rearrange("p b c -> p (b c)"))
+
+            linear = keep.tile([P, ROW_TILES, width], F32, name="linear%d" % s)
+            for n0 in range(0, ROW_TILES, 2):
+                d_acc = psum.tile([P, 2, width], F32, name="d_acc")
+                for i in range(2):
+                    m = slice((n0 + i) * P, (n0 + i + 1) * P)
+                    times_table(
+                        d_acc[:, i, :],
+                        [w3_codes[:, a, m] for a in range(PASSES)],
+                        [w3_plane[:, a, m] for a in range(PASSES)],
+                        cols,
+                    )
+                nc.scalar.copy(linear[:, n0 : n0 + 2, :], d_acc[:])
+
+            if s == 0:
+                whole = keep.tile([P, S], F32, name="picked_whole")
+                for u in range(0, S, GATHER):
+                    nc.vector.tensor_copy(whole[:, u : u + GATHER], state[0][:].indirect(listed(u, GATHER)))
+            if first % GATHER == 0:
+                tag = "slice%d" % s
+                rest = keep.tile([P, ROW_TILES - 1, GATHER], F32, name="picked_rest", tag=tag, align_bytes=64)
+                for n in range(1, ROW_TILES):
+                    nc.vector.tensor_copy(rest[:, n - 1, :], state[n][:].indirect(listed(first, GATHER)))
+                rest_first = first
+
+            for n0 in range(0, ROW_TILES, 2):
+                y_acc = psum.tile([P, 2, width], F32, name="y_acc")
+                for i in range(2):
+                    n = n0 + i
+                    for c in range(0, width, P):
+                        for b in range(PASSES):
+                            h_cols = slice(b * width + c, b * width + c + P)
+                            nc.tensor.matmul_mx(
+                                y_acc[:, i, c : c + P],
+                                lhsT=w2_codes[:, b, 2 * n * P : 2 * (n + 1) * P].bitcast(E2M1),
+                                lhsT_scale=w2_plane[:, b, n * P : (n + 1) * P],
+                                rhs=h_codes[:, h_cols].bitcast(E4M3),
+                                rhs_scale=h_plane[:, h_cols],
+                                start=(b == 0),
+                                stop=(b == PASSES - 1),
+                            )
+                offset = ring.tile([P, 2, width], F32, name="offset")
+                nc.vector.tensor_tensor(offset[:], y_acc[:], linear[:, n0 : n0 + 2, :], MULT)
+                for i in range(2):
+                    n = n0 + i
+                    if n == 0:
+                        old = whole[:, cols]
+                    else:
+                        old = rest[:, n - 1, first - rest_first : first - rest_first + width]
+                    nc.vector.tensor_tensor(state[n][:].indirect(listed(first, width)), old, offset[:, i, :], ADD)
+            first += width
+
+        for n in range(ROW_TILES):
+            nc.sync.dma_start(out[n * P : (n + 1) * P, :], state[n][:])

@@ -25,9 +25,9 @@ PASSES = K // PASS
 BANK = 512
 ROW_TILES = N // P
 PER_COLUMN = 16
-GATHER = 256
+TAB_PLANE_ROW = 8
 SLICES = (128, 128, 256, 256, 256)
-CAST_ON_VECTOR = (0, 64, 128, 128)
+CASTS_ON_SCALAR = ((0, 0, 0), (0, 0, 1), (0, 1, 1))
 
 
 def tile_list_sense_drift_rewrite_kernel(
@@ -39,32 +39,29 @@ def tile_list_sense_drift_rewrite_kernel(
         ring = ctx.enter_context(tc.tile_pool(name="ring", bufs=3))
         psum = ctx.enter_context(tc.psum_pool(name="psum", bufs=2))
 
-        offsets = keep.tile([P, S // PER_COLUMN], U16, name="offsets")
-        nc.sync.dma_start(offsets[:], offs)
-
-        def listed(first, count):
-            return offsets[:, first // PER_COLUMN : (first + count) // PER_COLUMN]
-
-        tab_plane = keep.tile([P, T], U8, name="tab_plane", align_bytes=64)
-        nc.gpsimd.memset(tab_plane[:].bitcast(I32), 0)
-        tab = [keep.tile([P, T], U32, name="tab%d" % a, align_bytes=64) for a in range(PASSES)]
-        nc.sync.dma_start(tab[0][:].bitcast(I32), tab_words[0].rearrange("p t i -> p (t i)").bitcast(I32))
-        for q in range(4):
-            nc.sync.dma_start(
-                tab_plane[32 * q : 32 * q + 4 * PASSES, :].bitcast(I32),
-                tab_scales[:, 4 * q : 4 * q + 4, :].bitcast(I32),
-            )
-        nc.sync.dma_start(tab[1][:].bitcast(I32), tab_words[1].rearrange("p t i -> p (t i)").bitcast(I32))
-
-        def load_plane(scales, name):
-            plane = keep.tile([P, PASSES, N], U8, name=name, align_bytes=64)
+        def zeroed_plane(shape, name):
+            plane = keep.tile(shape, U8, name=name, align_bytes=64)
             nc.gpsimd.memset(plane[:].bitcast(I32), 0)
+            return plane
+
+        def load_table_pass(a):
+            words = keep.tile([P, T], U32, name="tab%d" % a, align_bytes=64)
+            nc.sync.dma_start(words[:].bitcast(I32), tab_words[a].rearrange("p t i -> p (t i)").bitcast(I32))
+            return words
+
+        def load_table_scales(a):
             for q in range(4):
+                row = 32 * q + TAB_PLANE_ROW + 4 * a
+                nc.sync.dma_start(
+                    tab_plane[row : row + 4, :].bitcast(I32), tab_scales[a, 4 * q : 4 * q + 4, :].bitcast(I32)
+                )
+
+        def load_weight_scales(plane, scales, quadrants):
+            for q in quadrants:
                 nc.sync.dma_start(
                     plane[32 * q : 32 * q + 4, :, :].bitcast(I32),
                     scales[:, 4 * q : 4 * q + 4, :].rearrange("a q c -> q a c").bitcast(I32),
                 )
-            return plane
 
         def load_w1(b, a):
             raw = keep.tile([P, PACK, PASS], F32, name="w1_raw%d%d" % (b, a))
@@ -74,28 +71,42 @@ def tile_list_sense_drift_rewrite_kernel(
             )
             return raw
 
-        w1_raw = {}
+        tab_plane = zeroed_plane([P, T], "tab_plane")
+        w3_plane = zeroed_plane([P, PASSES, N], "w3_plane")
+        w2_plane = zeroed_plane([P, PASSES, N], "w2_plane")
+
+        tab = [load_table_pass(0)]
+        offsets = keep.tile([P, S // PER_COLUMN], U16, name="offsets")
+        nc.sync.dma_start(offsets[:], offs)
+        load_table_scales(0)
+        tab.append(load_table_pass(1))
+        load_table_scales(1)
+        w1_raw = {(0, 0): load_w1(0, 0)}
         gains = keep.tile([P, PASSES, PACK], F32, name="gains")
         nc.sync.dma_start(gains[:], gain.rearrange("(b p t) -> p b t", b=PASSES, t=PACK))
-        w3_plane = load_plane(w3_scales, "w3_plane")
-        w1_raw[0, 0] = load_w1(0, 0)
-        w2_plane = load_plane(w2_scales, "w2_plane")
+        load_weight_scales(w3_plane, w3_scales, range(4))
+        load_weight_scales(w2_plane, w2_scales, range(1))
         w1_raw[0, 1] = load_w1(0, 1)
+        load_weight_scales(w2_plane, w2_scales, range(1, 4))
         w1_raw[1, 0] = load_w1(1, 0)
         w1_raw[1, 1] = load_w1(1, 1)
         state = [keep.tile([P, T], F32, name="state%d" % n) for n in range(ROW_TILES)]
+        nc.sync.dma_start(state[0][:], gT[0:P, :])
         w3_codes = keep.tile([P, PASSES, N], U32, name="w3_codes", align_bytes=64)
         nc.sync.dma_start(w3_codes[:].bitcast(I32), w3_words.rearrange("a p c i -> p a (c i)").bitcast(I32))
         w2_codes = keep.tile([P, PASSES, 2 * N], U8, name="w2_codes", align_bytes=64)
         nc.sync.dma_start(w2_codes[:].bitcast(I32), w2_words.rearrange("a p c -> p a c").bitcast(I32))
-        for n in range(ROW_TILES):
+        for n in range(1, ROW_TILES):
             nc.sync.dma_start(state[n][:], gT[n * P : (n + 1) * P, :])
 
-        v_plane = keep.tile([P, S], U8, name="v_plane", align_bytes=64)
-        nc.vector.tensor_copy(v_plane[:], tab_plane[:].indirect(offsets[:]))
+        def listed(first, count):
+            return offsets[:, first // PER_COLUMN : (first + count) // PER_COLUMN]
+
         v_codes = [keep.tile([P, S], U32, name="v_codes%d" % a, align_bytes=64) for a in range(PASSES)]
         for a in range(PASSES):
             nc.vector.tensor_copy(v_codes[a][:], tab[a][:].indirect(offsets[:]))
+        v_plane = keep.tile([P, S], U8, name="v_plane", align_bytes=64)
+        nc.vector.tensor_copy(v_plane[:], tab_plane[:].indirect(offsets[:]))
 
         w1_codes, w1_plane = {}, {}
         for b in range(PASSES):
@@ -103,55 +114,64 @@ def tile_list_sense_drift_rewrite_kernel(
                 grouped = keep.tile([P, PACK * PASS], BF16, name="w1_grouped%d%d" % (b, a), align_bytes=64)
                 dst = grouped[:].rearrange("p (t m j) -> p m j t", t=PACK, j=PACK)
                 src = w1_raw[b, a][:].rearrange("p j (m t) -> p m j t", t=PACK)
-                split = CAST_ON_VECTOR[PASSES * b + a]
-                if split > 0:
-                    nc.vector.tensor_copy(dst[:, :split], src[:, :split])
-                if split < P:
-                    nc.scalar.copy(dst[:, split:], src[:, split:])
+                for u in range(2):
+                    cast = nc.scalar.copy if (b, a, u) in CASTS_ON_SCALAR else nc.vector.tensor_copy
+                    cast(dst[:, :, :, 2 * u : 2 * u + 2], src[:, :, :, 2 * u : 2 * u + 2])
                 w1_codes[b, a] = keep.tile([P, PASS], U32, name="w1_codes%d%d" % (b, a), align_bytes=64)
                 w1_plane[b, a] = keep.tile([P, PASS], U8, name="w1_plane%d%d" % (b, a), align_bytes=64)
-                nc.vector.quantize_mx(w1_codes[b, a][:].bitcast(E4M3), w1_plane[b, a][:], grouped[:])
+                for u in range(2):
+                    half = slice(2 * u * P, 2 * (u + 1) * P)
+                    nc.vector.quantize_mx(
+                        w1_codes[b, a][:, half].bitcast(E4M3),
+                        w1_plane[b, a][:, half],
+                        grouped[:, PACK * half.start : PACK * half.stop],
+                    )
 
-        def times_table(acc, codes, planes, cols):
-            for a in range(PASSES):
+        def times_table(acc, codes, planes, first_column, cols, one_group=False):
+            blocks = acc.shape[1]
+            order = [(i, a) for i in range(blocks) for a in range(PASSES)]
+            if one_group:
+                order = [(i, a) for a in range(PASSES) for i in range(blocks)]
+            for i, a in order:
+                m = slice(first_column + i * P, first_column + (i + 1) * P)
                 nc.tensor.matmul_mx(
-                    acc,
-                    lhsT=codes[a].bitcast(E4M3),
-                    lhsT_scale=planes[a],
+                    acc[:, i, :],
+                    lhsT=codes[a][:, m].bitcast(E4M3),
+                    lhsT_scale=planes[a][:, m],
                     rhs=v_codes[a][:, cols].bitcast(E4M3),
-                    rhs_scale=v_plane[4 * a :, cols],
-                    start=(a == 0),
-                    stop=(a == PASSES - 1),
+                    rhs_scale=v_plane[TAB_PLANE_ROW + 4 * a :, cols],
+                    start=(i, a) == order[0] if one_group else a == 0,
+                    stop=(i, a) == order[-1] if one_group else a == PASSES - 1,
                 )
 
-        first = 0
-        for s, width in enumerate(SLICES):
-            cols = slice(first, first + width)
+        def hidden(s, cols):
+            width = SLICES[s]
             per_bank = BANK // width
-            h_grouped = keep.tile([P, PASSES, width * PACK], BF16, name="h_grouped", tag="slice%d" % s, align_bytes=64)
-            h_codes = keep.tile([P, PASSES * width], U32, name="h_codes%d" % s, align_bytes=64)
-            h_plane = keep.tile([P, PASSES * width], U8, name="h_plane%d" % s, align_bytes=64)
+            grouped = [
+                keep.tile([P, PASSES, P * PACK], BF16, name="h_grouped", tag="h%d_%d" % (s, c), align_bytes=64)
+                for c in range(width // P)
+            ]
             for b in range(PASSES):
                 short_way = s == 0 and b == PASSES - 1
                 if not short_way:
                     h_rows = ring.tile([P, PACK, width], BF16, name="h_rows")
                 for t0 in range(0, PACK, per_bank):
                     pre = psum.tile([P, per_bank, width], F32, name="pre", bufs=4)
-                    for i in range(per_bank):
-                        m = slice((t0 + i) * P, (t0 + i + 1) * P)
-                        times_table(
-                            pre[:, i, :],
-                            [w1_codes[b, a][:, m] for a in range(PASSES)],
-                            [w1_plane[b, a][:, m] for a in range(PASSES)],
-                            cols,
-                        )
+                    times_table(
+                        pre,
+                        [w1_codes[b, a] for a in range(PASSES)],
+                        [w1_plane[b, a] for a in range(PASSES)],
+                        t0 * P,
+                        cols,
+                        one_group=short_way,
+                    )
                     act = ring.tile([P, BANK], F32, name="act")
                     if short_way:
-                        act3 = act[:].rearrange("p (c t) -> p c t", t=PACK)
-                        nc.scalar.activation(act3, pre[:].rearrange("p t c -> p c t"), TANH)
+                        by_column = act[:].rearrange("p (c t) -> p c t", t=PACK)
+                        nc.scalar.activation(by_column, pre[:].rearrange("p t c -> p c t"), TANH)
                         nc.vector.tensor_tensor(
-                            h_grouped[:, b, :].rearrange("p (c t) -> p c t", t=PACK),
-                            act3,
+                            grouped[0][:, b, :].rearrange("p (c t) -> p c t", t=PACK),
+                            by_column,
                             gains[:, b : b + 1, :].to_broadcast([P, width, PACK]),
                             MULT,
                         )
@@ -165,62 +185,120 @@ def tile_list_sense_drift_rewrite_kernel(
                                 scale=gains[:, b, t0 + i : t0 + i + 1],
                             )
                 if not short_way:
-                    nc.scalar.copy(
-                        h_grouped[:, b, :].rearrange("p (c i t) -> p c t i", i=4, t=PACK),
-                        h_rows[:].rearrange("p t (c i) -> p c t i", i=4),
-                    )
-            nc.vector.quantize_mx(h_codes[:].bitcast(E4M3), h_plane[:], h_grouped[:].rearrange("p b c -> p (b c)"))
+                    for c in range(width // P):
+                        nc.scalar.copy(
+                            grouped[c][:, b, :].rearrange("p (c i t) -> p c t i", i=4, t=PACK),
+                            h_rows[:, :, c * P : (c + 1) * P].rearrange("p t (c i) -> p c t i", i=4),
+                        )
+            h = []
+            for c in range(width // P):
+                codes = keep.tile([P, PASSES, P], U32, name="h_codes%d_%d" % (s, c), align_bytes=64)
+                plane = keep.tile([P, PASSES, P], U8, name="h_plane%d_%d" % (s, c), align_bytes=64)
+                nc.vector.quantize_mx(
+                    codes[:].rearrange("p b c -> p (b c)").bitcast(E4M3),
+                    plane[:].rearrange("p b c -> p (b c)"),
+                    grouped[c][:].rearrange("p b c -> p (b c)"),
+                )
+                h.append((codes, plane))
+            return h
 
+        def linear_branch(s, cols):
+            width = SLICES[s]
             linear = keep.tile([P, ROW_TILES, width], F32, name="linear%d" % s)
             for n0 in range(0, ROW_TILES, 2):
                 d_acc = psum.tile([P, 2, width], F32, name="d_acc")
-                for i in range(2):
-                    m = slice((n0 + i) * P, (n0 + i + 1) * P)
-                    times_table(
-                        d_acc[:, i, :],
-                        [w3_codes[:, a, m] for a in range(PASSES)],
-                        [w3_plane[:, a, m] for a in range(PASSES)],
-                        cols,
-                    )
+                times_table(
+                    d_acc,
+                    [w3_codes[:, a, :] for a in range(PASSES)],
+                    [w3_plane[:, a, :] for a in range(PASSES)],
+                    n0 * P,
+                    cols,
+                )
                 nc.scalar.copy(linear[:, n0 : n0 + 2, :], d_acc[:])
+            return linear
 
-            if s == 0:
-                whole = keep.tile([P, S], F32, name="picked_whole")
-                for u in range(0, S, GATHER):
-                    nc.vector.tensor_copy(whole[:, u : u + GATHER], state[0][:].indirect(listed(u, GATHER)))
-            if first % GATHER == 0:
-                tag = "slice%d" % s
-                rest = keep.tile([P, ROW_TILES - 1, GATHER], F32, name="picked_rest", tag=tag, align_bytes=64)
-                for n in range(1, ROW_TILES):
-                    nc.vector.tensor_copy(rest[:, n - 1, :], state[n][:].indirect(listed(first, GATHER)))
-                rest_first = first
+        def drift_pair(dst, n0, h, linear):
+            width = linear.shape[2]
+            y_acc = psum.tile([P, 2, width], F32, name="y_acc")
+            for i in range(2):
+                n = n0 + i
+                for c, (codes, plane) in enumerate(h):
+                    for b in range(PASSES):
+                        nc.tensor.matmul_mx(
+                            y_acc[:, i, c * P : (c + 1) * P],
+                            lhsT=w2_codes[:, b, 2 * n * P : 2 * (n + 1) * P].bitcast(E2M1),
+                            lhsT_scale=w2_plane[:, b, n * P : (n + 1) * P],
+                            rhs=codes[:, b, :].bitcast(E4M3),
+                            rhs_scale=plane[:, b, :],
+                            start=(b == 0),
+                            stop=(b == PASSES - 1),
+                        )
+            nc.vector.tensor_tensor(dst, y_acc[:], linear[:, n0 : n0 + 2, :], MULT)
 
+        picked = {}
+
+        def pick(rows, first, count, after=None):
+            name = "picked%d_%d" % (rows[0], first)
+            tag = name if after is None else "h%d_%d" % after
+            tile = keep.tile([P, len(rows), count], F32, name=name, tag=tag, align_bytes=64)
+            for i, n in enumerate(rows):
+                nc.vector.tensor_copy(tile[:, i, :], state[n][:].indirect(listed(first, count)))
+                picked[n, first] = tile[:, i, :]
+
+        def put_back(n, first, count, drift, picked_from):
+            old = picked[n, picked_from][:, first - picked_from : first - picked_from + count]
+            nc.vector.tensor_tensor(state[n][:].indirect(listed(first, count)), old, drift, ADD)
+
+        def branches(s):
+            first = sum(SLICES[:s])
+            cols = slice(first, first + SLICES[s])
+            return hidden(s, cols), linear_branch(s, cols)
+
+        def drifts(dst, part):
+            h, linear = part
             for n0 in range(0, ROW_TILES, 2):
-                y_acc = psum.tile([P, 2, width], F32, name="y_acc")
-                for i in range(2):
-                    n = n0 + i
-                    for c in range(0, width, P):
-                        for b in range(PASSES):
-                            h_cols = slice(b * width + c, b * width + c + P)
-                            nc.tensor.matmul_mx(
-                                y_acc[:, i, c : c + P],
-                                lhsT=w2_codes[:, b, 2 * n * P : 2 * (n + 1) * P].bitcast(E2M1),
-                                lhsT_scale=w2_plane[:, b, n * P : (n + 1) * P],
-                                rhs=h_codes[:, h_cols].bitcast(E4M3),
-                                rhs_scale=h_plane[:, h_cols],
-                                start=(b == 0),
-                                stop=(b == PASSES - 1),
-                            )
-                offset = ring.tile([P, 2, width], F32, name="offset")
-                nc.vector.tensor_tensor(offset[:], y_acc[:], linear[:, n0 : n0 + 2, :], MULT)
-                for i in range(2):
-                    n = n0 + i
-                    if n == 0:
-                        old = whole[:, cols]
-                    else:
-                        old = rest[:, n - 1, first - rest_first : first - rest_first + width]
-                    nc.vector.tensor_tensor(state[n][:].indirect(listed(first, width)), old, offset[:, i, :], ADD)
-            first += width
+                drift_pair(dst[:, n0 : n0 + 2, :], n0, h, linear)
+
+        def finish(first, count, part, picked_from):
+            drift = ring.tile([P, ROW_TILES, count], F32, name="drift")
+            drifts(drift, part)
+            for n in range(ROW_TILES):
+                put_back(n, first, count, drift[:, n, :], picked_from)
+
+        part = branches(0)
+        pick([0], 0, 256)
+        pick([0], 256, 256)
+        pick([0], 512, 512, after=(0, 0))
+        drift = ring.tile([P, ROW_TILES, 128], F32, name="drift")
+        drifts(drift, part)
+        put_back(0, 0, 128, drift[:, 0, :], 0)
+        part = branches(1)
+        pick([1], 0, 256, after=(1, 0))
+        pick([2], 0, 256)
+        pick([3], 0, 256)
+        for n in range(1, ROW_TILES):
+            put_back(n, 0, 128, drift[:, n, :], 0)
+        finish(128, 128, part, 0)
+
+        part = branches(2)
+        pick([1, 2], 256, 256, after=(2, 0))
+        pick([3], 256, 256, after=(2, 1))
+        finish(256, 256, part, 256)
+
+        drift = keep.tile([P, ROW_TILES, 512], F32, name="drift_last")
+        part = branches(3)
+        pick([2], 512, 512, after=(3, 0))
+        pick([3], 512, 512, after=(3, 1))
+        drifts(drift[:, :, :256], part)
+        put_back(0, 512, 256, drift[:, 0, :256], 512)
+        part = branches(4)
+        pick([1], 512, 512, after=(4, 0))
+        put_back(1, 512, 256, drift[:, 1, :256], 512)
+        drifts(drift[:, :, 256:], part)
+        for n in range(2):
+            put_back(n, 768, 256, drift[:, n, 256:], 512)
+        for n in range(2, ROW_TILES):
+            put_back(n, 512, 512, drift[:, n, :], 512)
 
         for n in range(ROW_TILES):
             nc.sync.dma_start(out[n * P : (n + 1) * P, :], state[n][:])

@@ -26,8 +26,8 @@ BANK = 512
 ROW_TILES = N // P
 PER_COLUMN = 16
 TAB_PLANE_ROW = 8
-SLICES = (128, 128, 256, 256, 256)
-CASTS_ON_SCALAR = ((0, 0, 0), (0, 0, 1), (0, 1, 1))
+WIDTH = 256
+SLICES = S // WIDTH
 
 
 def tile_list_sense_drift_rewrite_kernel(
@@ -36,12 +36,12 @@ def tile_list_sense_drift_rewrite_kernel(
     nc = tc.nc
     with ExitStack() as ctx:
         keep = ctx.enter_context(tc.tile_pool(name="keep", bufs=1))
-        ring = ctx.enter_context(tc.tile_pool(name="ring", bufs=3))
+        ring = ctx.enter_context(tc.tile_pool(name="ring", bufs=4))
         psum = ctx.enter_context(tc.psum_pool(name="psum", bufs=2))
 
         def zeroed_plane(shape, name):
             plane = keep.tile(shape, U8, name=name, align_bytes=64)
-            nc.gpsimd.memset(plane[:].bitcast(I32), 0)
+            nc.vector.memset(plane[:].bitcast(I32), 0)
             return plane
 
         def load_table_pass(a):
@@ -49,16 +49,9 @@ def tile_list_sense_drift_rewrite_kernel(
             nc.sync.dma_start(words[:].bitcast(I32), tab_words[a].rearrange("p t i -> p (t i)").bitcast(I32))
             return words
 
-        def load_table_scales(a):
+        def load_weight_scales(plane, scales):
             for q in range(4):
-                row = 32 * q + TAB_PLANE_ROW + 4 * a
-                nc.sync.dma_start(
-                    tab_plane[row : row + 4, :].bitcast(I32), tab_scales[a, 4 * q : 4 * q + 4, :].bitcast(I32)
-                )
-
-        def load_weight_scales(plane, scales, quadrants):
-            for q in quadrants:
-                nc.sync.dma_start(
+                nc.gpsimd.dma_start(
                     plane[32 * q : 32 * q + 4, :, :].bitcast(I32),
                     scales[:, 4 * q : 4 * q + 4, :].rearrange("a q c -> q a c").bitcast(I32),
                 )
@@ -74,231 +67,195 @@ def tile_list_sense_drift_rewrite_kernel(
         tab_plane = zeroed_plane([P, T], "tab_plane")
         w3_plane = zeroed_plane([P, PASSES, N], "w3_plane")
         w2_plane = zeroed_plane([P, PASSES, N], "w2_plane")
+        load_weight_scales(w3_plane, w3_scales)
+        load_weight_scales(w2_plane, w2_scales)
 
-        tab = [load_table_pass(0)]
         offsets = keep.tile([P, S // PER_COLUMN], U16, name="offsets")
         nc.sync.dma_start(offsets[:], offs)
-        load_table_scales(0)
-        tab.append(load_table_pass(1))
-        load_table_scales(1)
         w1_raw = {(0, 0): load_w1(0, 0)}
+        for q in range(4):
+            row = 32 * q + TAB_PLANE_ROW
+            nc.sync.dma_start(
+                tab_plane[row : row + 8, :].bitcast(I32), tab_scales[:, 4 * q : 4 * q + 4, :].bitcast(I32)
+            )
+        tab = [load_table_pass(0)]
         gains = keep.tile([P, PASSES, PACK], F32, name="gains")
         nc.sync.dma_start(gains[:], gain.rearrange("(b p t) -> p b t", b=PASSES, t=PACK))
-        load_weight_scales(w3_plane, w3_scales, range(4))
-        load_weight_scales(w2_plane, w2_scales, range(1))
         w1_raw[0, 1] = load_w1(0, 1)
-        load_weight_scales(w2_plane, w2_scales, range(1, 4))
+        tab.append(load_table_pass(1))
         w1_raw[1, 0] = load_w1(1, 0)
         w1_raw[1, 1] = load_w1(1, 1)
         state = [keep.tile([P, T], F32, name="state%d" % n) for n in range(ROW_TILES)]
-        nc.sync.dma_start(state[0][:], gT[0:P, :])
+        for n in range(2):
+            nc.sync.dma_start(state[n][:], gT[n * P : (n + 1) * P, :])
         w3_codes = keep.tile([P, PASSES, N], U32, name="w3_codes", align_bytes=64)
         nc.sync.dma_start(w3_codes[:].bitcast(I32), w3_words.rearrange("a p c i -> p a (c i)").bitcast(I32))
+        nc.sync.dma_start(state[2][:], gT[2 * P : 3 * P, :])
         w2_codes = keep.tile([P, PASSES, 2 * N], U8, name="w2_codes", align_bytes=64)
         nc.sync.dma_start(w2_codes[:].bitcast(I32), w2_words.rearrange("a p c -> p a c").bitcast(I32))
-        for n in range(1, ROW_TILES):
-            nc.sync.dma_start(state[n][:], gT[n * P : (n + 1) * P, :])
+        nc.sync.dma_start(state[ROW_TILES - 1][:], gT[(ROW_TILES - 1) * P :, :])
 
         def listed(first, count):
             return offsets[:, first // PER_COLUMN : (first + count) // PER_COLUMN]
 
-        v_codes = [keep.tile([P, S], U32, name="v_codes%d" % a, align_bytes=64) for a in range(PASSES)]
-        for a in range(PASSES):
-            nc.vector.tensor_copy(v_codes[a][:], tab[a][:].indirect(offsets[:]))
+        w1_codes, w1_plane = {}, {}
+
+        def quantise_w1(b, a, engines):
+            grouped = keep.tile([P, PACK * PASS], BF16, name="w1_grouped%d%d" % (b, a), align_bytes=64)
+            dst = grouped[:].rearrange("p (t m j) -> p m j t", t=PACK, j=PACK)
+            src = w1_raw[b, a][:].rearrange("p j (m t) -> p m j t", t=PACK)
+            share = P // len(engines)
+            for i, cast in enumerate(engines):
+                cast(dst[:, i * share : (i + 1) * share], src[:, i * share : (i + 1) * share])
+            w1_codes[b, a] = keep.tile([P, PASS], U32, name="w1_codes%d%d" % (b, a), align_bytes=64)
+            w1_plane[b, a] = keep.tile([P, PASS], U8, name="w1_plane%d%d" % (b, a), align_bytes=64)
+            nc.vector.quantize_mx(w1_codes[b, a][:].bitcast(E4M3), w1_plane[b, a][:], grouped[:])
+
         v_plane = keep.tile([P, S], U8, name="v_plane", align_bytes=64)
         nc.vector.tensor_copy(v_plane[:], tab_plane[:].indirect(offsets[:]))
+        v_codes = [keep.tile([P, S], U32, name="v_codes%d" % a, align_bytes=64) for a in range(PASSES)]
+        nc.vector.tensor_copy(v_codes[0][:], tab[0][:].indirect(offsets[:]))
+        quantise_w1(0, 0, [nc.scalar.copy])
+        quantise_w1(0, 1, [nc.vector.tensor_copy, nc.scalar.copy])
+        nc.vector.tensor_copy(v_codes[1][:, :WIDTH], tab[1][:].indirect(listed(0, WIDTH)))
+        nc.vector.tensor_copy(v_codes[1][:, WIDTH:], tab[1][:].indirect(listed(WIDTH, S - WIDTH)))
+        quantise_w1(1, 0, [nc.vector.tensor_copy])
+        quantise_w1(1, 1, [nc.vector.tensor_copy])
 
-        w1_codes, w1_plane = {}, {}
-        for b in range(PASSES):
-            for a in range(PASSES):
-                grouped = keep.tile([P, PACK * PASS], BF16, name="w1_grouped%d%d" % (b, a), align_bytes=64)
-                dst = grouped[:].rearrange("p (t m j) -> p m j t", t=PACK, j=PACK)
-                src = w1_raw[b, a][:].rearrange("p j (m t) -> p m j t", t=PACK)
-                for u in range(2):
-                    cast = nc.scalar.copy if (b, a, u) in CASTS_ON_SCALAR else nc.vector.tensor_copy
-                    cast(dst[:, :, :, 2 * u : 2 * u + 2], src[:, :, :, 2 * u : 2 * u + 2])
-                w1_codes[b, a] = keep.tile([P, PASS], U32, name="w1_codes%d%d" % (b, a), align_bytes=64)
-                w1_plane[b, a] = keep.tile([P, PASS], U8, name="w1_plane%d%d" % (b, a), align_bytes=64)
-                for u in range(2):
-                    half = slice(2 * u * P, 2 * (u + 1) * P)
-                    nc.vector.quantize_mx(
-                        w1_codes[b, a][:, half].bitcast(E4M3),
-                        w1_plane[b, a][:, half],
-                        grouped[:, PACK * half.start : PACK * half.stop],
-                    )
+        picked = []
+        for n in range(ROW_TILES):
+            tile = keep.tile([P, S], F32, name="picked%d" % n)
+            nc.vector.tensor_copy(tile[:], state[n][:].indirect(offsets[:]))
+            picked.append(tile)
 
-        def times_table(acc, codes, planes, first_column, cols, one_group=False):
-            blocks = acc.shape[1]
-            order = [(i, a) for i in range(blocks) for a in range(PASSES)]
-            if one_group:
-                order = [(i, a) for a in range(PASSES) for i in range(blocks)]
-            for i, a in order:
+        def columns(s):
+            return slice(s * WIDTH, (s + 1) * WIDTH)
+
+        def times_table(acc, codes, planes, first_column, cols):
+            for i in range(2):
                 m = slice(first_column + i * P, first_column + (i + 1) * P)
-                nc.tensor.matmul_mx(
-                    acc[:, i, :],
-                    lhsT=codes[a][:, m].bitcast(E4M3),
-                    lhsT_scale=planes[a][:, m],
-                    rhs=v_codes[a][:, cols].bitcast(E4M3),
-                    rhs_scale=v_plane[TAB_PLANE_ROW + 4 * a :, cols],
-                    start=(i, a) == order[0] if one_group else a == 0,
-                    stop=(i, a) == order[-1] if one_group else a == PASSES - 1,
-                )
-
-        def hidden(s, cols):
-            width = SLICES[s]
-            per_bank = BANK // width
-            grouped = [
-                keep.tile([P, PASSES, P * PACK], BF16, name="h_grouped", tag="h%d_%d" % (s, c), align_bytes=64)
-                for c in range(width // P)
-            ]
-            for b in range(PASSES):
-                short_way = s == 0 and b == PASSES - 1
-                if not short_way:
-                    h_rows = ring.tile([P, PACK, width], BF16, name="h_rows")
-                for t0 in range(0, PACK, per_bank):
-                    pre = psum.tile([P, per_bank, width], F32, name="pre", bufs=4)
-                    times_table(
-                        pre,
-                        [w1_codes[b, a] for a in range(PASSES)],
-                        [w1_plane[b, a] for a in range(PASSES)],
-                        t0 * P,
-                        cols,
-                        one_group=short_way,
+                for a in range(PASSES):
+                    nc.tensor.matmul_mx(
+                        acc[:, i, :],
+                        lhsT=codes[a][:, m].bitcast(E4M3),
+                        lhsT_scale=planes[a][:, m],
+                        rhs=v_codes[a][:, cols].bitcast(E4M3),
+                        rhs_scale=v_plane[TAB_PLANE_ROW + 4 * a :, cols],
+                        start=a == 0,
+                        stop=a == PASSES - 1,
                     )
-                    act = ring.tile([P, BANK], F32, name="act")
-                    if short_way:
-                        by_column = act[:].rearrange("p (c t) -> p c t", t=PACK)
-                        nc.scalar.activation(by_column, pre[:].rearrange("p t c -> p c t"), TANH)
-                        nc.vector.tensor_tensor(
-                            grouped[0][:, b, :].rearrange("p (c t) -> p c t", t=PACK),
-                            by_column,
-                            gains[:, b : b + 1, :].to_broadcast([P, width, PACK]),
-                            MULT,
-                        )
-                    else:
-                        nc.scalar.activation(act[:], pre[:].rearrange("p t c -> p (t c)"), TANH)
-                        for i in range(per_bank):
-                            nc.scalar.activation(
-                                h_rows[:, t0 + i, :],
-                                act[:, i * width : (i + 1) * width],
-                                COPY,
-                                scale=gains[:, b, t0 + i : t0 + i + 1],
-                            )
-                if not short_way:
-                    for c in range(width // P):
-                        nc.scalar.copy(
-                            grouped[c][:, b, :].rearrange("p (c i t) -> p c t i", i=4, t=PACK),
-                            h_rows[:, :, c * P : (c + 1) * P].rearrange("p t (c i) -> p c t i", i=4),
-                        )
-            h = []
-            for c in range(width // P):
-                codes = keep.tile([P, PASSES, P], U32, name="h_codes%d_%d" % (s, c), align_bytes=64)
-                plane = keep.tile([P, PASSES, P], U8, name="h_plane%d_%d" % (s, c), align_bytes=64)
-                nc.vector.quantize_mx(
-                    codes[:].rearrange("p b c -> p (b c)").bitcast(E4M3),
-                    plane[:].rearrange("p b c -> p (b c)"),
-                    grouped[c][:].rearrange("p b c -> p (b c)"),
-                )
-                h.append((codes, plane))
-            return h
 
-        def linear_branch(s, cols):
-            width = SLICES[s]
-            linear = keep.tile([P, ROW_TILES, width], F32, name="linear%d" % s)
-            for n0 in range(0, ROW_TILES, 2):
-                d_acc = psum.tile([P, 2, width], F32, name="d_acc")
-                times_table(
-                    d_acc,
-                    [w3_codes[:, a, :] for a in range(PASSES)],
-                    [w3_plane[:, a, :] for a in range(PASSES)],
-                    n0 * P,
-                    cols,
+        grouped = [
+            keep.tile([P, PASSES, WIDTH * PACK], BF16, name="h_grouped%d" % s, align_bytes=64) for s in range(SLICES)
+        ]
+
+        h_rows = {}
+
+        def hidden_half(s, b, t0):
+            if t0 == 0:
+                h_rows[s, b] = keep.tile([P, PACK, WIDTH], BF16, name="h_rows", tag="rows%d_%d" % (s, b))
+            pre = psum.tile([P, 2, WIDTH], F32, name="pre", bufs=4)
+            times_table(
+                pre,
+                [w1_codes[b, a] for a in range(PASSES)],
+                [w1_plane[b, a] for a in range(PASSES)],
+                t0 * P,
+                columns(s),
+            )
+            act = ring.tile([P, 2, WIDTH], F32, name="act")
+            nc.scalar.activation(act[:], pre[:], TANH)
+            for i in range(2):
+                nc.scalar.activation(
+                    h_rows[s, b][:, t0 + i, :], act[:, i, :], COPY, scale=gains[:, b, t0 + i : t0 + i + 1]
                 )
-                nc.scalar.copy(linear[:, n0 : n0 + 2, :], d_acc[:])
+            if t0 == 2:
+                nc.scalar.copy(
+                    grouped[s][:, b, :].rearrange("p (c i t) -> p c t i", i=4, t=PACK),
+                    h_rows[s, b][:].rearrange("p t (c i) -> p c t i", i=4),
+                )
+
+        def hidden(s, b):
+            hidden_half(s, b, 0)
+            hidden_half(s, b, 2)
+
+        h = {}
+
+        def quantise_h(s):
+            codes = keep.tile([P, PASSES, WIDTH], U32, name="h_codes%d" % s, align_bytes=64)
+            plane = keep.tile([P, PASSES, WIDTH], U8, name="h_plane%d" % s, align_bytes=64)
+            nc.vector.quantize_mx(
+                codes[:].rearrange("p b c -> p (b c)").bitcast(E4M3),
+                plane[:].rearrange("p b c -> p (b c)"),
+                grouped[s][:].rearrange("p b c -> p (b c)"),
+            )
+            h[s] = (codes, plane)
+
+        def linear_pair(s, n0, tag):
+            d_acc = psum.tile([P, 2, WIDTH], F32, name="d_acc")
+            times_table(
+                d_acc,
+                [w3_codes[:, a, :] for a in range(PASSES)],
+                [w3_plane[:, a, :] for a in range(PASSES)],
+                n0 * P,
+                columns(s),
+            )
+            linear = keep.tile([P, 2, WIDTH], F32, name="linear", tag=tag)
+            nc.scalar.copy(linear[:], d_acc[:])
             return linear
 
-        def drift_pair(dst, n0, h, linear):
-            width = linear.shape[2]
-            y_acc = psum.tile([P, 2, width], F32, name="y_acc")
+        def drift_pair(dst, s, n0, linear):
+            codes, plane = h[s]
+            y_acc = psum.tile([P, 2, WIDTH], F32, name="y_acc")
             for i in range(2):
                 n = n0 + i
-                for c, (codes, plane) in enumerate(h):
+                for c in range(WIDTH // P):
                     for b in range(PASSES):
                         nc.tensor.matmul_mx(
                             y_acc[:, i, c * P : (c + 1) * P],
                             lhsT=w2_codes[:, b, 2 * n * P : 2 * (n + 1) * P].bitcast(E2M1),
                             lhsT_scale=w2_plane[:, b, n * P : (n + 1) * P],
-                            rhs=codes[:, b, :].bitcast(E4M3),
-                            rhs_scale=plane[:, b, :],
+                            rhs=codes[:, b, c * P : (c + 1) * P].bitcast(E4M3),
+                            rhs_scale=plane[:, b, c * P : (c + 1) * P],
                             start=(b == 0),
                             stop=(b == PASSES - 1),
                         )
-            nc.vector.tensor_tensor(dst, y_acc[:], linear[:, n0 : n0 + 2, :], MULT)
+            nc.vector.tensor_tensor(dst, y_acc[:], linear[:], MULT)
 
-        picked = {}
+        drift = keep.tile([P, ROW_TILES, S], F32, name="drift")
 
-        def pick(rows, first, count, after=None):
-            name = "picked%d_%d" % (rows[0], first)
-            tag = name if after is None else "h%d_%d" % after
-            tile = keep.tile([P, len(rows), count], F32, name=name, tag=tag, align_bytes=64)
-            for i, n in enumerate(rows):
-                nc.vector.tensor_copy(tile[:, i, :], state[n][:].indirect(listed(first, count)))
-                picked[n, first] = tile[:, i, :]
+        def put_back(n, first, count):
+            nc.vector.tensor_tensor(
+                state[n][:].indirect(listed(first, count)),
+                picked[n][:, first : first + count],
+                drift[:, n, first : first + count],
+                ADD,
+            )
 
-        def put_back(n, first, count, drift, picked_from):
-            old = picked[n, picked_from][:, first - picked_from : first - picked_from + count]
-            nc.vector.tensor_tensor(state[n][:].indirect(listed(first, count)), old, drift, ADD)
+        def pair(s, n0, tag):
+            drift_pair(drift[:, n0 : n0 + 2, columns(s)], s, n0, linear_pair(s, n0, tag))
 
-        def branches(s):
-            first = sum(SLICES[:s])
-            cols = slice(first, first + SLICES[s])
-            return hidden(s, cols), linear_branch(s, cols)
-
-        def drifts(dst, part):
-            h, linear = part
-            for n0 in range(0, ROW_TILES, 2):
-                drift_pair(dst[:, n0 : n0 + 2, :], n0, h, linear)
-
-        def finish(first, count, part, picked_from):
-            drift = ring.tile([P, ROW_TILES, count], F32, name="drift")
-            drifts(drift, part)
-            for n in range(ROW_TILES):
-                put_back(n, first, count, drift[:, n, :], picked_from)
-
-        part = branches(0)
-        pick([0], 0, 256)
-        pick([0], 256, 256)
-        pick([0], 512, 512, after=(0, 0))
-        drift = ring.tile([P, ROW_TILES, 128], F32, name="drift")
-        drifts(drift, part)
-        put_back(0, 0, 128, drift[:, 0, :], 0)
-        part = branches(1)
-        pick([1], 0, 256, after=(1, 0))
-        pick([2], 0, 256)
-        pick([3], 0, 256)
-        for n in range(1, ROW_TILES):
-            put_back(n, 0, 128, drift[:, n, :], 0)
-        finish(128, 128, part, 0)
-
-        part = branches(2)
-        pick([1, 2], 256, 256, after=(2, 0))
-        pick([3], 256, 256, after=(2, 1))
-        finish(256, 256, part, 256)
-
-        drift = keep.tile([P, ROW_TILES, 512], F32, name="drift_last")
-        part = branches(3)
-        pick([2], 512, 512, after=(3, 0))
-        pick([3], 512, 512, after=(3, 1))
-        drifts(drift[:, :, :256], part)
-        put_back(0, 512, 256, drift[:, 0, :256], 512)
-        part = branches(4)
-        pick([1], 512, 512, after=(4, 0))
-        put_back(1, 512, 256, drift[:, 1, :256], 512)
-        drifts(drift[:, :, 256:], part)
-        for n in range(2):
-            put_back(n, 768, 256, drift[:, n, 256:], 512)
-        for n in range(2, ROW_TILES):
-            put_back(n, 512, 512, drift[:, n, :], 512)
+        last = SLICES - 1
+        hidden(0, 0)
+        hidden_half(1, 0, 0)
+        hidden(0, 1)
+        quantise_h(0)
+        for s in range(SLICES):
+            pair(s, 0, "linear%d" % s)
+            put_back(0, s * WIDTH, WIDTH)
+            put_back(1, s * WIDTH, WIDTH)
+            if s < last:
+                if s > 0:
+                    hidden_half(s + 1, 0, 0)
+                hidden_half(s + 1, 0, 2)
+                hidden(s + 1, 1)
+                quantise_h(s + 1)
+                pair(s, 2, "rows%d_1" % (s + 1))
+            else:
+                pair(s, 2, "linear_last")
+            put_back(2, s * WIDTH, WIDTH)
+            if s < last - 1:
+                put_back(3, s * WIDTH, WIDTH)
+        put_back(3, (last - 1) * WIDTH, 2 * WIDTH)
 
         for n in range(ROW_TILES):
             nc.sync.dma_start(out[n * P : (n + 1) * P, :], state[n][:])

@@ -37,7 +37,7 @@ def tile_list_sense_drift_rewrite_kernel(
     with ExitStack() as ctx:
         keep = ctx.enter_context(tc.tile_pool(name="keep", bufs=1))
         ring = ctx.enter_context(tc.tile_pool(name="ring", bufs=4))
-        psum = ctx.enter_context(tc.psum_pool(name="psum", bufs=2))
+        psum = ctx.enter_context(tc.psum_pool(name="psum", bufs=8))
 
         def zeroed_plane(shape, name):
             plane = keep.tile(shape, U8, name=name, align_bytes=64)
@@ -51,7 +51,7 @@ def tile_list_sense_drift_rewrite_kernel(
 
         def load_weight_scales(plane, scales):
             for q in range(4):
-                nc.gpsimd.dma_start(
+                nc.sync.dma_start(
                     plane[32 * q : 32 * q + 4, :, :].bitcast(I32),
                     scales[:, 4 * q : 4 * q + 4, :].rearrange("a q c -> q a c").bitcast(I32),
                 )
@@ -67,8 +67,6 @@ def tile_list_sense_drift_rewrite_kernel(
         tab_plane = zeroed_plane([P, T], "tab_plane")
         w3_plane = zeroed_plane([P, PASSES, N], "w3_plane")
         w2_plane = zeroed_plane([P, PASSES, N], "w2_plane")
-        load_weight_scales(w3_plane, w3_scales)
-        load_weight_scales(w2_plane, w2_scales)
 
         offsets = keep.tile([P, S // PER_COLUMN], U16, name="offsets")
         nc.sync.dma_start(offsets[:], offs)
@@ -81,19 +79,21 @@ def tile_list_sense_drift_rewrite_kernel(
         tab = [load_table_pass(0)]
         gains = keep.tile([P, PASSES, PACK], F32, name="gains")
         nc.sync.dma_start(gains[:], gain.rearrange("(b p t) -> p b t", b=PASSES, t=PACK))
-        w1_raw[0, 1] = load_w1(0, 1)
+        load_weight_scales(w3_plane, w3_scales)
         tab.append(load_table_pass(1))
+        load_weight_scales(w2_plane, w2_scales)
+        w1_raw[0, 1] = load_w1(0, 1)
         w1_raw[1, 0] = load_w1(1, 0)
-        w1_raw[1, 1] = load_w1(1, 1)
         state = [keep.tile([P, T], F32, name="state%d" % n) for n in range(ROW_TILES)]
-        for n in range(2):
+        nc.sync.dma_start(state[0][:], gT[0:P, :])
+        w1_raw[1, 1] = load_w1(1, 1)
+        for n in range(1, ROW_TILES - 1):
             nc.sync.dma_start(state[n][:], gT[n * P : (n + 1) * P, :])
         w3_codes = keep.tile([P, PASSES, N], U32, name="w3_codes", align_bytes=64)
         nc.sync.dma_start(w3_codes[:].bitcast(I32), w3_words.rearrange("a p c i -> p a (c i)").bitcast(I32))
-        nc.sync.dma_start(state[2][:], gT[2 * P : 3 * P, :])
+        nc.sync.dma_start(state[ROW_TILES - 1][:], gT[(ROW_TILES - 1) * P :, :])
         w2_codes = keep.tile([P, PASSES, 2 * N], U8, name="w2_codes", align_bytes=64)
         nc.sync.dma_start(w2_codes[:].bitcast(I32), w2_words.rearrange("a p c -> p a c").bitcast(I32))
-        nc.sync.dma_start(state[ROW_TILES - 1][:], gT[(ROW_TILES - 1) * P :, :])
 
         def listed(first, count):
             return offsets[:, first // PER_COLUMN : (first + count) // PER_COLUMN]
@@ -116,9 +116,8 @@ def tile_list_sense_drift_rewrite_kernel(
         v_codes = [keep.tile([P, S], U32, name="v_codes%d" % a, align_bytes=64) for a in range(PASSES)]
         nc.vector.tensor_copy(v_codes[0][:], tab[0][:].indirect(offsets[:]))
         quantise_w1(0, 0, [nc.scalar.copy])
+        nc.vector.tensor_copy(v_codes[1][:], tab[1][:].indirect(offsets[:]))
         quantise_w1(0, 1, [nc.vector.tensor_copy, nc.scalar.copy])
-        nc.vector.tensor_copy(v_codes[1][:, :WIDTH], tab[1][:].indirect(listed(0, WIDTH)))
-        nc.vector.tensor_copy(v_codes[1][:, WIDTH:], tab[1][:].indirect(listed(WIDTH, S - WIDTH)))
         quantise_w1(1, 0, [nc.vector.tensor_copy])
         quantise_w1(1, 1, [nc.vector.tensor_copy])
 
@@ -132,7 +131,7 @@ def tile_list_sense_drift_rewrite_kernel(
             return slice(s * WIDTH, (s + 1) * WIDTH)
 
         def times_table(acc, codes, planes, first_column, cols):
-            for i in range(2):
+            for i in range(acc.shape[1]):
                 m = slice(first_column + i * P, first_column + (i + 1) * P)
                 for a in range(PASSES):
                     nc.tensor.matmul_mx(
@@ -145,53 +144,40 @@ def tile_list_sense_drift_rewrite_kernel(
                         stop=a == PASSES - 1,
                     )
 
-        grouped = [
-            keep.tile([P, PASSES, WIDTH * PACK], BF16, name="h_grouped%d" % s, align_bytes=64) for s in range(SLICES)
-        ]
-
-        h_rows = {}
-
-        def hidden_half(s, b, t0):
-            if t0 == 0:
-                h_rows[s, b] = keep.tile([P, PACK, WIDTH], BF16, name="h_rows", tag="rows%d_%d" % (s, b))
-            pre = psum.tile([P, 2, WIDTH], F32, name="pre", bufs=4)
-            times_table(
-                pre,
-                [w1_codes[b, a] for a in range(PASSES)],
-                [w1_plane[b, a] for a in range(PASSES)],
-                t0 * P,
-                columns(s),
-            )
-            act = ring.tile([P, 2, WIDTH], F32, name="act")
-            nc.scalar.activation(act[:], pre[:], TANH)
-            for i in range(2):
-                nc.scalar.activation(
-                    h_rows[s, b][:, t0 + i, :], act[:, i, :], COPY, scale=gains[:, b, t0 + i : t0 + i + 1]
-                )
-            if t0 == 2:
-                nc.scalar.copy(
-                    grouped[s][:, b, :].rearrange("p (c i t) -> p c t i", i=4, t=PACK),
-                    h_rows[s, b][:].rearrange("p t (c i) -> p c t i", i=4),
-                )
+        grouped, h_codes, h_plane = {}, {}, {}
 
         def hidden(s, b):
-            hidden_half(s, b, 0)
-            hidden_half(s, b, 2)
-
-        h = {}
-
-        def quantise_h(s):
-            codes = keep.tile([P, PASSES, WIDTH], U32, name="h_codes%d" % s, align_bytes=64)
-            plane = keep.tile([P, PASSES, WIDTH], U8, name="h_plane%d" % s, align_bytes=64)
-            nc.vector.quantize_mx(
-                codes[:].rearrange("p b c -> p (b c)").bitcast(E4M3),
-                plane[:].rearrange("p b c -> p (b c)"),
-                grouped[s][:].rearrange("p b c -> p (b c)"),
+            h_rows = ring.tile([P, PACK, WIDTH], BF16, name="h_rows", bufs=2)
+            for t0 in range(0, PACK, 2):
+                pre = psum.tile([P, 2, WIDTH], F32, name="pre", tag="bank")
+                times_table(
+                    pre,
+                    [w1_codes[b, a] for a in range(PASSES)],
+                    [w1_plane[b, a] for a in range(PASSES)],
+                    t0 * P,
+                    columns(s),
+                )
+                act = ring.tile([P, 2, WIDTH], F32, name="act")
+                nc.scalar.activation(act[:], pre[:], TANH)
+                for i in range(2):
+                    nc.scalar.activation(
+                        h_rows[:, t0 + i, :], act[:, i, :], COPY, scale=gains[:, b, t0 + i : t0 + i + 1]
+                    )
+            grouped[s, b] = ring.tile(
+                [P, WIDTH * PACK], BF16, name="grouped", tag="from_scalar", bufs=12, align_bytes=64
             )
-            h[s] = (codes, plane)
+            nc.scalar.copy(
+                grouped[s, b][:].rearrange("p (c i t) -> p c t i", i=4, t=PACK),
+                h_rows[:].rearrange("p t (c i) -> p c t i", i=4),
+            )
 
-        def linear_pair(s, n0, tag):
-            d_acc = psum.tile([P, 2, WIDTH], F32, name="d_acc")
+        def quantise_h(s, b):
+            h_codes[s, b] = ring.tile([P, WIDTH], U32, name="h_codes", tag="from_vector", bufs=8, align_bytes=64)
+            h_plane[s, b] = keep.tile([P, WIDTH], U8, name="h_plane%d_%d" % (s, b), align_bytes=64)
+            nc.vector.quantize_mx(h_codes[s, b][:].bitcast(E4M3), h_plane[s, b][:], grouped[s, b][:])
+
+        def linear_pair(s, n0):
+            d_acc = psum.tile([P, 2, WIDTH], F32, name="d_acc", tag="bank")
             times_table(
                 d_acc,
                 [w3_codes[:, a, :] for a in range(PASSES)],
@@ -199,13 +185,12 @@ def tile_list_sense_drift_rewrite_kernel(
                 n0 * P,
                 columns(s),
             )
-            linear = keep.tile([P, 2, WIDTH], F32, name="linear", tag=tag)
+            linear = ring.tile([P, 2, WIDTH], F32, name="linear", tag="from_scalar", bufs=12, align_bytes=64)
             nc.scalar.copy(linear[:], d_acc[:])
             return linear
 
-        def drift_pair(dst, s, n0, linear):
-            codes, plane = h[s]
-            y_acc = psum.tile([P, 2, WIDTH], F32, name="y_acc")
+        def nonlinear_pair(s, n0):
+            y_acc = psum.tile([P, 2, WIDTH], F32, name="y_acc", tag="bank")
             for i in range(2):
                 n = n0 + i
                 for c in range(WIDTH // P):
@@ -214,48 +199,60 @@ def tile_list_sense_drift_rewrite_kernel(
                             y_acc[:, i, c * P : (c + 1) * P],
                             lhsT=w2_codes[:, b, 2 * n * P : 2 * (n + 1) * P].bitcast(E2M1),
                             lhsT_scale=w2_plane[:, b, n * P : (n + 1) * P],
-                            rhs=codes[:, b, c * P : (c + 1) * P].bitcast(E4M3),
-                            rhs_scale=plane[:, b, c * P : (c + 1) * P],
+                            rhs=h_codes[s, b][:, c * P : (c + 1) * P].bitcast(E4M3),
+                            rhs_scale=h_plane[s, b][:, c * P : (c + 1) * P],
                             start=(b == 0),
                             stop=(b == PASSES - 1),
                         )
-            nc.vector.tensor_tensor(dst, y_acc[:], linear[:], MULT)
+            return y_acc
 
-        drift = keep.tile([P, ROW_TILES, S], F32, name="drift")
+        def drift_tile(width):
+            return ring.tile([P, 2, width], F32, name="drift", tag="from_vector", bufs=8, align_bytes=64)
 
-        def put_back(n, first, count):
+        def put_back(n, first, drift):
+            count = drift.shape[1]
             nc.vector.tensor_tensor(
-                state[n][:].indirect(listed(first, count)),
-                picked[n][:, first : first + count],
-                drift[:, n, first : first + count],
-                ADD,
+                state[n][:].indirect(listed(first, count)), picked[n][:, first : first + count], drift, ADD
             )
-
-        def pair(s, n0, tag):
-            drift_pair(drift[:, n0 : n0 + 2, columns(s)], s, n0, linear_pair(s, n0, tag))
 
         last = SLICES - 1
         hidden(0, 0)
-        hidden_half(1, 0, 0)
+        quantise_h(0, 0)
+        hidden(1, 0)
         hidden(0, 1)
-        quantise_h(0)
+        quantise_h(0, 1)
+        linear = linear_pair(0, 0)
         for s in range(SLICES):
-            pair(s, 0, "linear%d" % s)
-            put_back(0, s * WIDTH, WIDTH)
-            put_back(1, s * WIDTH, WIDTH)
+            first = s * WIDTH
             if s < last:
-                if s > 0:
-                    hidden_half(s + 1, 0, 0)
-                hidden_half(s + 1, 0, 2)
                 hidden(s + 1, 1)
-                quantise_h(s + 1)
-                pair(s, 2, "rows%d_1" % (s + 1))
-            else:
-                pair(s, 2, "linear_last")
-            put_back(2, s * WIDTH, WIDTH)
+            y_low = nonlinear_pair(s, 0)
+            linear_high = linear_pair(s, 2)
+            y_high = nonlinear_pair(s, 2)
+            drift = drift_tile(WIDTH)
+            nc.vector.tensor_tensor(drift[:], y_low[:], linear[:], MULT)
+            if s < last:
+                quantise_h(s + 1, 0)
+            put_back(0, first, drift[:, 0, :])
+            put_back(1, first, drift[:, 1, :])
             if s < last - 1:
-                put_back(3, s * WIDTH, WIDTH)
-        put_back(3, (last - 1) * WIDTH, 2 * WIDTH)
+                drift = drift_tile(WIDTH)
+                high = drift[:]
+            elif s < last:
+                wide = drift_tile(2 * WIDTH)
+                high = wide[:, :, :WIDTH]
+            else:
+                high = wide[:, :, WIDTH:]
+            nc.vector.tensor_tensor(high, y_high[:], linear_high[:], MULT)
+            if s < last:
+                quantise_h(s + 1, 1)
+            put_back(2, first, high[:, 0, :])
+            if s < last - 1:
+                put_back(3, first, high[:, 1, :])
+                hidden(s + 2, 0)
+            if s < last:
+                linear = linear_pair(s + 1, 0)
+        put_back(3, (last - 1) * WIDTH, wide[:, 1, :])
 
         for n in range(ROW_TILES):
             nc.sync.dma_start(out[n * P : (n + 1) * P, :], state[n][:])

@@ -49,11 +49,15 @@ def tile_list_sense_drift_rewrite_kernel(
             nc.sync.dma_start(words[:].bitcast(I32), tab_words[a].rearrange("p t i -> p (t i)").bitcast(I32))
             return words
 
+        def load_table_scales(a):
+            for r in range(4):
+                row = TAB_PLANE_ROW + 4 * a + r
+                nc.sync.dma_start(tab_plane[row:P:32, :].bitcast(I32), tab_scales[a, r:16:4, :].bitcast(I32))
+
         def load_weight_scales(plane, scales):
-            for q in range(4):
+            for r in range(4):
                 nc.sync.dma_start(
-                    plane[32 * q : 32 * q + 4, :, :].bitcast(I32),
-                    scales[:, 4 * q : 4 * q + 4, :].rearrange("a q c -> q a c").bitcast(I32),
+                    plane[r:P:32, :, :].bitcast(I32), scales[:, r:16:4, :].rearrange("a q c -> q a c").bitcast(I32)
                 )
 
         def load_w1(b, a):
@@ -68,21 +72,18 @@ def tile_list_sense_drift_rewrite_kernel(
         w3_plane = zeroed_plane([P, PASSES, N], "w3_plane")
         w2_plane = zeroed_plane([P, PASSES, N], "w2_plane")
 
+        tab = [load_table_pass(0)]
         offsets = keep.tile([P, S // PER_COLUMN], U16, name="offsets")
         nc.sync.dma_start(offsets[:], offs)
-        w1_raw = {(0, 0): load_w1(0, 0)}
-        for q in range(4):
-            row = 32 * q + TAB_PLANE_ROW
-            nc.sync.dma_start(
-                tab_plane[row : row + 8, :].bitcast(I32), tab_scales[:, 4 * q : 4 * q + 4, :].bitcast(I32)
-            )
-        tab = [load_table_pass(0)]
+        load_table_scales(0)
+        tab.append(load_table_pass(1))
         gains = keep.tile([P, PASSES, PACK], F32, name="gains")
         nc.sync.dma_start(gains[:], gain.rearrange("(b p t) -> p b t", b=PASSES, t=PACK))
+        load_table_scales(1)
+        w1_raw = {(0, 0): load_w1(0, 0)}
         load_weight_scales(w3_plane, w3_scales)
-        tab.append(load_table_pass(1))
-        load_weight_scales(w2_plane, w2_scales)
         w1_raw[0, 1] = load_w1(0, 1)
+        load_weight_scales(w2_plane, w2_scales)
         w1_raw[1, 0] = load_w1(1, 0)
         state = [keep.tile([P, T], F32, name="state%d" % n) for n in range(ROW_TILES)]
         nc.sync.dma_start(state[0][:], gT[0:P, :])
@@ -107,25 +108,33 @@ def tile_list_sense_drift_rewrite_kernel(
             share = P // len(engines)
             for i, cast in enumerate(engines):
                 cast(dst[:, i * share : (i + 1) * share], src[:, i * share : (i + 1) * share])
-            w1_codes[b, a] = keep.tile([P, PASS], U32, name="w1_codes%d%d" % (b, a), align_bytes=64)
+            if (b, a) == (1, 1):
+                w1_codes[b, a] = ring.tile([P, PASS], U32, name="w1_codes", tag="from_vector", bufs=13, align_bytes=64)
+            else:
+                w1_codes[b, a] = keep.tile([P, PASS], U32, name="w1_codes%d%d" % (b, a), align_bytes=64)
             w1_plane[b, a] = keep.tile([P, PASS], U8, name="w1_plane%d%d" % (b, a), align_bytes=64)
             nc.vector.quantize_mx(w1_codes[b, a][:].bitcast(E4M3), w1_plane[b, a][:], grouped[:])
 
-        v_plane = keep.tile([P, S], U8, name="v_plane", align_bytes=64)
-        nc.vector.tensor_copy(v_plane[:], tab_plane[:].indirect(offsets[:]))
         v_codes = [keep.tile([P, S], U32, name="v_codes%d" % a, align_bytes=64) for a in range(PASSES)]
         nc.vector.tensor_copy(v_codes[0][:], tab[0][:].indirect(offsets[:]))
-        quantise_w1(0, 0, [nc.scalar.copy])
         nc.vector.tensor_copy(v_codes[1][:], tab[1][:].indirect(offsets[:]))
+        v_plane = keep.tile([P, S], U8, name="v_plane", align_bytes=64)
+        nc.vector.tensor_copy(v_plane[:], tab_plane[:].indirect(offsets[:]))
+        quantise_w1(0, 0, [nc.scalar.copy])
         quantise_w1(0, 1, [nc.vector.tensor_copy, nc.scalar.copy])
         quantise_w1(1, 0, [nc.vector.tensor_copy])
-        quantise_w1(1, 1, [nc.vector.tensor_copy])
 
         picked = []
-        for n in range(ROW_TILES):
-            tile = keep.tile([P, S], F32, name="picked%d" % n)
+
+        def pick(n):
+            tile = ring.tile([P, S], F32, name="picked", tag="from_vector", bufs=13, align_bytes=64)
             nc.vector.tensor_copy(tile[:], state[n][:].indirect(offsets[:]))
             picked.append(tile)
+
+        pick(0)
+        quantise_w1(1, 1, [nc.vector.tensor_copy])
+        pick(1)
+        pick(2)
 
         def columns(s):
             return slice(s * WIDTH, (s + 1) * WIDTH)
@@ -172,7 +181,7 @@ def tile_list_sense_drift_rewrite_kernel(
             )
 
         def quantise_h(s, b):
-            h_codes[s, b] = ring.tile([P, WIDTH], U32, name="h_codes", tag="from_vector", bufs=8, align_bytes=64)
+            h_codes[s, b] = ring.tile([P, WIDTH], U32, name="h_codes", tag="from_vector", bufs=13, align_bytes=64)
             h_plane[s, b] = keep.tile([P, WIDTH], U8, name="h_plane%d_%d" % (s, b), align_bytes=64)
             nc.vector.quantize_mx(h_codes[s, b][:].bitcast(E4M3), h_plane[s, b][:], grouped[s, b][:])
 
@@ -207,7 +216,7 @@ def tile_list_sense_drift_rewrite_kernel(
             return y_acc
 
         def drift_tile(width):
-            return ring.tile([P, 2, width], F32, name="drift", tag="from_vector", bufs=8, align_bytes=64)
+            return ring.tile([P, 2, width], F32, name="drift", tag="from_vector", bufs=13, align_bytes=64)
 
         def put_back(n, first, drift):
             count = drift.shape[1]
@@ -221,6 +230,7 @@ def tile_list_sense_drift_rewrite_kernel(
         hidden(1, 0)
         hidden(0, 1)
         quantise_h(0, 1)
+        pick(3)
         linear = linear_pair(0, 0)
         for s in range(SLICES):
             first = s * WIDTH

@@ -26,6 +26,7 @@ BANK = 512
 ROW_TILES = N // P
 PER_COLUMN = 16
 TAB_PLANE_ROW = 8
+W3_PLANE_ROW = 12
 WIDTH = 256
 SLICES = S // WIDTH
 
@@ -49,16 +50,19 @@ def tile_list_sense_drift_rewrite_kernel(
             nc.sync.dma_start(words[:].bitcast(I32), tab_words[a].rearrange("p t i -> p (t i)").bitcast(I32))
             return words
 
-        def load_table_scales(a):
-            for r in range(4):
-                row = TAB_PLANE_ROW + 4 * a + r
-                nc.sync.dma_start(tab_plane[row:P:32, :].bitcast(I32), tab_scales[a, r:16:4, :].bitcast(I32))
+        def load_table_scales(rows):
+            for r in rows:
+                for a in range(PASSES):
+                    row = TAB_PLANE_ROW + 4 * a + r
+                    nc.sync.dma_start(tab_plane[row:P:32, :].bitcast(I32), tab_scales[a, r:16:4, :].bitcast(I32))
 
-        def load_weight_scales(plane, scales):
-            for r in range(4):
-                nc.sync.dma_start(
-                    plane[r:P:32, :, :].bitcast(I32), scales[:, r:16:4, :].rearrange("a q c -> q a c").bitcast(I32)
-                )
+        def load_weight_scales(rows):
+            for r in rows:
+                for plane, scales, row in ((w3_plane, w3_scales, W3_PLANE_ROW + r), (w2_plane, w2_scales, r)):
+                    nc.sync.dma_start(
+                        plane[row:P:32, :, :].bitcast(I32),
+                        scales[:, r:16:4, :].rearrange("a q c -> q a c").bitcast(I32),
+                    )
 
         def load_w1(b, a):
             raw = keep.tile([P, PACK, PASS], F32, name="w1_raw%d%d" % (b, a))
@@ -75,26 +79,33 @@ def tile_list_sense_drift_rewrite_kernel(
         tab = [load_table_pass(0)]
         offsets = keep.tile([P, S // PER_COLUMN], U16, name="offsets")
         nc.sync.dma_start(offsets[:], offs)
-        load_table_scales(0)
+        load_table_scales((0, 1))
         tab.append(load_table_pass(1))
         gains = keep.tile([P, PASSES, PACK], F32, name="gains")
         nc.sync.dma_start(gains[:], gain.rearrange("(b p t) -> p b t", b=PASSES, t=PACK))
-        load_table_scales(1)
+        load_table_scales((2, 3))
         w1_raw = {(0, 0): load_w1(0, 0)}
-        load_weight_scales(w3_plane, w3_scales)
+        load_weight_scales((0, 1))
         w1_raw[0, 1] = load_w1(0, 1)
-        load_weight_scales(w2_plane, w2_scales)
+        load_weight_scales((2, 3))
         w1_raw[1, 0] = load_w1(1, 0)
         state = [keep.tile([P, T], F32, name="state%d" % n) for n in range(ROW_TILES)]
         nc.sync.dma_start(state[0][:], gT[0:P, :])
         w1_raw[1, 1] = load_w1(1, 1)
-        for n in range(1, ROW_TILES - 1):
+        for n in range(1, ROW_TILES):
             nc.sync.dma_start(state[n][:], gT[n * P : (n + 1) * P, :])
-        w3_codes = keep.tile([P, PASSES, N], U32, name="w3_codes", align_bytes=64)
-        nc.sync.dma_start(w3_codes[:].bitcast(I32), w3_words.rearrange("a p c i -> p a (c i)").bitcast(I32))
-        nc.sync.dma_start(state[ROW_TILES - 1][:], gT[(ROW_TILES - 1) * P :, :])
-        w2_codes = keep.tile([P, PASSES, 2 * N], U8, name="w2_codes", align_bytes=64)
-        nc.sync.dma_start(w2_codes[:].bitcast(I32), w2_words.rearrange("a p c -> p a c").bitcast(I32))
+        w3_codes, w2_codes = [], []
+        for half in range(2):
+            cols = slice(half * N // 2, (half + 1) * N // 2)
+            w3_codes.append(keep.tile([P, PASSES, N // 2], U32, name="w3_codes%d" % half, align_bytes=64))
+            nc.sync.dma_start(
+                w3_codes[half][:].bitcast(I32), w3_words.rearrange("a p c i -> p a (c i)").bitcast(I32)[:, :, cols]
+            )
+            w2_codes.append(keep.tile([P, PASSES, N], U8, name="w2_codes%d" % half, align_bytes=64))
+            nc.sync.dma_start(
+                w2_codes[half][:].bitcast(I32),
+                w2_words.rearrange("a p c -> p a c")[:, :, half * N : (half + 1) * N].bitcast(I32),
+            )
 
         def listed(first, count):
             return offsets[:, first // PER_COLUMN : (first + count) // PER_COLUMN]
@@ -155,30 +166,40 @@ def tile_list_sense_drift_rewrite_kernel(
 
         grouped, h_codes, h_plane = {}, {}, {}
 
-        def hidden(s, b):
-            h_rows = ring.tile([P, PACK, WIDTH], BF16, name="h_rows", bufs=2)
-            for t0 in range(0, PACK, 2):
-                pre = psum.tile([P, 2, WIDTH], F32, name="pre", tag="bank")
-                times_table(
-                    pre,
-                    [w1_codes[b, a] for a in range(PASSES)],
-                    [w1_plane[b, a] for a in range(PASSES)],
-                    t0 * P,
-                    columns(s),
+        h_rows = {}
+
+        def first_sums(s, b, t0):
+            pre = psum.tile([P, 2, WIDTH], F32, name="pre", tag="bank")
+            times_table(
+                pre,
+                [w1_codes[b, a] for a in range(PASSES)],
+                [w1_plane[b, a] for a in range(PASSES)],
+                t0 * P,
+                columns(s),
+            )
+            return pre
+
+        def hidden_half(s, b, t0, pre):
+            if t0 == 0:
+                h_rows[s, b] = ring.tile([P, PACK, WIDTH], BF16, name="h_rows", bufs=3)
+            act = ring.tile([P, 2, WIDTH], F32, name="act", tag="from_scalar", bufs=16, align_bytes=64)
+            nc.scalar.activation(act[:], pre[:], TANH)
+            for i in range(2):
+                nc.scalar.activation(
+                    h_rows[s, b][:, t0 + i, :], act[:, i, :], COPY, scale=gains[:, b, t0 + i : t0 + i + 1]
                 )
-                act = ring.tile([P, 2, WIDTH], F32, name="act")
-                nc.scalar.activation(act[:], pre[:], TANH)
-                for i in range(2):
-                    nc.scalar.activation(
-                        h_rows[:, t0 + i, :], act[:, i, :], COPY, scale=gains[:, b, t0 + i : t0 + i + 1]
-                    )
-            grouped[s, b] = ring.tile(
-                [P, WIDTH * PACK], BF16, name="grouped", tag="from_scalar", bufs=12, align_bytes=64
-            )
-            nc.scalar.copy(
-                grouped[s, b][:].rearrange("p (c i t) -> p c t i", i=4, t=PACK),
-                h_rows[:].rearrange("p t (c i) -> p c t i", i=4),
-            )
+            if t0 == 2:
+                grouped[s, b] = ring.tile(
+                    [P, WIDTH * PACK], BF16, name="grouped", tag="from_scalar", bufs=16, align_bytes=64
+                )
+                nc.scalar.copy(
+                    grouped[s, b][:].rearrange("p (c i t) -> p c t i", i=4, t=PACK),
+                    h_rows[s, b][:].rearrange("p t (c i) -> p c t i", i=4),
+                )
+
+        def hidden(s, b):
+            hidden_half(s, b, 0, first_sums(s, b, 0))
+            hidden_half(s, b, 2, first_sums(s, b, 2))
 
         def quantise_h(s, b):
             h_codes[s, b] = ring.tile([P, WIDTH], U32, name="h_codes", tag="from_vector", bufs=13, align_bytes=64)
@@ -189,12 +210,12 @@ def tile_list_sense_drift_rewrite_kernel(
             d_acc = psum.tile([P, 2, WIDTH], F32, name="d_acc", tag="bank")
             times_table(
                 d_acc,
-                [w3_codes[:, a, :] for a in range(PASSES)],
-                [w3_plane[:, a, :] for a in range(PASSES)],
-                n0 * P,
+                [w3_codes[n0 // 2][:, a, :] for a in range(PASSES)],
+                [w3_plane[W3_PLANE_ROW:, a, n0 * P : (n0 + 2) * P] for a in range(PASSES)],
+                0,
                 columns(s),
             )
-            linear = ring.tile([P, 2, WIDTH], F32, name="linear", tag="from_scalar", bufs=12, align_bytes=64)
+            linear = ring.tile([P, 2, WIDTH], F32, name="linear", tag="from_scalar", bufs=16, align_bytes=64)
             nc.scalar.copy(linear[:], d_acc[:])
             return linear
 
@@ -206,7 +227,7 @@ def tile_list_sense_drift_rewrite_kernel(
                     for b in range(PASSES):
                         nc.tensor.matmul_mx(
                             y_acc[:, i, c * P : (c + 1) * P],
-                            lhsT=w2_codes[:, b, 2 * n * P : 2 * (n + 1) * P].bitcast(E2M1),
+                            lhsT=w2_codes[n0 // 2][:, b, 2 * i * P : 2 * (i + 1) * P].bitcast(E2M1),
                             lhsT_scale=w2_plane[:, b, n * P : (n + 1) * P],
                             rhs=h_codes[s, b][:, c * P : (c + 1) * P].bitcast(E4M3),
                             rhs_scale=h_plane[s, b][:, c * P : (c + 1) * P],
@@ -227,16 +248,21 @@ def tile_list_sense_drift_rewrite_kernel(
         last = SLICES - 1
         hidden(0, 0)
         quantise_h(0, 0)
-        hidden(1, 0)
+        hidden_half(1, 0, 0, first_sums(1, 0, 0))
         hidden(0, 1)
         quantise_h(0, 1)
         pick(3)
+        hidden_half(1, 0, 2, first_sums(1, 0, 2))
+        ahead = [first_sums(1, 1, t0) for t0 in (0, 2)]
         linear = linear_pair(0, 0)
         for s in range(SLICES):
             first = s * WIDTH
-            if s < last:
+            if 0 < s < last:
                 hidden(s + 1, 1)
             y_low = nonlinear_pair(s, 0)
+            if s == 0:
+                hidden_half(1, 1, 0, ahead[0])
+                hidden_half(1, 1, 2, ahead[1])
             linear_high = linear_pair(s, 2)
             y_high = nonlinear_pair(s, 2)
             drift = drift_tile(WIDTH)

@@ -80,32 +80,38 @@ def tile_list_sense_drift_rewrite_kernel(
         offsets = keep.tile([P, S // PER_COLUMN], U16, name="offsets")
         nc.sync.dma_start(offsets[:], offs)
         load_table_scales((0, 1))
-        tab.append(load_table_pass(1))
+        w1_raw = {(0, 0): load_w1(0, 0)}
         gains = keep.tile([P, PASSES, PACK], F32, name="gains")
         nc.sync.dma_start(gains[:], gain.rearrange("(b p t) -> p b t", b=PASSES, t=PACK))
         load_table_scales((2, 3))
-        w1_raw = {(0, 0): load_w1(0, 0)}
-        load_weight_scales((0, 1))
         w1_raw[0, 1] = load_w1(0, 1)
-        load_weight_scales((2, 3))
+        tab.append(load_table_pass(1))
+        load_weight_scales((0, 1))
         w1_raw[1, 0] = load_w1(1, 0)
+        load_weight_scales((2, 3))
         state = [keep.tile([P, T], F32, name="state%d" % n) for n in range(ROW_TILES)]
         nc.sync.dma_start(state[0][:], gT[0:P, :])
         w1_raw[1, 1] = load_w1(1, 1)
-        for n in range(1, ROW_TILES):
+
+        def load_w3_half(half):
+            codes = keep.tile([P, PASSES, N // 2], U32, name="w3_codes%d" % half, align_bytes=64)
+            words = w3_words.rearrange("a p c i -> p a (c i)").bitcast(I32)
+            nc.sync.dma_start(codes[:].bitcast(I32), words[:, :, half * N // 2 : (half + 1) * N // 2])
+            return codes
+
+        def load_w2_half(half):
+            codes = keep.tile([P, PASSES, N], U8, name="w2_codes%d" % half, align_bytes=64)
+            words = w2_words.rearrange("a p c -> p a c")[:, :, half * N : (half + 1) * N]
+            nc.sync.dma_start(codes[:].bitcast(I32), words.bitcast(I32))
+            return codes
+
+        for n in range(1, ROW_TILES - 1):
             nc.sync.dma_start(state[n][:], gT[n * P : (n + 1) * P, :])
-        w3_codes, w2_codes = [], []
-        for half in range(2):
-            cols = slice(half * N // 2, (half + 1) * N // 2)
-            w3_codes.append(keep.tile([P, PASSES, N // 2], U32, name="w3_codes%d" % half, align_bytes=64))
-            nc.sync.dma_start(
-                w3_codes[half][:].bitcast(I32), w3_words.rearrange("a p c i -> p a (c i)").bitcast(I32)[:, :, cols]
-            )
-            w2_codes.append(keep.tile([P, PASSES, N], U8, name="w2_codes%d" % half, align_bytes=64))
-            nc.sync.dma_start(
-                w2_codes[half][:].bitcast(I32),
-                w2_words.rearrange("a p c -> p a c")[:, :, half * N : (half + 1) * N].bitcast(I32),
-            )
+        w3_codes = [load_w3_half(0)]
+        nc.sync.dma_start(state[ROW_TILES - 1][:], gT[(ROW_TILES - 1) * P :, :])
+        w2_codes = [load_w2_half(0)]
+        w3_codes.append(load_w3_half(1))
+        w2_codes.append(load_w2_half(1))
 
         def listed(first, count):
             return offsets[:, first // PER_COLUMN : (first + count) // PER_COLUMN]
@@ -128,11 +134,12 @@ def tile_list_sense_drift_rewrite_kernel(
 
         v_codes = [keep.tile([P, S], U32, name="v_codes%d" % a, align_bytes=64) for a in range(PASSES)]
         nc.vector.tensor_copy(v_codes[0][:], tab[0][:].indirect(offsets[:]))
-        nc.vector.tensor_copy(v_codes[1][:], tab[1][:].indirect(offsets[:]))
         v_plane = keep.tile([P, S], U8, name="v_plane", align_bytes=64)
         nc.vector.tensor_copy(v_plane[:], tab_plane[:].indirect(offsets[:]))
         quantise_w1(0, 0, [nc.scalar.copy])
         quantise_w1(0, 1, [nc.vector.tensor_copy, nc.scalar.copy])
+        nc.vector.tensor_copy(v_codes[1][:, : S // 2], tab[1][:].indirect(listed(0, S // 2)))
+        nc.vector.tensor_copy(v_codes[1][:, S // 2 :], tab[1][:].indirect(listed(S // 2, S // 2)))
         quantise_w1(1, 0, [nc.vector.tensor_copy])
 
         picked = []
@@ -197,6 +204,29 @@ def tile_list_sense_drift_rewrite_kernel(
                     h_rows[s, b][:].rearrange("p t (c i) -> p c t i", i=4),
                 )
 
+        def first_block_wide():
+            rows = keep.tile([P, PACK, 2 * WIDTH], BF16, name="rows_wide")
+            for t in range(PACK):
+                pre = psum.tile([P, 1, 2 * WIDTH], F32, name="pre", tag="bank")
+                times_table(
+                    pre,
+                    [w1_codes[0, a] for a in range(PASSES)],
+                    [w1_plane[0, a] for a in range(PASSES)],
+                    t * P,
+                    slice(0, 2 * WIDTH),
+                )
+                act = ring.tile([P, 2 * WIDTH], F32, name="act", tag="from_scalar", bufs=16, align_bytes=64)
+                nc.scalar.activation(act[:], pre[:, 0, :], TANH)
+                nc.scalar.activation(rows[:, t, :], act[:], COPY, scale=gains[:, 0, t : t + 1])
+            for s in range(2):
+                grouped[s, 0] = ring.tile(
+                    [P, WIDTH * PACK], BF16, name="grouped", tag="from_scalar", bufs=16, align_bytes=64
+                )
+                nc.scalar.copy(
+                    grouped[s, 0][:].rearrange("p (c i t) -> p c t i", i=4, t=PACK),
+                    rows[:, :, columns(s)].rearrange("p t (c i) -> p c t i", i=4),
+                )
+
         def hidden(s, b):
             hidden_half(s, b, 0, first_sums(s, b, 0))
             hidden_half(s, b, 2, first_sums(s, b, 2))
@@ -246,13 +276,12 @@ def tile_list_sense_drift_rewrite_kernel(
             )
 
         last = SLICES - 1
-        hidden(0, 0)
+        first_block_wide()
         quantise_h(0, 0)
-        hidden_half(1, 0, 0, first_sums(1, 0, 0))
+        hidden_half(2, 0, 0, first_sums(2, 0, 0))
         hidden(0, 1)
         quantise_h(0, 1)
         pick(3)
-        hidden_half(1, 0, 2, first_sums(1, 0, 2))
         ahead = [first_sums(1, 1, t0) for t0 in (0, 2)]
         linear = linear_pair(0, 0)
         for s in range(SLICES):
@@ -285,7 +314,9 @@ def tile_list_sense_drift_rewrite_kernel(
             put_back(2, first, high[:, 0, :])
             if s < last - 1:
                 put_back(3, first, high[:, 1, :])
-                hidden(s + 2, 0)
+                if s > 0:
+                    hidden_half(s + 2, 0, 0, first_sums(s + 2, 0, 0))
+                hidden_half(s + 2, 0, 2, first_sums(s + 2, 0, 2))
             if s < last:
                 linear = linear_pair(s + 1, 0)
         put_back(3, (last - 1) * WIDTH, wide[:, 1, :])

@@ -158,18 +158,18 @@ def tile_list_sense_drift_rewrite_kernel(
             return slice(s * WIDTH, (s + 1) * WIDTH)
 
         def times_table(acc, codes, planes, first_column, cols):
-            for i in range(acc.shape[1]):
+            order = [(a, i) for a in range(PASSES) for i in range(acc.shape[1])]
+            for a, i in order:
                 m = slice(first_column + i * P, first_column + (i + 1) * P)
-                for a in range(PASSES):
-                    nc.tensor.matmul_mx(
-                        acc[:, i, :],
-                        lhsT=codes[a][:, m].bitcast(E4M3),
-                        lhsT_scale=planes[a][:, m],
-                        rhs=v_codes[a][:, cols].bitcast(E4M3),
-                        rhs_scale=v_plane[TAB_PLANE_ROW + 4 * a :, cols],
-                        start=a == 0,
-                        stop=a == PASSES - 1,
-                    )
+                nc.tensor.matmul_mx(
+                    acc[:, i, :],
+                    lhsT=codes[a][:, m].bitcast(E4M3),
+                    lhsT_scale=planes[a][:, m],
+                    rhs=v_codes[a][:, cols].bitcast(E4M3),
+                    rhs_scale=v_plane[TAB_PLANE_ROW + 4 * a :, cols],
+                    start=(a, i) == order[0],
+                    stop=(a, i) == order[-1],
+                )
 
         grouped, h_codes, h_plane = {}, {}, {}
 
@@ -251,19 +251,18 @@ def tile_list_sense_drift_rewrite_kernel(
 
         def nonlinear_pair(s, n0):
             y_acc = psum.tile([P, 2, WIDTH], F32, name="y_acc", tag="bank")
-            for i in range(2):
+            order = [(b, i, c) for b in range(PASSES) for i in range(2) for c in range(WIDTH // P)]
+            for b, i, c in order:
                 n = n0 + i
-                for c in range(WIDTH // P):
-                    for b in range(PASSES):
-                        nc.tensor.matmul_mx(
-                            y_acc[:, i, c * P : (c + 1) * P],
-                            lhsT=w2_codes[n0 // 2][:, b, 2 * i * P : 2 * (i + 1) * P].bitcast(E2M1),
-                            lhsT_scale=w2_plane[:, b, n * P : (n + 1) * P],
-                            rhs=h_codes[s, b][:, c * P : (c + 1) * P].bitcast(E4M3),
-                            rhs_scale=h_plane[s, b][:, c * P : (c + 1) * P],
-                            start=(b == 0),
-                            stop=(b == PASSES - 1),
-                        )
+                nc.tensor.matmul_mx(
+                    y_acc[:, i, c * P : (c + 1) * P],
+                    lhsT=w2_codes[n0 // 2][:, b, 2 * i * P : 2 * (i + 1) * P].bitcast(E2M1),
+                    lhsT_scale=w2_plane[:, b, n * P : (n + 1) * P],
+                    rhs=h_codes[s, b][:, c * P : (c + 1) * P].bitcast(E4M3),
+                    rhs_scale=h_plane[s, b][:, c * P : (c + 1) * P],
+                    start=(b, i, c) == order[0],
+                    stop=(b, i, c) == order[-1],
+                )
             return y_acc
 
         def drift_tile(width):
@@ -288,16 +287,20 @@ def tile_list_sense_drift_rewrite_kernel(
             first = s * WIDTH
             if 0 < s < last:
                 hidden(s + 1, 1)
+            if s > 0:
+                linear_high = linear_pair(s, 2)
             y_low = nonlinear_pair(s, 0)
             if s == 0:
                 hidden_half(1, 1, 0, ahead[0])
                 hidden_half(1, 1, 2, ahead[1])
-            linear_high = linear_pair(s, 2)
+                linear_high = linear_pair(s, 2)
             y_high = nonlinear_pair(s, 2)
             drift = drift_tile(WIDTH)
             nc.vector.tensor_tensor(drift[:], y_low[:], linear[:], MULT)
             if s < last:
                 quantise_h(s + 1, 0)
+            else:
+                nc.vector.tensor_tensor(wide[:, :, WIDTH:], y_high[:], linear_high[:], MULT)
             put_back(0, first, drift[:, 0, :])
             put_back(1, first, drift[:, 1, :])
             if s < last - 1:
@@ -308,8 +311,8 @@ def tile_list_sense_drift_rewrite_kernel(
                 high = wide[:, :, :WIDTH]
             else:
                 high = wide[:, :, WIDTH:]
-            nc.vector.tensor_tensor(high, y_high[:], linear_high[:], MULT)
             if s < last:
+                nc.vector.tensor_tensor(high, y_high[:], linear_high[:], MULT)
                 quantise_h(s + 1, 1)
             put_back(2, first, high[:, 0, :])
             if s < last - 1:

@@ -86,9 +86,7 @@ def tile_list_sense_drift_rewrite_kernel(
         load_table_scales((2, 3))
         w1_raw[0, 1] = load_w1(0, 1)
         tab.append(load_table_pass(1))
-        load_weight_scales((0, 1))
         w1_raw[1, 0] = load_w1(1, 0)
-        load_weight_scales((2, 3))
         state = [keep.tile([P, T], F32, name="state%d" % n) for n in range(ROW_TILES)]
         nc.sync.dma_start(state[0][:], gT[0:P, :])
         w1_raw[1, 1] = load_w1(1, 1)
@@ -105,10 +103,12 @@ def tile_list_sense_drift_rewrite_kernel(
             nc.sync.dma_start(codes[:].bitcast(I32), words.bitcast(I32))
             return codes
 
-        for n in range(1, ROW_TILES - 1):
-            nc.sync.dma_start(state[n][:], gT[n * P : (n + 1) * P, :])
+        nc.sync.dma_start(state[1][:], gT[P : 2 * P, :])
+        load_weight_scales((0, 1))
+        nc.sync.dma_start(state[2][:], gT[2 * P : 3 * P, :])
+        load_weight_scales((2, 3))
+        nc.sync.dma_start(state[3][:], gT[3 * P :, :])
         w3_codes = [load_w3_half(0)]
-        nc.sync.dma_start(state[ROW_TILES - 1][:], gT[(ROW_TILES - 1) * P :, :])
         w2_codes = [load_w2_half(0)]
         w3_codes.append(load_w3_half(1))
         w2_codes.append(load_w2_half(1))
@@ -122,35 +122,37 @@ def tile_list_sense_drift_rewrite_kernel(
             grouped = keep.tile([P, PACK * PASS], BF16, name="w1_grouped%d%d" % (b, a), align_bytes=64)
             dst = grouped[:].rearrange("p (t m j) -> p m j t", t=PACK, j=PACK)
             src = w1_raw[b, a][:].rearrange("p j (m t) -> p m j t", t=PACK)
-            share = P // len(engines)
-            for i, cast in enumerate(engines):
-                cast(dst[:, i * share : (i + 1) * share], src[:, i * share : (i + 1) * share])
-            if (b, a) == (1, 1):
-                w1_codes[b, a] = ring.tile([P, PASS], U32, name="w1_codes", tag="from_vector", bufs=13, align_bytes=64)
-            else:
-                w1_codes[b, a] = keep.tile([P, PASS], U32, name="w1_codes%d%d" % (b, a), align_bytes=64)
+            for u, cast in enumerate(engines):
+                cast(dst[:, :, :, 2 * u : 2 * u + 2], src[:, :, :, 2 * u : 2 * u + 2])
+            w1_codes[b, a] = ring.tile([P, PASS], U32, name="w1_codes", tag="from_vector", bufs=17, align_bytes=64)
             w1_plane[b, a] = keep.tile([P, PASS], U8, name="w1_plane%d%d" % (b, a), align_bytes=64)
-            nc.vector.quantize_mx(w1_codes[b, a][:].bitcast(E4M3), w1_plane[b, a][:], grouped[:])
+            for u in range(2):
+                half = slice(2 * u * P, 2 * (u + 1) * P)
+                nc.vector.quantize_mx(
+                    w1_codes[b, a][:, half].bitcast(E4M3),
+                    w1_plane[b, a][:, half],
+                    grouped[:, PACK * half.start : PACK * half.stop],
+                )
 
         v_codes = [keep.tile([P, S], U32, name="v_codes%d" % a, align_bytes=64) for a in range(PASSES)]
         nc.vector.tensor_copy(v_codes[0][:], tab[0][:].indirect(offsets[:]))
-        v_plane = keep.tile([P, S], U8, name="v_plane", align_bytes=64)
+        v_plane = ring.tile([P, S], U8, name="v_plane", tag="from_vector", bufs=17, align_bytes=64)
         nc.vector.tensor_copy(v_plane[:], tab_plane[:].indirect(offsets[:]))
-        quantise_w1(0, 0, [nc.scalar.copy])
+        quantise_w1(0, 0, [nc.scalar.copy, nc.scalar.copy])
         quantise_w1(0, 1, [nc.vector.tensor_copy, nc.scalar.copy])
         nc.vector.tensor_copy(v_codes[1][:, : S // 2], tab[1][:].indirect(listed(0, S // 2)))
         nc.vector.tensor_copy(v_codes[1][:, S // 2 :], tab[1][:].indirect(listed(S // 2, S // 2)))
-        quantise_w1(1, 0, [nc.vector.tensor_copy])
+        quantise_w1(1, 0, [nc.vector.tensor_copy, nc.vector.tensor_copy])
 
         picked = []
 
         def pick(n):
-            tile = ring.tile([P, S], F32, name="picked", tag="from_vector", bufs=13, align_bytes=64)
+            tile = ring.tile([P, S], F32, name="picked", tag="from_vector", bufs=17, align_bytes=64)
             nc.vector.tensor_copy(tile[:], state[n][:].indirect(offsets[:]))
             picked.append(tile)
 
         pick(0)
-        quantise_w1(1, 1, [nc.vector.tensor_copy])
+        quantise_w1(1, 1, [nc.vector.tensor_copy, nc.vector.tensor_copy])
         pick(1)
         pick(2)
 
@@ -232,7 +234,7 @@ def tile_list_sense_drift_rewrite_kernel(
             hidden_half(s, b, 2, first_sums(s, b, 2))
 
         def quantise_h(s, b):
-            h_codes[s, b] = ring.tile([P, WIDTH], U32, name="h_codes", tag="from_vector", bufs=13, align_bytes=64)
+            h_codes[s, b] = ring.tile([P, WIDTH], U32, name="h_codes", tag="from_vector", bufs=17, align_bytes=64)
             h_plane[s, b] = keep.tile([P, WIDTH], U8, name="h_plane%d_%d" % (s, b), align_bytes=64)
             nc.vector.quantize_mx(h_codes[s, b][:].bitcast(E4M3), h_plane[s, b][:], grouped[s, b][:])
 
@@ -266,7 +268,7 @@ def tile_list_sense_drift_rewrite_kernel(
             return y_acc
 
         def drift_tile(width):
-            return ring.tile([P, 2, width], F32, name="drift", tag="from_vector", bufs=13, align_bytes=64)
+            return ring.tile([P, 2, width], F32, name="drift", tag="from_vector", bufs=17, align_bytes=64)
 
         def put_back(n, first, drift):
             count = drift.shape[1]
@@ -281,7 +283,8 @@ def tile_list_sense_drift_rewrite_kernel(
         hidden(0, 1)
         quantise_h(0, 1)
         pick(3)
-        ahead = [first_sums(1, 1, t0) for t0 in (0, 2)]
+        hidden_half(1, 1, 0, first_sums(1, 1, 0))
+        ahead = first_sums(1, 1, 2)
         linear = linear_pair(0, 0)
         for s in range(SLICES):
             first = s * WIDTH
@@ -291,8 +294,7 @@ def tile_list_sense_drift_rewrite_kernel(
                 linear_high = linear_pair(s, 2)
             y_low = nonlinear_pair(s, 0)
             if s == 0:
-                hidden_half(1, 1, 0, ahead[0])
-                hidden_half(1, 1, 2, ahead[1])
+                hidden_half(1, 1, 2, ahead)
                 linear_high = linear_pair(s, 2)
             y_high = nonlinear_pair(s, 2)
             drift = drift_tile(WIDTH)
@@ -324,5 +326,8 @@ def tile_list_sense_drift_rewrite_kernel(
                 linear = linear_pair(s + 1, 0)
         put_back(3, (last - 1) * WIDTH, wide[:, 1, :])
 
-        for n in range(ROW_TILES):
+        for n in range(ROW_TILES - 1):
             nc.sync.dma_start(out[n * P : (n + 1) * P, :], state[n][:])
+        n = ROW_TILES - 1
+        nc.sync.dma_start(out[n * P :, : T // 2], state[n][:, : T // 2])
+        nc.scalar.dma_start(out[n * P :, T // 2 :], state[n][:, T // 2 :])

@@ -72,6 +72,11 @@ def tile_list_sense_drift_rewrite_kernel(
             )
             return raw
 
+        def load_gains(b):
+            tile = keep.tile([P, PACK], F32, name="gains%d" % b)
+            nc.sync.dma_start(tile[:], gain[b * PASS : (b + 1) * PASS].rearrange("(p t) -> p t", t=PACK))
+            return tile
+
         tab_plane = zeroed_plane([P, T], "tab_plane")
         w3_plane = zeroed_plane([P, PASSES, N], "w3_plane")
         w2_plane = zeroed_plane([P, PASSES, N], "w2_plane")
@@ -81,11 +86,10 @@ def tile_list_sense_drift_rewrite_kernel(
         nc.sync.dma_start(offsets[:], offs)
         load_table_scales((0, 1))
         w1_raw = {(0, 0): load_w1(0, 0)}
-        gains = keep.tile([P, PASSES, PACK], F32, name="gains")
-        nc.sync.dma_start(gains[:], gain.rearrange("(b p t) -> p b t", b=PASSES, t=PACK))
         load_table_scales((2, 3))
         w1_raw[0, 1] = load_w1(0, 1)
         tab.append(load_table_pass(1))
+        gains = [load_gains(0)]
         w1_raw[1, 0] = load_w1(1, 0)
         state = [keep.tile([P, T], F32, name="state%d" % n) for n in range(ROW_TILES)]
         nc.sync.dma_start(state[0][:], gT[0:P, :])
@@ -104,6 +108,7 @@ def tile_list_sense_drift_rewrite_kernel(
             return codes
 
         nc.sync.dma_start(state[1][:], gT[P : 2 * P, :])
+        gains.append(load_gains(1))
         load_weight_scales((0, 1))
         nc.sync.dma_start(state[2][:], gT[2 * P : 3 * P, :])
         load_weight_scales((2, 3))
@@ -195,7 +200,7 @@ def tile_list_sense_drift_rewrite_kernel(
             nc.scalar.activation(act[:], pre[:], TANH)
             for i in range(2):
                 nc.scalar.activation(
-                    h_rows[s, b][:, t0 + i, :], act[:, i, :], COPY, scale=gains[:, b, t0 + i : t0 + i + 1]
+                    h_rows[s, b][:, t0 + i, :], act[:, i, :], COPY, scale=gains[b][:, t0 + i : t0 + i + 1]
                 )
             if t0 == 2:
                 grouped[s, b] = ring.tile(
@@ -219,7 +224,7 @@ def tile_list_sense_drift_rewrite_kernel(
                 )
                 act = ring.tile([P, 2 * WIDTH], F32, name="act", tag="from_scalar", bufs=16, align_bytes=64)
                 nc.scalar.activation(act[:], pre[:, 0, :], TANH)
-                nc.scalar.activation(rows[:, t, :], act[:], COPY, scale=gains[:, 0, t : t + 1])
+                nc.scalar.activation(rows[:, t, :], act[:], COPY, scale=gains[0][:, t : t + 1])
             for s in range(2):
                 grouped[s, 0] = ring.tile(
                     [P, WIDTH * PACK], BF16, name="grouped", tag="from_scalar", bufs=16, align_bytes=64

@@ -37,8 +37,17 @@ def tile_list_sense_drift_rewrite_kernel(
     nc = tc.nc
     with ExitStack() as ctx:
         keep = ctx.enter_context(tc.tile_pool(name="keep", bufs=1))
-        ring = ctx.enter_context(tc.tile_pool(name="ring", bufs=4))
+        ring = ctx.enter_context(tc.tile_pool(name="ring", bufs=1))
         psum = ctx.enter_context(tc.psum_pool(name="psum", bufs=8))
+
+        def from_vector(shape, dtype, name):
+            return ring.tile(shape, dtype, name=name, tag="from_vector", bufs=20, align_bytes=64)
+
+        def from_scalar(shape, dtype, name):
+            return ring.tile(shape, dtype, name=name, tag="from_scalar", bufs=18, align_bytes=64)
+
+        def bank(name):
+            return psum.tile([P, 2, WIDTH], F32, name=name, tag="bank")
 
         def zeroed_plane(shape, name):
             plane = keep.tile(shape, U8, name=name, align_bytes=64)
@@ -64,36 +73,13 @@ def tile_list_sense_drift_rewrite_kernel(
                         scales[:, r:16:4, :].rearrange("a q c -> q a c").bitcast(I32),
                     )
 
-        def load_w1(b, a):
-            raw = keep.tile([P, PACK, PASS], F32, name="w1_raw%d%d" % (b, a))
-            nc.sync.dma_start(
-                raw[:],
-                w1[a * PASS : (a + 1) * PASS, b * PASS : (b + 1) * PASS].rearrange("(p j) c -> p j c", j=PACK),
-            )
+        def load_w1_block(b):
+            raw = keep.tile([P, PACK, PASS], F32, name="w1_late%d" % b)
+            nc.sync.dma_start(raw[:], w1[PASS:, b * PASS : (b + 1) * PASS].rearrange("(p j) c -> p j c", j=PACK))
             return raw
 
-        def load_gains(b):
-            tile = keep.tile([P, PACK], F32, name="gains%d" % b)
-            nc.sync.dma_start(tile[:], gain[b * PASS : (b + 1) * PASS].rearrange("(p t) -> p t", t=PACK))
-            return tile
-
-        tab_plane = zeroed_plane([P, T], "tab_plane")
-        w3_plane = zeroed_plane([P, PASSES, N], "w3_plane")
-        w2_plane = zeroed_plane([P, PASSES, N], "w2_plane")
-
-        tab = [load_table_pass(0)]
-        offsets = keep.tile([P, S // PER_COLUMN], U16, name="offsets")
-        nc.sync.dma_start(offsets[:], offs)
-        load_table_scales((0, 1))
-        w1_raw = {(0, 0): load_w1(0, 0)}
-        load_table_scales((2, 3))
-        w1_raw[0, 1] = load_w1(0, 1)
-        tab.append(load_table_pass(1))
-        gains = [load_gains(0)]
-        w1_raw[1, 0] = load_w1(1, 0)
-        state = [keep.tile([P, T], F32, name="state%d" % n) for n in range(ROW_TILES)]
-        nc.sync.dma_start(state[0][:], gT[0:P, :])
-        w1_raw[1, 1] = load_w1(1, 1)
+        def load_state(n):
+            nc.sync.dma_start(state[n][:], gT[n * P : (n + 1) * P, :])
 
         def load_w3_half(half):
             codes = keep.tile([P, PASSES, N // 2], U32, name="w3_codes%d" % half, align_bytes=64)
@@ -107,162 +93,140 @@ def tile_list_sense_drift_rewrite_kernel(
             nc.sync.dma_start(codes[:].bitcast(I32), words.bitcast(I32))
             return codes
 
-        nc.sync.dma_start(state[1][:], gT[P : 2 * P, :])
-        gains.append(load_gains(1))
+        tab_plane = zeroed_plane([P, T], "tab_plane")
+        w3_plane = zeroed_plane([P, PASSES, N], "w3_plane")
+        w2_plane = zeroed_plane([P, PASSES, N], "w2_plane")
+        state = [keep.tile([P, T], F32, name="state%d" % n) for n in range(ROW_TILES)]
+
+        tab = [load_table_pass(0)]
+        offsets = keep.tile([P, S // PER_COLUMN], U16, name="offsets")
+        nc.sync.dma_start(offsets[:], offs)
+        load_table_scales((0, 1))
+        w1_early = keep.tile([P, PACK, H], F32, name="w1_early")
+        early_rows = w1[:PASS, :].rearrange("(p j) c -> p j c", j=PACK)
+        nc.sync.dma_start(w1_early[:, :2, :], early_rows[:, :2, :])
+        load_table_scales((2, 3))
+        nc.sync.dma_start(w1_early[:, 2:, :], early_rows[:, 2:, :])
+        tab.append(load_table_pass(1))
+        w1_raw = {(b, 0): w1_early[:, :, b * PASS : (b + 1) * PASS] for b in range(PASSES)}
+        w1_raw[0, 1] = load_w1_block(0)[:]
+        gains = keep.tile([P, PASSES, PACK], F32, name="gains")
+        nc.sync.dma_start(gains[:], gain.rearrange("(b p t) -> p b t", b=PASSES, t=PACK))
+        w1_raw[1, 1] = load_w1_block(1)[:]
+        load_state(0)
         load_weight_scales((0, 1))
-        nc.sync.dma_start(state[2][:], gT[2 * P : 3 * P, :])
+        load_state(2)
         load_weight_scales((2, 3))
-        nc.sync.dma_start(state[3][:], gT[3 * P :, :])
         w3_codes = [load_w3_half(0)]
+        load_state(3)
         w2_codes = [load_w2_half(0)]
         w3_codes.append(load_w3_half(1))
         w2_codes.append(load_w2_half(1))
+        load_state(1)
 
         def listed(first, count):
             return offsets[:, first // PER_COLUMN : (first + count) // PER_COLUMN]
 
-        w1_codes, w1_plane = {}, {}
-
-        def quantise_w1(b, a, engines):
-            grouped = keep.tile([P, PACK * PASS], BF16, name="w1_grouped%d%d" % (b, a), align_bytes=64)
-            dst = grouped[:].rearrange("p (t m j) -> p m j t", t=PACK, j=PACK)
-            src = w1_raw[b, a][:].rearrange("p j (m t) -> p m j t", t=PACK)
-            for u, cast in enumerate(engines):
-                cast(dst[:, :, :, 2 * u : 2 * u + 2], src[:, :, :, 2 * u : 2 * u + 2])
-            w1_codes[b, a] = ring.tile([P, PASS], U32, name="w1_codes", tag="from_vector", bufs=17, align_bytes=64)
-            w1_plane[b, a] = keep.tile([P, PASS], U8, name="w1_plane%d%d" % (b, a), align_bytes=64)
-            for u in range(2):
-                half = slice(2 * u * P, 2 * (u + 1) * P)
-                nc.vector.quantize_mx(
-                    w1_codes[b, a][:, half].bitcast(E4M3),
-                    w1_plane[b, a][:, half],
-                    grouped[:, PACK * half.start : PACK * half.stop],
-                )
-
-        v_codes = [keep.tile([P, S], U32, name="v_codes%d" % a, align_bytes=64) for a in range(PASSES)]
-        nc.vector.tensor_copy(v_codes[0][:], tab[0][:].indirect(offsets[:]))
-        v_plane = ring.tile([P, S], U8, name="v_plane", tag="from_vector", bufs=17, align_bytes=64)
-        nc.vector.tensor_copy(v_plane[:], tab_plane[:].indirect(offsets[:]))
-        quantise_w1(0, 0, [nc.scalar.copy, nc.scalar.copy])
-        quantise_w1(0, 1, [nc.vector.tensor_copy, nc.scalar.copy])
-        nc.vector.tensor_copy(v_codes[1][:, : S // 2], tab[1][:].indirect(listed(0, S // 2)))
-        nc.vector.tensor_copy(v_codes[1][:, S // 2 :], tab[1][:].indirect(listed(S // 2, S // 2)))
-        quantise_w1(1, 0, [nc.vector.tensor_copy, nc.vector.tensor_copy])
-
-        picked = []
-
-        def pick(n):
-            tile = ring.tile([P, S], F32, name="picked", tag="from_vector", bufs=17, align_bytes=64)
-            nc.vector.tensor_copy(tile[:], state[n][:].indirect(offsets[:]))
-            picked.append(tile)
-
-        pick(0)
-        quantise_w1(1, 1, [nc.vector.tensor_copy, nc.vector.tensor_copy])
-        pick(1)
-        pick(2)
-
         def columns(s):
             return slice(s * WIDTH, (s + 1) * WIDTH)
 
-        def times_table(acc, codes, planes, first_column, cols):
-            order = [(a, i) for a in range(PASSES) for i in range(acc.shape[1])]
+        w1_grouped, w1_codes, w1_plane = {}, {}, {}
+
+        def cast_w1(b, a, u, tile, cast):
+            grouped = tile([P, 2 * PASS], BF16, "w1_grouped")
+            src = w1_raw[b, a].rearrange("p j (m t) -> p m j t", t=PACK)
+            cast(grouped[:].rearrange("p (t m j) -> p m j t", t=2, j=PACK), src[:, :, :, 2 * u : 2 * u + 2])
+            w1_grouped[b, a, u] = grouped
+
+        def vector_cast(b, a, u):
+            cast_w1(b, a, u, from_vector, nc.vector.tensor_copy)
+
+        def scalar_cast(b, a, u):
+            cast_w1(b, a, u, from_scalar, nc.scalar.copy)
+
+        def quantise_w1(b, a, u):
+            w1_codes[b, a, u] = from_vector([P, 2 * P], U32, "w1_codes")
+            w1_plane[b, a, u] = keep.tile([P, 2 * P], U8, name="w1_plane%d%d%d" % (b, a, u), align_bytes=64)
+            nc.vector.quantize_mx(w1_codes[b, a, u][:].bitcast(E4M3), w1_plane[b, a, u][:], w1_grouped[b, a, u][:])
+
+        def gathered(window, dtype, name):
+            tile = from_vector([P, S], dtype, name)
+            nc.vector.tensor_copy(tile[:], window[:].indirect(offsets[:]))
+            return tile
+
+        v_codes = [gathered(tab[0], U32, "v_codes")]
+        v_plane = gathered(tab_plane, U8, "v_plane")
+        for u in range(2):
+            vector_cast(0, 0, u)
+            scalar_cast(1, 0, u)
+        for u in range(2):
+            quantise_w1(0, 0, u)
+        v_codes.append(gathered(tab[1], U32, "v_codes"))
+        vector_cast(0, 1, 0)
+        scalar_cast(0, 1, 1)
+        quantise_w1(1, 0, 0)
+        for u in range(2):
+            quantise_w1(0, 1, u)
+        quantise_w1(1, 0, 1)
+        for u in range(2):
+            vector_cast(1, 1, u)
+        for u in range(2):
+            quantise_w1(1, 1, u)
+
+        def times_table(acc, operands, passes=range(PASSES)):
+            order = [(a, i) for a in passes for i in range(len(operands))]
             for a, i in order:
-                m = slice(first_column + i * P, first_column + (i + 1) * P)
+                codes, planes, cols = operands[i]
                 nc.tensor.matmul_mx(
                     acc[:, i, :],
-                    lhsT=codes[a][:, m].bitcast(E4M3),
-                    lhsT_scale=planes[a][:, m],
+                    lhsT=codes[a].bitcast(E4M3),
+                    lhsT_scale=planes[a],
                     rhs=v_codes[a][:, cols].bitcast(E4M3),
                     rhs_scale=v_plane[TAB_PLANE_ROW + 4 * a :, cols],
                     start=(a, i) == order[0],
                     stop=(a, i) == order[-1],
                 )
 
-        grouped, h_codes, h_plane = {}, {}, {}
+        pre, act, h_rows, h_grouped, h_codes, h_plane = {}, {}, {}, {}, {}, {}
+        d_acc, linear, y_acc, drift, picked = {}, {}, {}, {}, {}
 
-        h_rows = {}
-
-        def first_sums(s, b, t0):
-            pre = psum.tile([P, 2, WIDTH], F32, name="pre", tag="bank")
-            times_table(
-                pre,
-                [w1_codes[b, a] for a in range(PASSES)],
-                [w1_plane[b, a] for a in range(PASSES)],
-                t0 * P,
-                columns(s),
-            )
-            return pre
-
-        def hidden_half(s, b, t0, pre):
-            if t0 == 0:
-                h_rows[s, b] = ring.tile([P, PACK, WIDTH], BF16, name="h_rows", bufs=3)
-            act = ring.tile([P, 2, WIDTH], F32, name="act", tag="from_scalar", bufs=16, align_bytes=64)
-            nc.scalar.activation(act[:], pre[:], TANH)
-            for i in range(2):
-                nc.scalar.activation(
-                    h_rows[s, b][:, t0 + i, :], act[:, i, :], COPY, scale=gains[b][:, t0 + i : t0 + i + 1]
-                )
-            if t0 == 2:
-                grouped[s, b] = ring.tile(
-                    [P, WIDTH * PACK], BF16, name="grouped", tag="from_scalar", bufs=16, align_bytes=64
-                )
-                nc.scalar.copy(
-                    grouped[s, b][:].rearrange("p (c i t) -> p c t i", i=4, t=PACK),
-                    h_rows[s, b][:].rearrange("p t (c i) -> p c t i", i=4),
-                )
-
-        def first_block_wide():
-            rows = keep.tile([P, PACK, 2 * WIDTH], BF16, name="rows_wide")
-            for t in range(PACK):
-                pre = psum.tile([P, 1, 2 * WIDTH], F32, name="pre", tag="bank")
+        def first_sums(s, b):
+            for u in range(2):
+                pre[s, b, u] = bank("pre")
                 times_table(
-                    pre,
-                    [w1_codes[0, a] for a in range(PASSES)],
-                    [w1_plane[0, a] for a in range(PASSES)],
-                    t * P,
-                    slice(0, 2 * WIDTH),
-                )
-                act = ring.tile([P, 2 * WIDTH], F32, name="act", tag="from_scalar", bufs=16, align_bytes=64)
-                nc.scalar.activation(act[:], pre[:, 0, :], TANH)
-                nc.scalar.activation(rows[:, t, :], act[:], COPY, scale=gains[0][:, t : t + 1])
-            for s in range(2):
-                grouped[s, 0] = ring.tile(
-                    [P, WIDTH * PACK], BF16, name="grouped", tag="from_scalar", bufs=16, align_bytes=64
-                )
-                nc.scalar.copy(
-                    grouped[s, 0][:].rearrange("p (c i t) -> p c t i", i=4, t=PACK),
-                    rows[:, :, columns(s)].rearrange("p t (c i) -> p c t i", i=4),
+                    pre[s, b, u],
+                    [
+                        (
+                            [w1_codes[b, a, u][:, i * P : (i + 1) * P] for a in range(PASSES)],
+                            [w1_plane[b, a, u][:, i * P : (i + 1) * P] for a in range(PASSES)],
+                            columns(s),
+                        )
+                        for i in range(2)
+                    ],
+                    range(PASSES) if s == 0 else reversed(range(PASSES)),
                 )
 
-        def hidden(s, b):
-            hidden_half(s, b, 0, first_sums(s, b, 0))
-            hidden_half(s, b, 2, first_sums(s, b, 2))
-
-        def quantise_h(s, b):
-            h_codes[s, b] = ring.tile([P, WIDTH], U32, name="h_codes", tag="from_vector", bufs=17, align_bytes=64)
-            h_plane[s, b] = keep.tile([P, WIDTH], U8, name="h_plane%d_%d" % (s, b), align_bytes=64)
-            nc.vector.quantize_mx(h_codes[s, b][:].bitcast(E4M3), h_plane[s, b][:], grouped[s, b][:])
-
-        def linear_pair(s, n0):
-            d_acc = psum.tile([P, 2, WIDTH], F32, name="d_acc", tag="bank")
+        def linear_sums(s, pair):
+            d_acc[s, pair] = bank("d_acc")
             times_table(
-                d_acc,
-                [w3_codes[n0 // 2][:, a, :] for a in range(PASSES)],
-                [w3_plane[W3_PLANE_ROW:, a, n0 * P : (n0 + 2) * P] for a in range(PASSES)],
-                0,
-                columns(s),
+                d_acc[s, pair],
+                [
+                    (
+                        [w3_codes[pair][:, a, i * P : (i + 1) * P] for a in range(PASSES)],
+                        [w3_plane[W3_PLANE_ROW:, a, (2 * pair + i) * P : (2 * pair + i + 1) * P] for a in range(PASSES)],
+                        columns(s),
+                    )
+                    for i in range(2)
+                ],
             )
-            linear = ring.tile([P, 2, WIDTH], F32, name="linear", tag="from_scalar", bufs=16, align_bytes=64)
-            nc.scalar.copy(linear[:], d_acc[:])
-            return linear
 
-        def nonlinear_pair(s, n0):
-            y_acc = psum.tile([P, 2, WIDTH], F32, name="y_acc", tag="bank")
+        def nonlinear_sums(s, n0):
+            acc = bank("y_acc")
             order = [(b, i, c) for b in range(PASSES) for i in range(2) for c in range(WIDTH // P)]
             for b, i, c in order:
                 n = n0 + i
                 nc.tensor.matmul_mx(
-                    y_acc[:, i, c * P : (c + 1) * P],
+                    acc[:, i, c * P : (c + 1) * P],
                     lhsT=w2_codes[n0 // 2][:, b, 2 * i * P : 2 * (i + 1) * P].bitcast(E2M1),
                     lhsT_scale=w2_plane[:, b, n * P : (n + 1) * P],
                     rhs=h_codes[s, b][:, c * P : (c + 1) * P].bitcast(E4M3),
@@ -270,66 +234,131 @@ def tile_list_sense_drift_rewrite_kernel(
                     start=(b, i, c) == order[0],
                     stop=(b, i, c) == order[-1],
                 )
-            return y_acc
+            y_acc[s, n0 // 2] = acc
 
-        def drift_tile(width):
-            return ring.tile([P, 2, width], F32, name="drift", tag="from_vector", bufs=17, align_bytes=64)
+        def squash(s, b, u):
+            act[s, b, u] = from_scalar([P, 2, WIDTH], F32, "act")
+            nc.scalar.activation(act[s, b, u][:], pre[s, b, u][:], TANH)
 
-        def put_back(n, first, drift):
-            count = drift.shape[1]
-            nc.vector.tensor_tensor(
-                state[n][:].indirect(listed(first, count)), picked[n][:, first : first + count], drift, ADD
+        def apply_gains(s, b):
+            h_rows[s, b] = from_scalar([P, PACK, WIDTH], BF16, "h_rows")
+            for t in range(PACK):
+                nc.scalar.activation(
+                    h_rows[s, b][:, t, :], act[s, b, t // 2][:, t % 2, :], COPY, scale=gains[:, b, t : t + 1]
+                )
+
+        def interleave(s, b):
+            h_grouped[s, b] = from_scalar([P, WIDTH * PACK], BF16, "h_grouped")
+            nc.scalar.copy(
+                h_grouped[s, b][:].rearrange("p (c i t) -> p c t i", i=4, t=PACK),
+                h_rows[s, b][:].rearrange("p t (c i) -> p c t i", i=4),
             )
 
+        def copy_linear(s, pair):
+            linear[s, pair] = from_scalar([P, 2, WIDTH], F32, "linear")
+            nc.scalar.copy(linear[s, pair][:], d_acc[s, pair][:])
+
+        def pick(n):
+            picked[n] = gathered(state[n], F32, "picked")
+
+        def quantise_h(s, b):
+            h_codes[s, b] = from_vector([P, WIDTH], U32, "h_codes")
+            h_plane[s, b] = keep.tile([P, WIDTH], U8, name="h_plane%d_%d" % (s, b), align_bytes=64)
+            nc.vector.quantize_mx(h_codes[s, b][:].bitcast(E4M3), h_plane[s, b][:], h_grouped[s, b][:])
+
+        def multiply(s, n):
+            drift[s, n] = from_vector([P, WIDTH], F32, "drift")[:]
+            nc.vector.tensor_tensor(drift[s, n], y_acc[s, 0][:, n, :], linear[s, 0][:, n, :], MULT)
+
+        def multiply_high(s, into):
+            nc.vector.tensor_tensor(into, y_acc[s, 1][:], linear[s, 1][:], MULT)
+            drift[s, 2], drift[s, 3] = into[:, 0, :], into[:, 1, :]
+
+        def scatter(n, first, values):
+            count = values.shape[1]
+            nc.vector.tensor_tensor(
+                state[n][:].indirect(listed(first, count)), picked[n][:, first : first + count], values, ADD
+            )
+
+        def put_back(s, n):
+            scatter(n, s * WIDTH, drift[s, n])
+
         last = SLICES - 1
-        first_block_wide()
+
+        first_sums(0, 0)
+        first_sums(0, 1)
+        first_sums(1, 0)
+        first_sums(1, 1)
+        squash(0, 0, 0)
+        squash(0, 0, 1)
+        apply_gains(0, 0)
+        squash(0, 1, 0)
+        interleave(0, 0)
+        squash(0, 1, 1)
+        apply_gains(0, 1)
+        squash(1, 0, 0)
+        interleave(0, 1)
+        pick(0)
+        pick(2)
         quantise_h(0, 0)
-        hidden_half(2, 0, 0, first_sums(2, 0, 0))
-        hidden(0, 1)
+        picked[3] = from_vector([P, S], F32, "picked")
+        nc.vector.tensor_copy(picked[3][:, : S // 2], state[3][:].indirect(listed(0, S // 2)))
         quantise_h(0, 1)
-        pick(3)
-        hidden_half(1, 1, 0, first_sums(1, 1, 0))
-        ahead = first_sums(1, 1, 2)
-        linear = linear_pair(0, 0)
+        nc.vector.tensor_copy(picked[3][:, S // 2 :], state[3][:].indirect(listed(S // 2, S // 2)))
+        linear_sums(0, 0)
+        nonlinear_sums(0, 0)
+        linear_sums(1, 0)
+        linear_sums(0, 1)
+        nonlinear_sums(0, 2)
+        squash(1, 0, 1)
+        copy_linear(0, 0)
+        apply_gains(1, 0)
+        squash(1, 1, 0)
+
         for s in range(SLICES):
-            first = s * WIDTH
-            if 0 < s < last:
-                hidden(s + 1, 1)
-            if s > 0:
-                linear_high = linear_pair(s, 2)
-            y_low = nonlinear_pair(s, 0)
+            ahead = s + 1
+            if s < last:
+                interleave(ahead, 0)
+                squash(ahead, 1, 1)
+                apply_gains(ahead, 1)
+                copy_linear(ahead, 0)
+                interleave(ahead, 1)
+                copy_linear(s, 1)
+            if s < last - 1:
+                first_sums(ahead + 1, 0)
+                first_sums(ahead + 1, 1)
+                linear_sums(ahead + 1, 0)
+                linear_sums(ahead, 1)
+                squash(ahead + 1, 0, 0)
+                squash(ahead + 1, 0, 1)
+                apply_gains(ahead + 1, 0)
+                squash(ahead + 1, 1, 0)
+            if s == last - 1:
+                linear_sums(last, 1)
+                copy_linear(last, 1)
+
+            multiply(s, 0)
+            multiply(s, 1)
+            put_back(s, 0)
             if s == 0:
-                hidden_half(1, 1, 2, ahead)
-                linear_high = linear_pair(s, 2)
-            y_high = nonlinear_pair(s, 2)
-            drift = drift_tile(WIDTH)
-            nc.vector.tensor_tensor(drift[:], y_low[:], linear[:], MULT)
+                pick(1)
+            if s == last:
+                multiply_high(s, wide[:, :, WIDTH:])
+            put_back(s, 1)
             if s < last:
-                quantise_h(s + 1, 0)
-            else:
-                nc.vector.tensor_tensor(wide[:, :, WIDTH:], y_high[:], linear_high[:], MULT)
-            put_back(0, first, drift[:, 0, :])
-            put_back(1, first, drift[:, 1, :])
+                quantise_h(ahead, 0)
+                if s == last - 1:
+                    wide = from_vector([P, 2, 2 * WIDTH], F32, "drift")
+                    multiply_high(s, wide[:, :, :WIDTH])
+                else:
+                    multiply_high(s, from_vector([P, 2, WIDTH], F32, "drift")[:])
+                quantise_h(ahead, 1)
+                nonlinear_sums(ahead, 0)
+                nonlinear_sums(ahead, 2)
+            put_back(s, 2)
             if s < last - 1:
-                drift = drift_tile(WIDTH)
-                high = drift[:]
-            elif s < last:
-                wide = drift_tile(2 * WIDTH)
-                high = wide[:, :, :WIDTH]
-            else:
-                high = wide[:, :, WIDTH:]
-            if s < last:
-                nc.vector.tensor_tensor(high, y_high[:], linear_high[:], MULT)
-                quantise_h(s + 1, 1)
-            put_back(2, first, high[:, 0, :])
-            if s < last - 1:
-                put_back(3, first, high[:, 1, :])
-                if s > 0:
-                    hidden_half(s + 2, 0, 0, first_sums(s + 2, 0, 0))
-                hidden_half(s + 2, 0, 2, first_sums(s + 2, 0, 2))
-            if s < last:
-                linear = linear_pair(s + 1, 0)
-        put_back(3, (last - 1) * WIDTH, wide[:, 1, :])
+                put_back(s, 3)
+        scatter(3, (last - 1) * WIDTH, wide[:, 1, :])
 
         for n in range(ROW_TILES - 1):
             nc.sync.dma_start(out[n * P : (n + 1) * P, :], state[n][:])

@@ -22,13 +22,13 @@ P = 128
 PACK = 4
 PASS = P * PACK
 PASSES = K // PASS
-BANK = 512
 ROW_TILES = N // P
 PER_COLUMN = 16
 TAB_PLANE_ROW = 8
 W3_PLANE_ROW = 12
 WIDTH = 256
 SLICES = S // WIDTH
+BLOCK_BYTES = PACK * PASS * 4
 
 
 def tile_list_sense_drift_rewrite_kernel(
@@ -37,17 +37,28 @@ def tile_list_sense_drift_rewrite_kernel(
     nc = tc.nc
     with ExitStack() as ctx:
         keep = ctx.enter_context(tc.tile_pool(name="keep", bufs=1))
+        raw = ctx.enter_context(tc.tile_pool(name="raw", bufs=1))
         ring = ctx.enter_context(tc.tile_pool(name="ring", bufs=1))
         psum = ctx.enter_context(tc.psum_pool(name="psum", bufs=8))
 
         def from_vector(shape, dtype, name):
-            return ring.tile(shape, dtype, name=name, tag="from_vector", bufs=20, align_bytes=64)
+            return ring.tile(shape, dtype, name=name, tag="from_vector", bufs=19, align_bytes=64)
 
         def from_scalar(shape, dtype, name):
-            return ring.tile(shape, dtype, name=name, tag="from_scalar", bufs=18, align_bytes=64)
+            return ring.tile(shape, dtype, name=name, tag="from_scalar", bufs=12, align_bytes=64)
 
-        def bank(name):
-            return psum.tile([P, 2, WIDTH], F32, name=name, tag="bank")
+        def from_gpsimd(shape, dtype, name):
+            return raw.tile(shape, dtype, name=name, tag="from_gpsimd", bufs=12, offset=0)
+
+        def handed(tag):
+            return lambda shape, dtype, name: ring.tile(shape, dtype, name=name, tag=tag, bufs=1, align_bytes=64)
+
+        def handed_late(tag):
+            place = 3 * BLOCK_BYTES + 2048 * ("rows31", "h31", "d2", "y2").index(tag)
+            return lambda shape, dtype, name: raw.tile(shape, dtype, name=name, tag=tag, bufs=1, align_bytes=64, offset=place)
+
+        def bank(name, parts):
+            return psum.tile([P, parts, 512 // parts], F32, name=name, tag="bank")
 
         def zeroed_plane(shape, name):
             plane = keep.tile(shape, U8, name=name, align_bytes=64)
@@ -74,9 +85,9 @@ def tile_list_sense_drift_rewrite_kernel(
                     )
 
         def load_w1_block(b):
-            raw = keep.tile([P, PACK, PASS], F32, name="w1_late%d" % b)
-            nc.sync.dma_start(raw[:], w1[PASS:, b * PASS : (b + 1) * PASS].rearrange("(p j) c -> p j c", j=PACK))
-            return raw
+            block = raw.tile([P, PACK, PASS], F32, name="w1_late%d" % b, offset=(2 + b) * BLOCK_BYTES)
+            nc.sync.dma_start(block[:], w1[PASS:, b * PASS : (b + 1) * PASS].rearrange("(p j) c -> p j c", j=PACK))
+            return block
 
         def load_state(n):
             nc.sync.dma_start(state[n][:], gT[n * P : (n + 1) * P, :])
@@ -102,7 +113,7 @@ def tile_list_sense_drift_rewrite_kernel(
         offsets = keep.tile([P, S // PER_COLUMN], U16, name="offsets")
         nc.sync.dma_start(offsets[:], offs)
         load_table_scales((0, 1))
-        w1_early = keep.tile([P, PACK, H], F32, name="w1_early")
+        w1_early = raw.tile([P, PACK, H], F32, name="w1_early", offset=0)
         early_rows = w1[:PASS, :].rearrange("(p j) c -> p j c", j=PACK)
         nc.sync.dma_start(w1_early[:, :2, :], early_rows[:, :2, :])
         load_table_scales((2, 3))
@@ -113,22 +124,22 @@ def tile_list_sense_drift_rewrite_kernel(
         gains = keep.tile([P, PASSES, PACK], F32, name="gains")
         nc.sync.dma_start(gains[:], gain.rearrange("(b p t) -> p b t", b=PASSES, t=PACK))
         w1_raw[1, 1] = load_w1_block(1)[:]
-        load_state(0)
-        load_weight_scales((0, 1))
         load_state(2)
+        load_weight_scales((0, 1))
+        load_state(3)
         load_weight_scales((2, 3))
         w3_codes = [load_w3_half(0)]
-        load_state(3)
         w2_codes = [load_w2_half(0)]
+        load_state(1)
+        load_state(0)
         w3_codes.append(load_w3_half(1))
         w2_codes.append(load_w2_half(1))
-        load_state(1)
 
         def listed(first, count):
             return offsets[:, first // PER_COLUMN : (first + count) // PER_COLUMN]
 
-        def columns(s):
-            return slice(s * WIDTH, (s + 1) * WIDTH)
+        def columns(s, first=0, count=WIDTH):
+            return slice(s * WIDTH + first, s * WIDTH + first + count)
 
         w1_grouped, w1_codes, w1_plane = {}, {}, {}
 
@@ -138,8 +149,8 @@ def tile_list_sense_drift_rewrite_kernel(
             cast(grouped[:].rearrange("p (t m j) -> p m j t", t=2, j=PACK), src[:, :, :, 2 * u : 2 * u + 2])
             w1_grouped[b, a, u] = grouped
 
-        def vector_cast(b, a, u):
-            cast_w1(b, a, u, from_vector, nc.vector.tensor_copy)
+        def vector_cast(b, a, u, tile=from_vector):
+            cast_w1(b, a, u, tile, nc.vector.tensor_copy)
 
         def scalar_cast(b, a, u):
             cast_w1(b, a, u, from_scalar, nc.scalar.copy)
@@ -168,12 +179,12 @@ def tile_list_sense_drift_rewrite_kernel(
         for u in range(2):
             quantise_w1(0, 1, u)
         quantise_w1(1, 0, 1)
-        for u in range(2):
-            vector_cast(1, 1, u)
+        vector_cast(1, 1, 0)
+        vector_cast(1, 1, 1, handed("after_w1"))
         for u in range(2):
             quantise_w1(1, 1, u)
 
-        def times_table(acc, operands, passes=range(PASSES)):
+        def times_table(acc, operands, passes):
             order = [(a, i) for a in passes for i in range(len(operands))]
             for a, i in order:
                 codes, planes, cols = operands[i]
@@ -188,26 +199,31 @@ def tile_list_sense_drift_rewrite_kernel(
                 )
 
         pre, act, h_rows, h_grouped, h_codes, h_plane = {}, {}, {}, {}, {}, {}
-        d_acc, linear, y_acc, drift, picked = {}, {}, {}, {}, {}
+        d_acc, y_acc, linear, nonlinear, drift, picked, fresh = {}, {}, {}, {}, {}, {}, {}
 
-        def first_sums(s, b):
+        def w1_operand(b, t, cols):
+            u, i = divmod(t, 2)
+            return (
+                [w1_codes[b, a, u][:, i * P : (i + 1) * P] for a in range(PASSES)],
+                [w1_plane[b, a, u][:, i * P : (i + 1) * P] for a in range(PASSES)],
+                cols,
+            )
+
+        def passes_of(s):
+            return range(PASSES)
+
+        def sums_by_rows(s, b):
             for u in range(2):
-                pre[s, b, u] = bank("pre")
-                times_table(
-                    pre[s, b, u],
-                    [
-                        (
-                            [w1_codes[b, a, u][:, i * P : (i + 1) * P] for a in range(PASSES)],
-                            [w1_plane[b, a, u][:, i * P : (i + 1) * P] for a in range(PASSES)],
-                            columns(s),
-                        )
-                        for i in range(2)
-                    ],
-                    range(PASSES) if s == 0 else reversed(range(PASSES)),
-                )
+                pre[s, b, u] = bank("pre", 2)
+                times_table(pre[s, b, u], [w1_operand(b, 2 * u + i, columns(s)) for i in range(2)], passes_of(s))
+
+        def sums_by_columns(s, b):
+            for c in range(2):
+                pre[s, b, c] = bank("pre", PACK)
+                times_table(pre[s, b, c], [w1_operand(b, t, columns(s, c * P, P)) for t in range(PACK)], passes_of(s))
 
         def linear_sums(s, pair):
-            d_acc[s, pair] = bank("d_acc")
+            d_acc[s, pair] = bank("d_acc", 2)
             times_table(
                 d_acc[s, pair],
                 [
@@ -218,147 +234,212 @@ def tile_list_sense_drift_rewrite_kernel(
                     )
                     for i in range(2)
                 ],
+                range(PASSES),
             )
 
-        def nonlinear_sums(s, n0):
-            acc = bank("y_acc")
-            order = [(b, i, c) for b in range(PASSES) for i in range(2) for c in range(WIDTH // P)]
-            for b, i, c in order:
-                n = n0 + i
+        def nonlinear_sums(s, rows):
+            acc = bank("y_acc", 2)
+            order = [(b, n) for b in range(PASSES) for n in rows]
+            for b, n in order:
                 nc.tensor.matmul_mx(
-                    acc[:, i, c * P : (c + 1) * P],
-                    lhsT=w2_codes[n0 // 2][:, b, 2 * i * P : 2 * (i + 1) * P].bitcast(E2M1),
+                    acc[:, n - rows[0], :],
+                    lhsT=w2_codes[n // 2][:, b, 2 * (n % 2) * P : 2 * (n % 2 + 1) * P].bitcast(E2M1),
                     lhsT_scale=w2_plane[:, b, n * P : (n + 1) * P],
-                    rhs=h_codes[s, b][:, c * P : (c + 1) * P].bitcast(E4M3),
-                    rhs_scale=h_plane[s, b][:, c * P : (c + 1) * P],
-                    start=(b, i, c) == order[0],
-                    stop=(b, i, c) == order[-1],
+                    rhs=h_codes[s, b].bitcast(E4M3),
+                    rhs_scale=h_plane[s, b][:],
+                    start=(b, n) == order[0],
+                    stop=(b, n) == order[-1],
                 )
-            y_acc[s, n0 // 2] = acc
+            y_acc[s, rows] = acc
 
-        def squash(s, b, u):
-            act[s, b, u] = from_scalar([P, 2, WIDTH], F32, "act")
-            nc.scalar.activation(act[s, b, u][:], pre[s, b, u][:], TANH)
+        def squash(s, b):
+            for u in range(2):
+                act[s, b, u] = from_scalar([P, 2, WIDTH], F32, "act")
+                nc.scalar.activation(act[s, b, u][:], pre[s, b, u][:], TANH)
 
-        def apply_gains(s, b):
-            h_rows[s, b] = from_scalar([P, PACK, WIDTH], BF16, "h_rows")
+        def squash_interleaved(s, b):
+            act[s, b] = from_scalar([P, WIDTH, PACK], F32, "act")
+            for c in range(2):
+                nc.scalar.activation(
+                    act[s, b][:, c * P : (c + 1) * P, :], pre[s, b, c][:].rearrange("p t c -> p c t"), TANH
+                )
+
+        def apply_gains(s, b, tile=from_scalar):
+            h_rows[s, b] = tile([P, PACK, WIDTH], BF16, "h_rows")
             for t in range(PACK):
                 nc.scalar.activation(
                     h_rows[s, b][:, t, :], act[s, b, t // 2][:, t % 2, :], COPY, scale=gains[:, b, t : t + 1]
                 )
 
-        def interleave(s, b):
-            h_grouped[s, b] = from_scalar([P, WIDTH * PACK], BF16, "h_grouped")
+        def interleave(s, b, tile=from_scalar):
+            h_grouped[s, b] = tile([P, WIDTH * PACK], BF16, "h_grouped")
             nc.scalar.copy(
                 h_grouped[s, b][:].rearrange("p (c i t) -> p c t i", i=4, t=PACK),
                 h_rows[s, b][:].rearrange("p t (c i) -> p c t i", i=4),
             )
 
-        def copy_linear(s, pair):
-            linear[s, pair] = from_scalar([P, 2, WIDTH], F32, "linear")
-            nc.scalar.copy(linear[s, pair][:], d_acc[s, pair][:])
+        def copy_linear(s, pair, tile=from_scalar):
+            both = tile([P, 2, WIDTH], F32, "linear")
+            nc.scalar.copy(both[:], d_acc[s, pair][:])
+            linear[s, (2 * pair, 2 * pair + 1)] = both[:]
+            for i in range(2):
+                linear[s, (2 * pair + i,)] = both[:, i : i + 1, :]
+
+        def copy_nonlinear(s, rows, tile=from_scalar):
+            copy = tile([P, len(rows), WIDTH], F32, "nonlinear")
+            nc.scalar.copy(copy[:], y_acc[s, rows][:, : len(rows), :])
+            nonlinear[s, rows] = copy[:]
+
+        def gains_and_round(s, b, tile):
+            h_grouped[s, b] = tile([P, WIDTH * PACK], BF16, "h_grouped")
+            nc.gpsimd.tensor_tensor(
+                h_grouped[s, b][:].rearrange("p (c t) -> p c t", t=PACK),
+                act[s, b][:],
+                gains[:, b : b + 1, :].to_broadcast([P, WIDTH, PACK]),
+                MULT,
+            )
+
+        def multiply(s, rows, tile=from_gpsimd):
+            product = tile([P, len(rows), WIDTH], F32, "drift")
+            nc.gpsimd.tensor_tensor(product[:], nonlinear[s, rows], linear[s, rows], MULT)
+            for i, n in enumerate(rows):
+                drift[s, n] = product[:, i, :]
+
+        def add_state(s, n, tile=from_gpsimd, into=None):
+            if into is None:
+                into = tile([P, WIDTH], F32, "fresh")[:]
+            nc.gpsimd.tensor_tensor(into, drift[s, n], picked[n][:, columns(s)], ADD)
+            fresh[s, n] = into
 
         def pick(n):
             picked[n] = gathered(state[n], F32, "picked")
 
-        def quantise_h(s, b):
-            h_codes[s, b] = from_vector([P, WIDTH], U32, "h_codes")
-            h_plane[s, b] = keep.tile([P, WIDTH], U8, name="h_plane%d_%d" % (s, b), align_bytes=64)
-            nc.vector.quantize_mx(h_codes[s, b][:].bitcast(E4M3), h_plane[s, b][:], h_grouped[s, b][:])
-
-        def multiply(s, n):
-            drift[s, n] = from_vector([P, WIDTH], F32, "drift")[:]
-            nc.vector.tensor_tensor(drift[s, n], y_acc[s, 0][:, n, :], linear[s, 0][:, n, :], MULT)
-
-        def multiply_high(s, into):
-            nc.vector.tensor_tensor(into, y_acc[s, 1][:], linear[s, 1][:], MULT)
-            drift[s, 2], drift[s, 3] = into[:, 0, :], into[:, 1, :]
+        def quantise_h(s, tile=from_vector):
+            codes = tile([P, PASSES * WIDTH], U32, "h_codes")
+            for b in range(PASSES):
+                h_codes[s, b] = codes[:, b * WIDTH : (b + 1) * WIDTH]
+                h_plane[s, b] = keep.tile([P, WIDTH], U8, name="h_plane%d_%d" % (s, b), align_bytes=64)
+                nc.vector.quantize_mx(h_codes[s, b].bitcast(E4M3), h_plane[s, b][:], h_grouped[s, b][:])
 
         def scatter(n, first, values):
-            count = values.shape[1]
-            nc.vector.tensor_tensor(
-                state[n][:].indirect(listed(first, count)), picked[n][:, first : first + count], values, ADD
-            )
+            nc.vector.tensor_copy(state[n][:].indirect(listed(first, values.shape[1])), values)
 
         def put_back(s, n):
-            scatter(n, s * WIDTH, drift[s, n])
+            scatter(n, s * WIDTH, fresh[s, n])
 
-        last = SLICES - 1
+        low, high = (0, 1), (2, 3)
+        in_turn = handed("in_turn")
 
-        first_sums(0, 0)
-        first_sums(0, 1)
-        first_sums(1, 0)
-        first_sums(1, 1)
-        squash(0, 0, 0)
-        squash(0, 0, 1)
+        sums_by_rows(0, 0)
+        sums_by_columns(1, 0)
+        sums_by_rows(2, 0)
+        sums_by_columns(0, 1)
+        sums_by_columns(1, 1)
+        squash(0, 0)
+        squash_interleaved(1, 0)
+        gains_and_round(1, 0, handed("after_w1"))
         apply_gains(0, 0)
-        squash(0, 1, 0)
+        squash_interleaved(0, 1)
+        gains_and_round(0, 1, in_turn)
         interleave(0, 0)
-        squash(0, 1, 1)
-        apply_gains(0, 1)
-        squash(1, 0, 0)
-        interleave(0, 1)
-        pick(0)
+        squash_interleaved(1, 1)
         pick(2)
-        quantise_h(0, 0)
-        picked[3] = from_vector([P, S], F32, "picked")
-        nc.vector.tensor_copy(picked[3][:, : S // 2], state[3][:].indirect(listed(0, S // 2)))
-        quantise_h(0, 1)
-        nc.vector.tensor_copy(picked[3][:, S // 2 :], state[3][:].indirect(listed(S // 2, S // 2)))
+        pick(3)
+        quantise_h(0)
+        gains_and_round(1, 1, in_turn)
+        pick(1)
+        squash(2, 0)
+        apply_gains(2, 0)
         linear_sums(0, 0)
-        nonlinear_sums(0, 0)
         linear_sums(1, 0)
-        linear_sums(0, 1)
-        nonlinear_sums(0, 2)
-        squash(1, 0, 1)
+        sums_by_rows(2, 1)
+        nonlinear_sums(0, low)
         copy_linear(0, 0)
-        apply_gains(1, 0)
-        squash(1, 1, 0)
+        copy_nonlinear(0, low)
+        interleave(2, 0, handed("h20"))
+        picked[0] = from_vector([P, S], F32, "picked")
+        nc.vector.tensor_copy(picked[0][:, :WIDTH], state[0][:].indirect(listed(0, WIDTH)))
+        nc.vector.tensor_copy(picked[0][:, WIDTH:], state[0][:].indirect(listed(WIDTH, S - WIDTH)))
+        quantise_h(1)
+        multiply(0, low)
+        add_state(0, 0)
+        add_state(0, 1, handed("after_w1"))
 
-        for s in range(SLICES):
-            ahead = s + 1
-            if s < last:
-                interleave(ahead, 0)
-                squash(ahead, 1, 1)
-                apply_gains(ahead, 1)
-                copy_linear(ahead, 0)
-                interleave(ahead, 1)
-                copy_linear(s, 1)
-            if s < last - 1:
-                first_sums(ahead + 1, 0)
-                first_sums(ahead + 1, 1)
-                linear_sums(ahead + 1, 0)
-                linear_sums(ahead, 1)
-                squash(ahead + 1, 0, 0)
-                squash(ahead + 1, 0, 1)
-                apply_gains(ahead + 1, 0)
-                squash(ahead + 1, 1, 0)
-            if s == last - 1:
-                linear_sums(last, 1)
-                copy_linear(last, 1)
+        linear_sums(0, 1)
+        nonlinear_sums(0, high)
+        linear_sums(1, 1)
+        nonlinear_sums(1, low)
+        nonlinear_sums(1, high)
+        copy_linear(1, 0)
+        copy_linear(0, 1)
+        copy_nonlinear(0, high)
+        squash(2, 1)
+        apply_gains(2, 1, handed("y1"))
+        copy_linear(1, 1)
+        interleave(2, 1, handed("h21"))
+        copy_nonlinear(1, low, handed("y1"))
+        copy_nonlinear(1, high)
+        multiply(0, high, in_turn)
+        add_state(0, 2)
+        add_state(0, 3)
+        for n in range(ROW_TILES):
+            put_back(0, n)
+        multiply(1, low)
+        add_state(1, 0)
 
-            multiply(s, 0)
-            multiply(s, 1)
-            put_back(s, 0)
-            if s == 0:
-                pick(1)
-            if s == last:
-                multiply_high(s, wide[:, :, WIDTH:])
-            put_back(s, 1)
-            if s < last:
-                quantise_h(ahead, 0)
-                if s == last - 1:
-                    wide = from_vector([P, 2, 2 * WIDTH], F32, "drift")
-                    multiply_high(s, wide[:, :, :WIDTH])
-                else:
-                    multiply_high(s, from_vector([P, 2, WIDTH], F32, "drift")[:])
-                quantise_h(ahead, 1)
-                nonlinear_sums(ahead, 0)
-                nonlinear_sums(ahead, 2)
-            put_back(s, 2)
-            if s < last - 1:
-                put_back(s, 3)
-        scatter(3, (last - 1) * WIDTH, wide[:, 1, :])
+        quantise_h(2, handed("y1"))
+        add_state(1, 1, handed("h20"))
+        multiply(1, high, handed("h21"))
+        add_state(1, 2)
+        add_state(1, 3)
+        for n in range(ROW_TILES):
+            put_back(1, n)
+        sums_by_rows(3, 0)
+        linear_sums(2, 0)
+        sums_by_rows(3, 1)
+        linear_sums(2, 1)
+        nonlinear_sums(2, low)
+        nonlinear_sums(2, high)
+        linear_sums(3, 0)
+        linear_sums(3, 1)
+        squash(3, 0)
+        apply_gains(3, 0, handed_late("y2"))
+        interleave(3, 0, handed("h30"))
+        squash(3, 1)
+        copy_linear(2, 0)
+        copy_nonlinear(2, low)
+        copy_linear(2, 1)
+        copy_nonlinear(2, high, handed_late("y2"))
+        apply_gains(3, 1, handed_late("rows31"))
+        interleave(3, 1, handed_late("h31"))
+        copy_linear(3, 0)
+        copy_linear(3, 1)
+        multiply(2, low)
+        add_state(2, 0)
+        multiply(2, high)
+        add_state(2, 1, handed_late("rows31"))
+
+        put_back(2, 0)
+        quantise_h(3, handed_late("y2"))
+        put_back(2, 1)
+        wide = handed_late("h31")([P, 2 * WIDTH], F32, "fresh")
+        add_state(2, 3, into=wide[:, :WIDTH])
+        nonlinear_sums(3, low)
+        nonlinear_sums(3, high)
+        add_state(2, 2, handed_late("y2"))
+        product = from_vector([P, 2, WIDTH], F32, "drift")
+        nc.vector.tensor_tensor(product[:], y_acc[3, low][:], linear[3, low], MULT)
+        drift[3, 0], drift[3, 1] = product[:, 0, :], product[:, 1, :]
+        put_back(2, 2)
+        copy_nonlinear(3, high)
+        add_state(3, 0)
+        add_state(3, 1)
+        multiply(3, high)
+        add_state(3, 2)
+        add_state(3, 3, into=wide[:, WIDTH:])
+        for n in range(ROW_TILES - 1):
+            put_back(3, n)
+        scatter(3, 2 * WIDTH, wide[:])
 
         for n in range(ROW_TILES - 1):
             nc.sync.dma_start(out[n * P : (n + 1) * P, :], state[n][:])

@@ -42,10 +42,10 @@ def tile_list_sense_drift_rewrite_kernel(
         psum = ctx.enter_context(tc.psum_pool(name="psum", bufs=8))
 
         def from_vector(shape, dtype, name):
-            return ring.tile(shape, dtype, name=name, tag="from_vector", bufs=19, align_bytes=64)
+            return ring.tile(shape, dtype, name=name, tag="from_vector", bufs=16, align_bytes=64)
 
         def from_scalar(shape, dtype, name):
-            return ring.tile(shape, dtype, name=name, tag="from_scalar", bufs=12, align_bytes=64)
+            return ring.tile(shape, dtype, name=name, tag="from_scalar", bufs=13, align_bytes=64)
 
         def from_gpsimd(shape, dtype, name):
             return raw.tile(shape, dtype, name=name, tag="from_gpsimd", bufs=12, offset=0)
@@ -54,7 +54,7 @@ def tile_list_sense_drift_rewrite_kernel(
             return lambda shape, dtype, name: ring.tile(shape, dtype, name=name, tag=tag, bufs=1, align_bytes=64)
 
         def handed_late(tag):
-            place = 3 * BLOCK_BYTES + 2048 * ("rows31", "h31", "d2", "y2").index(tag)
+            place = 3 * BLOCK_BYTES + 2048 * ("rows21", "rows31", "next_turn", "last_turn").index(tag)
             return lambda shape, dtype, name: raw.tile(shape, dtype, name=name, tag=tag, bufs=1, align_bytes=64, offset=place)
 
         def bank(name, parts):
@@ -126,11 +126,11 @@ def tile_list_sense_drift_rewrite_kernel(
         w1_raw[1, 1] = load_w1_block(1)[:]
         load_state(2)
         load_weight_scales((0, 1))
-        load_state(3)
+        load_state(1)
         load_weight_scales((2, 3))
         w3_codes = [load_w3_half(0)]
+        load_state(3)
         w2_codes = [load_w2_half(0)]
-        load_state(1)
         load_state(0)
         w3_codes.append(load_w3_half(1))
         w2_codes.append(load_w2_half(1))
@@ -179,7 +179,7 @@ def tile_list_sense_drift_rewrite_kernel(
         for u in range(2):
             quantise_w1(0, 1, u)
         quantise_w1(1, 0, 1)
-        vector_cast(1, 1, 0)
+        vector_cast(1, 1, 0, handed("after_cast"))
         vector_cast(1, 1, 1, handed("after_w1"))
         for u in range(2):
             quantise_w1(1, 1, u)
@@ -252,8 +252,8 @@ def tile_list_sense_drift_rewrite_kernel(
                 )
             y_acc[s, rows] = acc
 
-        def squash(s, b):
-            for u in range(2):
+        def squash(s, b, halves=(0, 1)):
+            for u in halves:
                 act[s, b, u] = from_scalar([P, 2, WIDTH], F32, "act")
                 nc.scalar.activation(act[s, b, u][:], pre[s, b, u][:], TANH)
 
@@ -272,9 +272,10 @@ def tile_list_sense_drift_rewrite_kernel(
                 )
 
         def interleave(s, b, tile=from_scalar):
-            h_grouped[s, b] = tile([P, WIDTH * PACK], BF16, "h_grouped")
+            grouped = tile([P, WIDTH * PACK], BF16, "h_grouped")
+            h_grouped[s, b] = [grouped[:]]
             nc.scalar.copy(
-                h_grouped[s, b][:].rearrange("p (c i t) -> p c t i", i=4, t=PACK),
+                grouped[:].rearrange("p (c i t) -> p c t i", i=4, t=PACK),
                 h_rows[s, b][:].rearrange("p t (c i) -> p c t i", i=4),
             )
 
@@ -290,36 +291,52 @@ def tile_list_sense_drift_rewrite_kernel(
             nc.scalar.copy(copy[:], y_acc[s, rows][:, : len(rows), :])
             nonlinear[s, rows] = copy[:]
 
-        def gains_and_round(s, b, tile):
-            h_grouped[s, b] = tile([P, WIDTH * PACK], BF16, "h_grouped")
+        def gains_and_round(s, b, into, first, count):
             nc.gpsimd.tensor_tensor(
-                h_grouped[s, b][:].rearrange("p (c t) -> p c t", t=PACK),
-                act[s, b][:],
-                gains[:, b : b + 1, :].to_broadcast([P, WIDTH, PACK]),
+                into.rearrange("p (c t) -> p c t", t=PACK),
+                act[s, b][:, first : first + count, :],
+                gains[:, b : b + 1, :].to_broadcast([P, count, PACK]),
                 MULT,
             )
 
         def multiply(s, rows, tile=from_gpsimd):
-            product = tile([P, len(rows), WIDTH], F32, "drift")
-            nc.gpsimd.tensor_tensor(product[:], nonlinear[s, rows], linear[s, rows], MULT)
+            drift[s, rows] = tile([P, len(rows), WIDTH], F32, "drift")[:]
+            nc.gpsimd.tensor_tensor(drift[s, rows], nonlinear[s, rows], linear[s, rows], MULT)
+
+        def add_state(s, rows, into):
+            nc.gpsimd.tensor_tensor(into, drift[s, rows], picked[s, rows], ADD)
             for i, n in enumerate(rows):
-                drift[s, n] = product[:, i, :]
+                fresh[s, n] = into[:, i, :]
 
-        def add_state(s, n, tile=from_gpsimd, into=None):
-            if into is None:
-                into = tile([P, WIDTH], F32, "fresh")[:]
-            nc.gpsimd.tensor_tensor(into, drift[s, n], picked[n][:, columns(s)], ADD)
-            fresh[s, n] = into
+        def fresh_tile(rows, tile=from_gpsimd):
+            return tile([P, len(rows), WIDTH], F32, "fresh")[:]
 
-        def pick(n):
-            picked[n] = gathered(state[n], F32, "picked")
+        def pick(n, into, first_slice):
+            count = into.shape[2]
+            nc.vector.tensor_copy(into[:, n % 2, :], state[n][:].indirect(listed(first_slice * WIDTH, count)))
 
-        def quantise_h(s, tile=from_vector):
+        def picked_tile(rows, first_slice, slices, tile):
+            both = tile([P, 2, slices * WIDTH], F32, "picked")
+            for s in range(slices):
+                picked[first_slice + s, rows] = both[:, :, columns(s)]
+                for i, n in enumerate(rows):
+                    picked[first_slice + s, (n,)] = both[:, i : i + 1, columns(s)]
+            return both
+
+        def quantise_h(s, tile):
             codes = tile([P, PASSES * WIDTH], U32, "h_codes")
             for b in range(PASSES):
                 h_codes[s, b] = codes[:, b * WIDTH : (b + 1) * WIDTH]
                 h_plane[s, b] = keep.tile([P, WIDTH], U8, name="h_plane%d_%d" % (s, b), align_bytes=64)
-                nc.vector.quantize_mx(h_codes[s, b].bitcast(E4M3), h_plane[s, b][:], h_grouped[s, b][:])
+                first = 0
+                for piece in h_grouped[s, b]:
+                    cols = slice(first, first + piece.shape[1] // PACK)
+                    nc.vector.quantize_mx(h_codes[s, b][:, cols].bitcast(E4M3), h_plane[s, b][:, cols], piece)
+                    first = cols.stop
+
+        def multiply_from_bank(s, rows):
+            drift[s, rows] = from_vector([P, len(rows), WIDTH], F32, "drift")[:]
+            nc.vector.tensor_tensor(drift[s, rows], y_acc[s, rows][:, : len(rows), :], linear[s, rows], MULT)
 
         def scatter(n, first, values):
             nc.vector.tensor_copy(state[n][:].indirect(listed(first, values.shape[1])), values)
@@ -328,6 +345,7 @@ def tile_list_sense_drift_rewrite_kernel(
             scatter(n, s * WIDTH, fresh[s, n])
 
         low, high = (0, 1), (2, 3)
+        half = P * PACK
         in_turn = handed("in_turn")
 
         sums_by_rows(0, 0)
@@ -337,64 +355,76 @@ def tile_list_sense_drift_rewrite_kernel(
         sums_by_columns(1, 1)
         squash(0, 0)
         squash_interleaved(1, 0)
-        gains_and_round(1, 0, handed("after_w1"))
+        h_early = handed("after_w1")([P, half], BF16, "h_grouped")
+        gains_and_round(1, 0, h_early[:], 0, P)
         apply_gains(0, 0)
         squash_interleaved(0, 1)
-        gains_and_round(0, 1, in_turn)
+        h_whole = in_turn([P, 2 * half], BF16, "h_grouped")
+        for c in range(2):
+            gains_and_round(0, 1, h_whole[:, c * half : (c + 1) * half], c * P, P)
+        h_grouped[0, 1] = [h_whole[:]]
         interleave(0, 0)
         squash_interleaved(1, 1)
-        pick(2)
-        pick(3)
-        quantise_h(0)
-        gains_and_round(1, 1, in_turn)
-        pick(1)
-        squash(2, 0)
-        apply_gains(2, 0)
+
+        high_all = picked_tile(high, 0, SLICES, handed("after_cast"))
+        pick(2, high_all, 0)
+        low_second = picked_tile(low, 1, 1, from_vector)
+        low_first = picked_tile(low, 0, 1, handed("low_first"))
+        low_late = picked_tile(low, 2, 2, handed("low_late"))
+        pick(1, low_second, 1)
+        pick(1, low_first, 0)
+        pick(1, low_late, 2)
+        quantise_h(0, from_vector)
+        h_late = in_turn([P, 3 * half], BF16, "h_grouped")
+        gains_and_round(1, 0, h_late[:, :half], P, P)
+        gains_and_round(1, 1, h_late[:, half:], 0, WIDTH)
+        h_grouped[1, 0] = [h_early[:], h_late[:, :half]]
+        h_grouped[1, 1] = [h_late[:, half:]]
+        pick(3, high_all, 0)
+
         linear_sums(0, 0)
         linear_sums(1, 0)
         sums_by_rows(2, 1)
         nonlinear_sums(0, low)
-        copy_linear(0, 0)
-        copy_nonlinear(0, low)
-        interleave(2, 0, handed("h20"))
-        picked[0] = from_vector([P, S], F32, "picked")
-        nc.vector.tensor_copy(picked[0][:, :WIDTH], state[0][:].indirect(listed(0, WIDTH)))
-        nc.vector.tensor_copy(picked[0][:, WIDTH:], state[0][:].indirect(listed(WIDTH, S - WIDTH)))
-        quantise_h(1)
-        multiply(0, low)
-        add_state(0, 0)
-        add_state(0, 1, handed("after_w1"))
-
+        sums_by_rows(3, 0)
         linear_sums(0, 1)
         nonlinear_sums(0, high)
-        linear_sums(1, 1)
-        nonlinear_sums(1, low)
-        nonlinear_sums(1, high)
+        squash(2, 0)
+        copy_linear(0, 0)
+        apply_gains(2, 0)
+        interleave(2, 0)
         copy_linear(1, 0)
+        squash(2, 1, (0,))
         copy_linear(0, 1)
         copy_nonlinear(0, high)
-        squash(2, 1)
-        apply_gains(2, 1, handed("y1"))
+        squash(2, 1, (1,))
+        apply_gains(2, 1, handed_late("rows21"))
+
+        multiply_from_bank(0, low)
+        pick(0, low_first, 0)
+        pick(0, low_second, 1)
+        pick(0, low_late, 2)
+        add_state(0, low, fresh_tile(low))
+        quantise_h(1, handed("low_first"))
+        nonlinear_sums(1, low)
+        linear_sums(1, 1)
+        nonlinear_sums(1, high)
+        copy_nonlinear(1, low)
+        interleave(2, 1, handed_late("next_turn"))
         copy_linear(1, 1)
-        interleave(2, 1, handed("h21"))
-        copy_nonlinear(1, low, handed("y1"))
         copy_nonlinear(1, high)
         multiply(0, high, in_turn)
-        add_state(0, 2)
-        add_state(0, 3)
+        add_state(0, high, fresh_tile(high))
         for n in range(ROW_TILES):
             put_back(0, n)
-        multiply(1, low)
-        add_state(1, 0)
+        multiply(1, low, in_turn)
+        add_state(1, low, fresh_tile(low, handed_late("rows21")))
 
-        quantise_h(2, handed("y1"))
-        add_state(1, 1, handed("h20"))
-        multiply(1, high, handed("h21"))
-        add_state(1, 2)
-        add_state(1, 3)
+        quantise_h(2, in_turn)
+        multiply(1, high, handed_late("next_turn"))
+        add_state(1, high, fresh_tile(high))
         for n in range(ROW_TILES):
             put_back(1, n)
-        sums_by_rows(3, 0)
         linear_sums(2, 0)
         sums_by_rows(3, 1)
         linear_sums(2, 1)
@@ -403,43 +433,40 @@ def tile_list_sense_drift_rewrite_kernel(
         linear_sums(3, 0)
         linear_sums(3, 1)
         squash(3, 0)
-        apply_gains(3, 0, handed_late("y2"))
-        interleave(3, 0, handed("h30"))
-        squash(3, 1)
+        apply_gains(3, 0)
         copy_linear(2, 0)
+        interleave(3, 0)
+        squash(3, 1)
         copy_nonlinear(2, low)
-        copy_linear(2, 1)
-        copy_nonlinear(2, high, handed_late("y2"))
         apply_gains(3, 1, handed_late("rows31"))
-        interleave(3, 1, handed_late("h31"))
+        interleave(3, 1, handed_late("last_turn"))
+        copy_linear(2, 1)
+        copy_nonlinear(2, high)
         copy_linear(3, 0)
         copy_linear(3, 1)
-        multiply(2, low)
-        add_state(2, 0)
-        multiply(2, high)
-        add_state(2, 1, handed_late("rows31"))
+        multiply(2, low, handed_late("next_turn"))
+        add_state(2, low, fresh_tile(low, handed_late("rows31")))
 
+        quantise_h(3, handed_late("next_turn"))
+        wide = keep.tile([P, 2, 2 * WIDTH], F32, name="wide")
+        multiply(2, high, handed_late("last_turn"))
+        add_state(2, high, wide[:, :, :WIDTH])
+        for rows in ((0,), (1,), high):
+            nonlinear_sums(3, rows)
         put_back(2, 0)
-        quantise_h(3, handed_late("y2"))
         put_back(2, 1)
-        wide = handed_late("h31")([P, 2 * WIDTH], F32, "fresh")
-        add_state(2, 3, into=wide[:, :WIDTH])
-        nonlinear_sums(3, low)
-        nonlinear_sums(3, high)
-        add_state(2, 2, handed_late("y2"))
-        product = from_vector([P, 2, WIDTH], F32, "drift")
-        nc.vector.tensor_tensor(product[:], y_acc[3, low][:], linear[3, low], MULT)
-        drift[3, 0], drift[3, 1] = product[:, 0, :], product[:, 1, :]
+        multiply_from_bank(3, (0,))
         put_back(2, 2)
+        copy_nonlinear(3, (1,))
         copy_nonlinear(3, high)
-        add_state(3, 0)
-        add_state(3, 1)
+        multiply(3, (1,))
+        for rows in ((0,), (1,)):
+            add_state(3, rows, fresh_tile(rows))
         multiply(3, high)
-        add_state(3, 2)
-        add_state(3, 3, into=wide[:, WIDTH:])
+        add_state(3, high, wide[:, :, WIDTH:])
         for n in range(ROW_TILES - 1):
             put_back(3, n)
-        scatter(3, 2 * WIDTH, wide[:])
+        scatter(3, 2 * WIDTH, wide[:, 1, :])
 
         for n in range(ROW_TILES - 1):
             nc.sync.dma_start(out[n * P : (n + 1) * P, :], state[n][:])

@@ -28,6 +28,7 @@ TAB_PLANE_ROW = 8
 W3_PLANE_ROW = 12
 WIDTH = 256
 SLICES = S // WIDTH
+EARLY = 192
 BLOCK_BYTES = PACK * PASS * 4
 
 
@@ -118,9 +119,9 @@ def tile_list_sense_drift_rewrite_kernel(
         nc.sync.dma_start(w1_early[:, :2, :], early_rows[:, :2, :])
         load_table_scales((2, 3))
         nc.sync.dma_start(w1_early[:, 2:, :], early_rows[:, 2:, :])
-        tab.append(load_table_pass(1))
         w1_raw = {(b, 0): w1_early[:, :, b * PASS : (b + 1) * PASS] for b in range(PASSES)}
         w1_raw[0, 1] = load_w1_block(0)[:]
+        tab.append(load_table_pass(1))
         gains = keep.tile([P, PASSES, PACK], F32, name="gains")
         nc.sync.dma_start(gains[:], gain.rearrange("(b p t) -> p b t", b=PASSES, t=PACK))
         w1_raw[1, 1] = load_w1_block(1)[:]
@@ -128,8 +129,8 @@ def tile_list_sense_drift_rewrite_kernel(
         load_weight_scales((0, 1))
         load_state(1)
         load_weight_scales((2, 3))
-        w3_codes = [load_w3_half(0)]
         load_state(3)
+        w3_codes = [load_w3_half(0)]
         w2_codes = [load_w2_half(0)]
         load_state(0)
         w3_codes.append(load_w3_half(1))
@@ -172,13 +173,15 @@ def tile_list_sense_drift_rewrite_kernel(
             scalar_cast(1, 0, u)
         for u in range(2):
             quantise_w1(0, 0, u)
-        v_codes.append(gathered(tab[1], U32, "v_codes"))
         vector_cast(0, 1, 0)
         scalar_cast(0, 1, 1)
-        quantise_w1(1, 0, 0)
+        for u in range(2):
+            quantise_w1(1, 0, u)
         for u in range(2):
             quantise_w1(0, 1, u)
-        quantise_w1(1, 0, 1)
+        v_codes.append(from_vector([P, S], U32, "v_codes"))
+        for first, count in ((0, WIDTH), (WIDTH, WIDTH), (2 * WIDTH, 2 * WIDTH)):
+            nc.vector.tensor_copy(v_codes[1][:, first : first + count], tab[1][:].indirect(listed(first, count)))
         vector_cast(1, 1, 0, handed("after_cast"))
         vector_cast(1, 1, 1, handed("after_w1"))
         for u in range(2):
@@ -345,7 +348,6 @@ def tile_list_sense_drift_rewrite_kernel(
             scatter(n, s * WIDTH, fresh[s, n])
 
         low, high = (0, 1), (2, 3)
-        half = P * PACK
         in_turn = handed("in_turn")
 
         sums_by_rows(0, 0)
@@ -355,13 +357,12 @@ def tile_list_sense_drift_rewrite_kernel(
         sums_by_columns(1, 1)
         squash(0, 0)
         squash_interleaved(1, 0)
-        h_early = handed("after_w1")([P, half], BF16, "h_grouped")
-        gains_and_round(1, 0, h_early[:], 0, P)
+        h_early = handed("after_w1")([P, EARLY * PACK], BF16, "h_grouped")
+        gains_and_round(1, 0, h_early[:], 0, EARLY)
         apply_gains(0, 0)
         squash_interleaved(0, 1)
-        h_whole = in_turn([P, 2 * half], BF16, "h_grouped")
-        for c in range(2):
-            gains_and_round(0, 1, h_whole[:, c * half : (c + 1) * half], c * P, P)
+        h_whole = in_turn([P, WIDTH * PACK], BF16, "h_grouped")
+        gains_and_round(0, 1, h_whole[:], 0, WIDTH)
         h_grouped[0, 1] = [h_whole[:]]
         interleave(0, 0)
         squash_interleaved(1, 1)
@@ -375,23 +376,24 @@ def tile_list_sense_drift_rewrite_kernel(
         pick(1, low_first, 0)
         pick(1, low_late, 2)
         quantise_h(0, from_vector)
-        h_late = in_turn([P, 3 * half], BF16, "h_grouped")
-        gains_and_round(1, 0, h_late[:, :half], P, P)
-        gains_and_round(1, 1, h_late[:, half:], 0, WIDTH)
-        h_grouped[1, 0] = [h_early[:], h_late[:, :half]]
-        h_grouped[1, 1] = [h_late[:, half:]]
+        rest = (WIDTH - EARLY) * PACK
+        h_late = in_turn([P, rest + WIDTH * PACK], BF16, "h_grouped")
+        gains_and_round(1, 0, h_late[:, :rest], EARLY, WIDTH - EARLY)
+        gains_and_round(1, 1, h_late[:, rest:], 0, WIDTH)
+        h_grouped[1, 0] = [h_early[:, : P * PACK], h_early[:, P * PACK :], h_late[:, :rest]]
+        h_grouped[1, 1] = [h_late[:, rest:]]
         pick(3, high_all, 0)
 
-        linear_sums(0, 0)
-        linear_sums(1, 0)
         sums_by_rows(2, 1)
+        linear_sums(0, 0)
         nonlinear_sums(0, low)
+        linear_sums(1, 0)
         sums_by_rows(3, 0)
         linear_sums(0, 1)
         nonlinear_sums(0, high)
         squash(2, 0)
-        copy_linear(0, 0)
         apply_gains(2, 0)
+        copy_linear(0, 0)
         interleave(2, 0)
         copy_linear(1, 0)
         squash(2, 1, (0,))

@@ -49,7 +49,7 @@ def tile_list_sense_drift_rewrite_kernel(
             return ring.tile(shape, dtype, name=name, tag="from_scalar", bufs=13, align_bytes=64)
 
         def from_gpsimd(shape, dtype, name):
-            return raw.tile(shape, dtype, name=name, tag="from_gpsimd", bufs=12, offset=0)
+            return raw.tile(shape, dtype, name=name, tag="from_gpsimd", bufs=6, offset=0)
 
         def handed(tag):
             return lambda shape, dtype, name: ring.tile(shape, dtype, name=name, tag=tag, bufs=1, align_bytes=64)
@@ -293,6 +293,8 @@ def tile_list_sense_drift_rewrite_kernel(
             copy = tile([P, len(rows), WIDTH], F32, "nonlinear")
             nc.scalar.copy(copy[:], y_acc[s, rows][:, : len(rows), :])
             nonlinear[s, rows] = copy[:]
+            for i, n in enumerate(rows):
+                nonlinear[s, (n,)] = copy[:, i : i + 1, :]
 
         def gains_and_round(s, b, into, first, count):
             nc.gpsimd.tensor_tensor(
@@ -450,25 +452,28 @@ def tile_list_sense_drift_rewrite_kernel(
         add_state(2, low, fresh_tile(low, handed_late("rows31")))
 
         quantise_h(3, handed_late("next_turn"))
-        wide = keep.tile([P, 2, 2 * WIDTH], F32, name="wide")
-        multiply(2, high, handed_late("last_turn"))
-        add_state(2, high, wide[:, :, :WIDTH])
-        for rows in ((0,), (1,), high):
-            nonlinear_sums(3, rows)
-        put_back(2, 0)
-        put_back(2, 1)
-        multiply_from_bank(3, (0,))
-        put_back(2, 2)
-        copy_nonlinear(3, (1,))
-        copy_nonlinear(3, high)
-        multiply(3, (1,))
-        for rows in ((0,), (1,)):
-            add_state(3, rows, fresh_tile(rows))
-        multiply(3, high)
-        add_state(3, high, wide[:, :, WIDTH:])
+        multiply(2, (2,), handed_late("last_turn"))
+        add_state(2, (2,), fresh_tile((2,)))
         for n in range(ROW_TILES - 1):
+            put_back(2, n)
+        for rows in (low, high):
+            nonlinear_sums(3, rows)
+            copy_nonlinear(3, rows)
+        multiply(3, low)
+        for n in low:
+            drift[3, (n,)] = drift[3, low][:, n : n + 1, :]
+            add_state(3, (n,), fresh_tile((n,)))
             put_back(3, n)
-        scatter(3, 2 * WIDTH, wide[:, 1, :])
+        wide = from_gpsimd([P, 2, 2 * WIDTH], F32, "drift")
+        nc.gpsimd.tensor_tensor(wide[:, :, WIDTH:], nonlinear[3, high], linear[3, high], MULT)
+        nc.gpsimd.tensor_tensor(wide[:, 1:, :WIDTH], nonlinear[2, (3,)], linear[2, (3,)], MULT)
+        for n, first in ((2, 3 * WIDTH), (3, 2 * WIDTH)):
+            nc.vector.tensor_tensor(
+                state[n][:].indirect(listed(first, S - first)),
+                high_all[:, n % 2, first:],
+                wide[:, n % 2, first - 2 * WIDTH :],
+                ADD,
+            )
 
         for n in range(ROW_TILES - 1):
             nc.sync.dma_start(out[n * P : (n + 1) * P, :], state[n][:])

@@ -28,7 +28,7 @@ TAB_PLANE_ROW = 8
 W3_PLANE_ROW = 12
 WIDTH = 256
 SLICES = S // WIDTH
-EARLY = 192
+AHEAD = 384
 BLOCK_BYTES = PACK * PASS * 4
 
 
@@ -127,9 +127,9 @@ def tile_list_sense_drift_rewrite_kernel(
         w1_raw[1, 1] = load_w1_block(1)[:]
         load_state(2)
         load_weight_scales((0, 1))
+        load_state(3)
         load_state(1)
         load_weight_scales((2, 3))
-        load_state(3)
         w3_codes = [load_w3_half(0)]
         w2_codes = [load_w2_half(0)]
         load_state(0)
@@ -296,11 +296,13 @@ def tile_list_sense_drift_rewrite_kernel(
             for i, n in enumerate(rows):
                 nonlinear[s, (n,)] = copy[:, i : i + 1, :]
 
-        def gains_and_round(s, b, into, first, count):
+        def gains_and_round(s, b, tile):
+            grouped = tile([P, WIDTH * PACK], BF16, "h_grouped")
+            h_grouped[s, b] = [grouped[:]]
             nc.gpsimd.tensor_tensor(
-                into.rearrange("p (c t) -> p c t", t=PACK),
-                act[s, b][:, first : first + count, :],
-                gains[:, b : b + 1, :].to_broadcast([P, count, PACK]),
+                grouped[:].rearrange("p (c t) -> p c t", t=PACK),
+                act[s, b][:],
+                gains[:, b : b + 1, :].to_broadcast([P, WIDTH, PACK]),
                 MULT,
             )
 
@@ -316,9 +318,9 @@ def tile_list_sense_drift_rewrite_kernel(
         def fresh_tile(rows, tile=from_gpsimd):
             return tile([P, len(rows), WIDTH], F32, "fresh")[:]
 
-        def pick(n, into, first_slice):
-            count = into.shape[2]
-            nc.vector.tensor_copy(into[:, n % 2, :], state[n][:].indirect(listed(first_slice * WIDTH, count)))
+        def pick(n, into, first_slice, start=0, stop=None):
+            part = into[:, n % 2, start:stop]
+            nc.vector.tensor_copy(part, state[n][:].indirect(listed(first_slice * WIDTH + start, part.shape[1])))
 
         def picked_tile(rows, first_slice, slices, tile):
             both = tile([P, 2, slices * WIDTH], F32, "picked")
@@ -359,32 +361,25 @@ def tile_list_sense_drift_rewrite_kernel(
         sums_by_columns(1, 1)
         squash(0, 0)
         squash_interleaved(1, 0)
-        h_early = handed("after_w1")([P, EARLY * PACK], BF16, "h_grouped")
-        gains_and_round(1, 0, h_early[:], 0, EARLY)
+        gains_and_round(1, 0, handed("after_w1"))
         apply_gains(0, 0)
         squash_interleaved(0, 1)
-        h_whole = in_turn([P, WIDTH * PACK], BF16, "h_grouped")
-        gains_and_round(0, 1, h_whole[:], 0, WIDTH)
-        h_grouped[0, 1] = [h_whole[:]]
+        gains_and_round(0, 1, in_turn)
         interleave(0, 0)
         squash_interleaved(1, 1)
 
         high_all = picked_tile(high, 0, SLICES, handed("after_cast"))
         pick(2, high_all, 0)
-        low_second = picked_tile(low, 1, 1, from_vector)
-        low_first = picked_tile(low, 0, 1, handed("low_first"))
-        low_late = picked_tile(low, 2, 2, handed("low_late"))
-        pick(1, low_second, 1)
-        pick(1, low_first, 0)
-        pick(1, low_late, 2)
-        quantise_h(0, from_vector)
-        rest = (WIDTH - EARLY) * PACK
-        h_late = in_turn([P, rest + WIDTH * PACK], BF16, "h_grouped")
-        gains_and_round(1, 0, h_late[:, :rest], EARLY, WIDTH - EARLY)
-        gains_and_round(1, 1, h_late[:, rest:], 0, WIDTH)
-        h_grouped[1, 0] = [h_early[:, : P * PACK], h_early[:, P * PACK :], h_late[:, :rest]]
-        h_grouped[1, 1] = [h_late[:, rest:]]
         pick(3, high_all, 0)
+        low_middle = picked_tile(low, 1, 2, from_vector)
+        low_first = picked_tile(low, 0, 1, handed("low_first"))
+        low_last = picked_tile(low, 3, 1, handed("low_late"))
+        pick(1, low_middle, 1, 0, AHEAD)
+        quantise_h(0, from_vector)
+        gains_and_round(1, 1, in_turn)
+        pick(1, low_middle, 1, AHEAD, 2 * WIDTH)
+        pick(1, low_first, 0)
+        pick(1, low_last, 3)
 
         sums_by_rows(2, 1)
         linear_sums(0, 0)
@@ -406,8 +401,8 @@ def tile_list_sense_drift_rewrite_kernel(
 
         multiply_from_bank(0, low)
         pick(0, low_first, 0)
-        pick(0, low_second, 1)
-        pick(0, low_late, 2)
+        pick(0, low_middle, 1)
+        pick(0, low_last, 3)
         add_state(0, low, fresh_tile(low))
         quantise_h(1, handed("low_first"))
         nonlinear_sums(1, low)

@@ -388,6 +388,7 @@ def tile_list_sense_drift_rewrite_kernel(
         sums_by_rows(3, 0)
         linear_sums(0, 1)
         nonlinear_sums(0, high)
+        linear_sums(1, 1)
         squash(2, 0)
         apply_gains(2, 0)
         copy_linear(0, 0)
@@ -406,11 +407,10 @@ def tile_list_sense_drift_rewrite_kernel(
         add_state(0, low, fresh_tile(low))
         quantise_h(1, handed("low_first"))
         nonlinear_sums(1, low)
-        linear_sums(1, 1)
         nonlinear_sums(1, high)
-        copy_nonlinear(1, low)
-        interleave(2, 1, handed_late("next_turn"))
         copy_linear(1, 1)
+        interleave(2, 1, handed_late("next_turn"))
+        copy_nonlinear(1, low)
         copy_nonlinear(1, high)
         multiply(0, high, in_turn)
         add_state(0, high, fresh_tile(high))
@@ -436,8 +436,8 @@ def tile_list_sense_drift_rewrite_kernel(
         copy_linear(2, 0)
         interleave(3, 0)
         squash(3, 1)
-        copy_nonlinear(2, low)
         apply_gains(3, 1, handed_late("rows31"))
+        copy_nonlinear(2, low)
         interleave(3, 1, handed_late("last_turn"))
         copy_linear(2, 1)
         copy_nonlinear(2, high)

@@ -1,6 +1,7 @@
 from contextlib import ExitStack
 
 import concourse.mybir as mybir
+from concourse.masks import make_identity
 
 K, T, S, H, N = 1024, 2048, 1024, 1024, 512
 FLOPS = 2 * S * (K * H + H * N + K * N)
@@ -110,6 +111,11 @@ def tile_list_sense_drift_rewrite_kernel(
         w2_plane = zeroed_plane([P, PASSES, N], "w2_plane")
         state = [keep.tile([P, T], F32, name="state%d" % n) for n in range(ROW_TILES)]
 
+        gain_rows = keep.tile([P, PASS], F32, name="gain_rows")
+        nc.gpsimd.memset(gain_rows[:], 0.0)
+        identity = keep.tile([P, P], F32, name="identity")
+        make_identity(nc, identity[:])
+
         tab = [load_table_pass(0)]
         offsets = keep.tile([P, S // PER_COLUMN], U16, name="offsets")
         nc.sync.dma_start(offsets[:], offs)
@@ -120,10 +126,9 @@ def tile_list_sense_drift_rewrite_kernel(
         load_table_scales((2, 3))
         nc.sync.dma_start(w1_early[:, 2:, :], early_rows[:, 2:, :])
         w1_raw = {(b, 0): w1_early[:, :, b * PASS : (b + 1) * PASS] for b in range(PASSES)}
+        nc.sync.dma_start(gain_rows[:PASSES, :], gain.rearrange("(b c) -> b c", b=PASSES))
         w1_raw[0, 1] = load_w1_block(0)[:]
         tab.append(load_table_pass(1))
-        gains = keep.tile([P, PASSES, PACK], F32, name="gains")
-        nc.sync.dma_start(gains[:], gain.rearrange("(b p t) -> p b t", b=PASSES, t=PACK))
         w1_raw[1, 1] = load_w1_block(1)[:]
         load_state(2)
         load_weight_scales((0, 1))
@@ -141,6 +146,12 @@ def tile_list_sense_drift_rewrite_kernel(
 
         def columns(s, first=0, count=WIDTH):
             return slice(s * WIDTH + first, s * WIDTH + first + count)
+
+        turned = bank("turned", PACK)
+        for t in range(PACK):
+            nc.tensor.transpose(turned[:, t, :], gain_rows[:, t:PASS:PACK], identity[:])
+        gains = keep.tile([P, PASSES, PACK], F32, name="gains")
+        nc.scalar.copy(gains[:], turned[:, :, :PASSES].rearrange("p t b -> p b t"))
 
         w1_grouped, w1_codes, w1_plane = {}, {}, {}
 

@@ -1,3 +1,4 @@
+import math
 from contextlib import ExitStack
 
 import concourse.mybir as mybir
@@ -29,7 +30,6 @@ TAB_PLANE_ROW = 8
 W3_PLANE_ROW = 12
 WIDTH = 256
 SLICES = S // WIDTH
-AHEAD = 384
 BLOCK_BYTES = PACK * PASS * 4
 
 
@@ -44,10 +44,10 @@ def tile_list_sense_drift_rewrite_kernel(
         psum = ctx.enter_context(tc.psum_pool(name="psum", bufs=8))
 
         def from_vector(shape, dtype, name):
-            return ring.tile(shape, dtype, name=name, tag="from_vector", bufs=16, align_bytes=64)
+            return ring.tile(shape, dtype, name=name, tag="from_vector", bufs=17, align_bytes=64)
 
         def from_scalar(shape, dtype, name):
-            return ring.tile(shape, dtype, name=name, tag="from_scalar", bufs=13, align_bytes=64)
+            return ring.tile(shape, dtype, name=name, tag="from_scalar", bufs=14, align_bytes=64)
 
         def from_gpsimd(shape, dtype, name):
             return raw.tile(shape, dtype, name=name, tag="from_gpsimd", bufs=6, offset=0)
@@ -55,9 +55,12 @@ def tile_list_sense_drift_rewrite_kernel(
         def handed(tag):
             return lambda shape, dtype, name: ring.tile(shape, dtype, name=name, tag=tag, bufs=1, align_bytes=64)
 
-        def handed_late(tag):
-            place = 3 * BLOCK_BYTES + 2048 * ("rows21", "rows31", "next_turn", "last_turn").index(tag)
-            return lambda shape, dtype, name: raw.tile(shape, dtype, name=name, tag=tag, bufs=1, align_bytes=64, offset=place)
+        def over(used):
+            def view(shape, dtype, name):
+                flat = used.bitcast(dtype)[:, : math.prod(shape[1:])]
+                return flat if len(shape) == 2 else flat.rearrange("p (r c) -> p r c", r=shape[1])
+
+            return view
 
         def bank(name, parts):
             return psum.tile([P, parts, 512 // parts], F32, name=name, tag="bank")
@@ -86,10 +89,11 @@ def tile_list_sense_drift_rewrite_kernel(
                         scales[:, r:16:4, :].rearrange("a q c -> q a c").bitcast(I32),
                     )
 
-        def load_w1_block(b):
-            block = raw.tile([P, PACK, PASS], F32, name="w1_late%d" % b, offset=(2 + b) * BLOCK_BYTES)
-            nc.sync.dma_start(block[:], w1[PASS:, b * PASS : (b + 1) * PASS].rearrange("(p j) c -> p j c", j=PACK))
-            return block
+        def load_w1_block(b, a):
+            block = raw.tile([P, PACK, PASS], F32, name="w1_raw%d%d" % (b, a), offset=(2 * b + a) * BLOCK_BYTES)
+            rows = w1[a * PASS : (a + 1) * PASS, b * PASS : (b + 1) * PASS]
+            nc.sync.dma_start(block[:], rows.rearrange("(p j) c -> p j c", j=PACK))
+            return block[:]
 
         def load_state(n):
             nc.sync.dma_start(state[n][:], gT[n * P : (n + 1) * P, :])
@@ -120,19 +124,16 @@ def tile_list_sense_drift_rewrite_kernel(
         offsets = keep.tile([P, S // PER_COLUMN], U16, name="offsets")
         nc.sync.dma_start(offsets[:], offs)
         load_table_scales((0, 1))
-        w1_early = raw.tile([P, PACK, H], F32, name="w1_early", offset=0)
-        early_rows = w1[:PASS, :].rearrange("(p j) c -> p j c", j=PACK)
-        nc.sync.dma_start(w1_early[:, :2, :], early_rows[:, :2, :])
+        w1_raw = {(0, 0): load_w1_block(0, 0)}
         load_table_scales((2, 3))
-        nc.sync.dma_start(w1_early[:, 2:, :], early_rows[:, 2:, :])
-        w1_raw = {(b, 0): w1_early[:, :, b * PASS : (b + 1) * PASS] for b in range(PASSES)}
+        w1_raw[0, 1] = load_w1_block(0, 1)
         nc.sync.dma_start(gain_rows[:PASSES, :], gain.rearrange("(b c) -> b c", b=PASSES))
-        w1_raw[0, 1] = load_w1_block(0)[:]
         tab.append(load_table_pass(1))
-        w1_raw[1, 1] = load_w1_block(1)[:]
         load_state(2)
-        load_weight_scales((0, 1))
+        w1_raw[1, 0] = load_w1_block(1, 0)
+        w1_raw[1, 1] = load_w1_block(1, 1)
         load_state(3)
+        load_weight_scales((0, 1))
         load_state(1)
         load_weight_scales((2, 3))
         w3_codes = [load_w3_half(0)]
@@ -158,7 +159,7 @@ def tile_list_sense_drift_rewrite_kernel(
         def cast_w1(b, a, u, tile, cast):
             grouped = tile([P, 2 * PASS], BF16, "w1_grouped")
             src = w1_raw[b, a].rearrange("p j (m t) -> p m j t", t=PACK)
-            cast(grouped[:].rearrange("p (t m j) -> p m j t", t=2, j=PACK), src[:, :, :, 2 * u : 2 * u + 2])
+            cast(grouped[:, :].rearrange("p (t m j) -> p m j t", t=2, j=PACK), src[:, :, :, 2 * u : 2 * u + 2])
             w1_grouped[b, a, u] = grouped
 
         def vector_cast(b, a, u, tile=from_vector):
@@ -170,7 +171,7 @@ def tile_list_sense_drift_rewrite_kernel(
         def quantise_w1(b, a, u):
             w1_codes[b, a, u] = from_vector([P, 2 * P], U32, "w1_codes")
             w1_plane[b, a, u] = keep.tile([P, 2 * P], U8, name="w1_plane%d%d%d" % (b, a, u), align_bytes=64)
-            nc.vector.quantize_mx(w1_codes[b, a, u][:].bitcast(E4M3), w1_plane[b, a, u][:], w1_grouped[b, a, u][:])
+            nc.vector.quantize_mx(w1_codes[b, a, u][:].bitcast(E4M3), w1_plane[b, a, u][:], w1_grouped[b, a, u][:, :])
 
         def gathered(window, dtype, name):
             tile = from_vector([P, S], dtype, name)
@@ -180,23 +181,16 @@ def tile_list_sense_drift_rewrite_kernel(
         v_codes = [gathered(tab[0], U32, "v_codes")]
         v_plane = gathered(tab_plane, U8, "v_plane")
         for u in range(2):
-            vector_cast(0, 0, u)
-            scalar_cast(1, 0, u)
+            scalar_cast(0, 0, u)
         for u in range(2):
             quantise_w1(0, 0, u)
-        vector_cast(0, 1, 0)
-        scalar_cast(0, 1, 1)
-        for u in range(2):
-            quantise_w1(1, 0, u)
+        scalar_cast(0, 1, 0)
+        vector_cast(0, 1, 1)
         for u in range(2):
             quantise_w1(0, 1, u)
         v_codes.append(from_vector([P, S], U32, "v_codes"))
         for first, count in ((0, WIDTH), (WIDTH, WIDTH), (2 * WIDTH, 2 * WIDTH)):
             nc.vector.tensor_copy(v_codes[1][:, first : first + count], tab[1][:].indirect(listed(first, count)))
-        vector_cast(1, 1, 0, handed("after_cast"))
-        vector_cast(1, 1, 1, handed("after_w1"))
-        for u in range(2):
-            quantise_w1(1, 1, u)
 
         def times_table(acc, operands, passes):
             order = [(a, i) for a in passes for i in range(len(operands))]
@@ -224,10 +218,10 @@ def tile_list_sense_drift_rewrite_kernel(
             )
 
         def passes_of(s):
-            return range(PASSES)
+            return range(PASSES) if s == 0 else range(PASSES - 1, -1, -1)
 
-        def sums_by_rows(s, b):
-            for u in range(2):
+        def sums_by_rows(s, b, halves=(0, 1)):
+            for u in halves:
                 pre[s, b, u] = bank("pre", 2)
                 times_table(pre[s, b, u], [w1_operand(b, 2 * u + i, columns(s)) for i in range(2)], passes_of(s))
 
@@ -307,13 +301,13 @@ def tile_list_sense_drift_rewrite_kernel(
             for i, n in enumerate(rows):
                 nonlinear[s, (n,)] = copy[:, i : i + 1, :]
 
-        def gains_and_round(s, b, tile):
-            grouped = tile([P, WIDTH * PACK], BF16, "h_grouped")
-            h_grouped[s, b] = [grouped[:]]
+        def gains_and_round(s, b, tile, first=0, count=WIDTH):
+            grouped = tile([P, count * PACK], BF16, "h_grouped")
+            h_grouped.setdefault((s, b), []).append(grouped[:])
             nc.gpsimd.tensor_tensor(
                 grouped[:].rearrange("p (c t) -> p c t", t=PACK),
-                act[s, b][:],
-                gains[:, b : b + 1, :].to_broadcast([P, WIDTH, PACK]),
+                act[s, b][:, first : first + count, :],
+                gains[:, b : b + 1, :].to_broadcast([P, count, PACK]),
                 MULT,
             )
 
@@ -341,10 +335,10 @@ def tile_list_sense_drift_rewrite_kernel(
                     picked[first_slice + s, (n,)] = both[:, i : i + 1, columns(s)]
             return both
 
-        def quantise_h(s, tile):
-            codes = tile([P, PASSES * WIDTH], U32, "h_codes")
-            for b in range(PASSES):
-                h_codes[s, b] = codes[:, b * WIDTH : (b + 1) * WIDTH]
+        def quantise_h(s, blocks, tile):
+            codes = tile([P, len(blocks) * WIDTH], U32, "h_codes")
+            for i, b in enumerate(blocks):
+                h_codes[s, b] = codes[:, i * WIDTH : (i + 1) * WIDTH]
                 h_plane[s, b] = keep.tile([P, WIDTH], U8, name="h_plane%d_%d" % (s, b), align_bytes=64)
                 first = 0
                 for piece in h_grouped[s, b]:
@@ -362,76 +356,92 @@ def tile_list_sense_drift_rewrite_kernel(
         def put_back(s, n):
             scatter(n, s * WIDTH, fresh[s, n])
 
+        def over_rows(s):
+            return over(h_rows[s, 1][:].rearrange("p t c -> p (t c)"))
+
         low, high = (0, 1), (2, 3)
         in_turn = handed("in_turn")
 
-        sums_by_rows(0, 0)
-        sums_by_columns(1, 0)
-        sums_by_rows(2, 0)
-        sums_by_columns(0, 1)
-        sums_by_columns(1, 1)
-        squash(0, 0)
-        squash_interleaved(1, 0)
-        gains_and_round(1, 0, handed("after_w1"))
-        apply_gains(0, 0)
-        squash_interleaved(0, 1)
-        gains_and_round(0, 1, in_turn)
-        interleave(0, 0)
-        squash_interleaved(1, 1)
+        first_h = handed("first_h")
+        sums_by_columns(0, 0)
+        sums_by_rows(1, 0)
+        sums_by_columns(2, 0)
+        sums_by_rows(3, 0, (0,))
+        squash_interleaved(0, 0)
+        gains_and_round(0, 0, first_h)
+        squash(1, 0)
+        apply_gains(1, 0)
+        squash(3, 0, (0,))
+        interleave(1, 0)
+        scalar_cast(1, 1, 1)
+        squash_interleaved(2, 0)
 
-        high_all = picked_tile(high, 0, SLICES, handed("after_cast"))
+        high_all = picked_tile(high, 0, SLICES, handed("high_all"))
         pick(2, high_all, 0)
+        vector_cast(1, 0, 0)
+        vector_cast(1, 0, 1)
+        quantise_w1(1, 0, 0)
+        vector_cast(1, 1, 0, lambda shape, dtype, name: high_all[:, 1, :PASS].bitcast(dtype))
+        quantise_w1(1, 0, 1)
+        quantise_w1(1, 1, 0)
+        quantise_w1(1, 1, 1)
+        quantise_h(0, (0,), from_vector)
+        quantise_h(1, (0,), from_vector)
+        gains_and_round(2, 0, over(h_grouped[1, 0][0]), 0, P)
+
+        sums_by_columns(0, 1)
+        sums_by_rows(1, 1)
+        squash_interleaved(0, 1)
+        gains_and_round(0, 1, first_h)
         pick(3, high_all, 0)
         low_middle = picked_tile(low, 1, 2, from_vector)
-        low_first = picked_tile(low, 0, 1, handed("low_first"))
-        low_last = picked_tile(low, 3, 1, handed("low_late"))
-        pick(1, low_middle, 1, 0, AHEAD)
-        quantise_h(0, from_vector)
-        gains_and_round(1, 1, in_turn)
-        pick(1, low_middle, 1, AHEAD, 2 * WIDTH)
-        pick(1, low_first, 0)
+        low_last = picked_tile(low, 3, 1, from_vector)
+        pick(1, low_middle, 1)
         pick(1, low_last, 3)
+        quantise_h(0, (1,), from_vector)
+        gains_and_round(2, 0, first_h, P, P)
+        low_first = picked_tile(low, 0, 1, handed("low_first"))
+        pick(1, low_first, 0)
 
         sums_by_rows(2, 1)
         linear_sums(0, 0)
         nonlinear_sums(0, low)
         linear_sums(1, 0)
-        sums_by_rows(3, 0)
+        sums_by_rows(3, 0, (1,))
         linear_sums(0, 1)
         nonlinear_sums(0, high)
         linear_sums(1, 1)
-        squash(2, 0)
-        apply_gains(2, 0)
+        squash(1, 1)
+        apply_gains(1, 1)
+        squash(2, 1)
         copy_linear(0, 0)
-        interleave(2, 0)
-        copy_linear(1, 0)
-        squash(2, 1, (0,))
+        interleave(1, 1)
         copy_linear(0, 1)
         copy_nonlinear(0, high)
-        squash(2, 1, (1,))
-        apply_gains(2, 1, handed_late("rows21"))
+        apply_gains(2, 1)
 
         multiply_from_bank(0, low)
         pick(0, low_first, 0)
         pick(0, low_middle, 1)
         pick(0, low_last, 3)
-        add_state(0, low, fresh_tile(low))
-        quantise_h(1, handed("low_first"))
+        add_state(0, low, fresh_tile(low, over_rows(1)))
+        quantise_h(1, (1,), handed("low_first"))
         nonlinear_sums(1, low)
         nonlinear_sums(1, high)
-        copy_linear(1, 1)
-        interleave(2, 1, handed_late("next_turn"))
+        copy_linear(1, 0)
         copy_nonlinear(1, low)
+        interleave(2, 1)
+        copy_linear(1, 1)
         copy_nonlinear(1, high)
-        multiply(0, high, in_turn)
+        multiply(0, high, over(h_grouped[1, 1][0]))
         add_state(0, high, fresh_tile(high))
         for n in range(ROW_TILES):
             put_back(0, n)
         multiply(1, low, in_turn)
-        add_state(1, low, fresh_tile(low, handed_late("rows21")))
+        add_state(1, low, fresh_tile(low, over_rows(2)))
 
-        quantise_h(2, in_turn)
-        multiply(1, high, handed_late("next_turn"))
+        quantise_h(2, (0, 1), in_turn)
+        multiply(1, high, over(h_grouped[2, 1][0]))
         add_state(1, high, fresh_tile(high))
         for n in range(ROW_TILES):
             put_back(1, n)
@@ -442,23 +452,23 @@ def tile_list_sense_drift_rewrite_kernel(
         nonlinear_sums(2, high)
         linear_sums(3, 0)
         linear_sums(3, 1)
-        squash(3, 0)
+        squash(3, 0, (1,))
         apply_gains(3, 0)
         copy_linear(2, 0)
         interleave(3, 0)
         squash(3, 1)
-        apply_gains(3, 1, handed_late("rows31"))
         copy_nonlinear(2, low)
-        interleave(3, 1, handed_late("last_turn"))
+        apply_gains(3, 1)
         copy_linear(2, 1)
+        interleave(3, 1)
         copy_nonlinear(2, high)
         copy_linear(3, 0)
         copy_linear(3, 1)
-        multiply(2, low, handed_late("next_turn"))
-        add_state(2, low, fresh_tile(low, handed_late("rows31")))
+        multiply(2, low, handed("next_turn"))
+        add_state(2, low, fresh_tile(low, over_rows(3)))
 
-        quantise_h(3, handed_late("next_turn"))
-        multiply(2, (2,), handed_late("last_turn"))
+        quantise_h(3, (0, 1), handed("next_turn"))
+        multiply(2, (2,), over(h_grouped[3, 1][0]))
         add_state(2, (2,), fresh_tile((2,)))
         for n in range(ROW_TILES - 1):
             put_back(2, n)

import math
from contextlib import ExitStack

import concourse.mybir as mybir
from concourse.masks import make_identity

K, T, S, H, N = 1024, 2048, 1024, 1024, 512
FLOPS = 2 * S * (K * H + H * N + K * N)

F32 = mybir.dt.float32
BF16 = mybir.dt.bfloat16
I32 = mybir.dt.int32
U32 = mybir.dt.uint32
U16 = mybir.dt.uint16
U8 = mybir.dt.uint8
E4M3 = mybir.dt.float8_e4m3fn_x4
E2M1 = mybir.dt.float4_e2m1fn_x4
MULT = mybir.AluOpType.mult
ADD = mybir.AluOpType.add
TANH = mybir.ActivationFunctionType.Tanh
COPY = mybir.ActivationFunctionType.Copy

P = 128
PACK = 4
PASS = P * PACK
PASSES = K // PASS
ROW_TILES = N // P
PER_COLUMN = 16
TAB_PLANE_ROW = 8
W3_PLANE_ROW = 12
WIDTH = 256
SLICES = S // WIDTH
BLOCK_BYTES = PACK * PASS * 4


def tile_list_sense_drift_rewrite_kernel(
    tc, tab_words, tab_scales, offs, gT, w1, gain, w2_words, w2_scales, w3_words, w3_scales, out
):
    nc = tc.nc
    with ExitStack() as ctx:
        keep = ctx.enter_context(tc.tile_pool(name="keep", bufs=1))
        raw = ctx.enter_context(tc.tile_pool(name="raw", bufs=1))
        ring = ctx.enter_context(tc.tile_pool(name="ring", bufs=1))
        psum = ctx.enter_context(tc.psum_pool(name="psum", bufs=8))

        def from_vector(shape, dtype, name):
            return ring.tile(shape, dtype, name=name, tag="from_vector", bufs=17, align_bytes=64)

        def from_scalar(shape, dtype, name):
            return ring.tile(shape, dtype, name=name, tag="from_scalar", bufs=14, align_bytes=64)

        def from_gpsimd(shape, dtype, name):
            return raw.tile(shape, dtype, name=name, tag="from_gpsimd", bufs=6, offset=0)

        def handed(tag):
            return lambda shape, dtype, name: ring.tile(shape, dtype, name=name, tag=tag, bufs=1, align_bytes=64)

        def over(used):
            def view(shape, dtype, name):
                flat = used.bitcast(dtype)[:, : math.prod(shape[1:])]
                return flat if len(shape) == 2 else flat.rearrange("p (r c) -> p r c", r=shape[1])

            return view

        def bank(name, parts):
            return psum.tile([P, parts, 512 // parts], F32, name=name, tag="bank")

        def zeroed_plane(shape, name):
            plane = keep.tile(shape, U8, name=name, align_bytes=64)
            nc.vector.memset(plane[:].bitcast(I32), 0)
            return plane

        def load_table_pass(a):
            words = keep.tile([P, T], U32, name="tab%d" % a, align_bytes=64)
            nc.sync.dma_start(words[:].bitcast(I32), tab_words[a].rearrange("p t i -> p (t i)").bitcast(I32))
            return words

        def load_table_scales(rows):
            for r in rows:
                for a in range(PASSES):
                    row = TAB_PLANE_ROW + 4 * a + r
                    nc.sync.dma_start(tab_plane[row:P:32, :].bitcast(I32), tab_scales[a, r:16:4, :].bitcast(I32))

        def load_weight_scales(rows):
            for r in rows:
                for plane, scales, row in ((w3_plane, w3_scales, W3_PLANE_ROW + r), (w2_plane, w2_scales, r)):
                    nc.sync.dma_start(
                        plane[row:P:32, :, :].bitcast(I32),
                        scales[:, r:16:4, :].rearrange("a q c -> q a c").bitcast(I32),
                    )

        def load_w1_block(b, a):
            block = raw.tile([P, PACK, PASS], F32, name="w1_raw%d%d" % (b, a), offset=(2 * b + a) * BLOCK_BYTES)
            rows = w1[a * PASS : (a + 1) * PASS, b * PASS : (b + 1) * PASS]
            nc.sync.dma_start(block[:], rows.rearrange("(p j) c -> p j c", j=PACK))
            return block[:]

        def load_state(n):
            nc.sync.dma_start(state[n][:], gT[n * P : (n + 1) * P, :])

        def load_w3_half(half):
            codes = keep.tile([P, PASSES, N // 2], U32, name="w3_codes%d" % half, align_bytes=64)
            words = w3_words.rearrange("a p c i -> p a (c i)").bitcast(I32)
            nc.sync.dma_start(codes[:].bitcast(I32), words[:, :, half * N // 2 : (half + 1) * N // 2])
            return codes

        def load_w2_half(half):
            codes = keep.tile([P, PASSES, N], U8, name="w2_codes%d" % half, align_bytes=64)
            words = w2_words.rearrange("a p c -> p a c")[:, :, half * N : (half + 1) * N]
            nc.sync.dma_start(codes[:].bitcast(I32), words.bitcast(I32))
            return codes

        tab_plane = zeroed_plane([P, T], "tab_plane")
        w3_plane = zeroed_plane([P, PASSES, N], "w3_plane")
        w2_plane = zeroed_plane([P, PASSES, N], "w2_plane")
        state = [keep.tile([P, T], F32, name="state%d" % n) for n in range(ROW_TILES)]

        gain_rows = keep.tile([P, PASS], F32, name="gain_rows")
        nc.gpsimd.memset(gain_rows[:], 0.0)
        identity = keep.tile([P, P], F32, name="identity")
        make_identity(nc, identity[:])

        tab = [load_table_pass(0)]
        offsets = keep.tile([P, S // PER_COLUMN], U16, name="offsets")
        nc.sync.dma_start(offsets[:], offs)
        load_table_scales((0, 1))
        w1_raw = {(0, 0): load_w1_block(0, 0)}
        load_table_scales((2, 3))
        w1_raw[0, 1] = load_w1_block(0, 1)
        nc.sync.dma_start(gain_rows[:PASSES, :], gain.rearrange("(b c) -> b c", b=PASSES))
        tab.append(load_table_pass(1))
        load_state(2)
        w1_raw[1, 0] = load_w1_block(1, 0)
        w1_raw[1, 1] = load_w1_block(1, 1)
        load_state(3)
        load_weight_scales((0, 1))
        load_state(1)
        load_weight_scales((2, 3))
        w3_codes = [load_w3_half(0)]
        w2_codes = [load_w2_half(0)]
        load_state(0)
        w3_codes.append(load_w3_half(1))
        w2_codes.append(load_w2_half(1))

        def listed(first, count):
            return offsets[:, first // PER_COLUMN : (first + count) // PER_COLUMN]

        def columns(s, first=0, count=WIDTH):
            return slice(s * WIDTH + first, s * WIDTH + first + count)

        turned = bank("turned", PACK)
        for t in range(PACK):
            nc.tensor.transpose(turned[:, t, :], gain_rows[:, t:PASS:PACK], identity[:])
        gains = keep.tile([P, PASSES, PACK], F32, name="gains")
        nc.scalar.copy(gains[:], turned[:, :, :PASSES].rearrange("p t b -> p b t"))

        w1_grouped, w1_codes, w1_plane = {}, {}, {}

        def cast_w1(b, a, u, tile, cast):
            grouped = tile([P, 2 * PASS], BF16, "w1_grouped")
            src = w1_raw[b, a].rearrange("p j (m t) -> p m j t", t=PACK)
            cast(grouped[:, :].rearrange("p (t m j) -> p m j t", t=2, j=PACK), src[:, :, :, 2 * u : 2 * u + 2])
            w1_grouped[b, a, u] = grouped

        def vector_cast(b, a, u, tile=from_vector):
            cast_w1(b, a, u, tile, nc.vector.tensor_copy)

        def scalar_cast(b, a, u):
            cast_w1(b, a, u, from_scalar, nc.scalar.copy)

        def quantise_w1(b, a, u):
            w1_codes[b, a, u] = from_vector([P, 2 * P], U32, "w1_codes")
            w1_plane[b, a, u] = keep.tile([P, 2 * P], U8, name="w1_plane%d%d%d" % (b, a, u), align_bytes=64)
            nc.vector.quantize_mx(w1_codes[b, a, u][:].bitcast(E4M3), w1_plane[b, a, u][:], w1_grouped[b, a, u][:, :])

        def gathered(window, dtype, name):
            tile = from_vector([P, S], dtype, name)
            nc.vector.tensor_copy(tile[:], window[:].indirect(offsets[:]))
            return tile

        v_codes = [gathered(tab[0], U32, "v_codes")]
        v_plane = gathered(tab_plane, U8, "v_plane")
        for u in range(2):
            scalar_cast(0, 0, u)
        for u in range(2):
            quantise_w1(0, 0, u)
        scalar_cast(0, 1, 0)
        vector_cast(0, 1, 1)
        for u in range(2):
            quantise_w1(0, 1, u)
        v_codes.append(from_vector([P, S], U32, "v_codes"))
        for first, count in ((0, WIDTH), (WIDTH, WIDTH), (2 * WIDTH, 2 * WIDTH)):
            nc.vector.tensor_copy(v_codes[1][:, first : first + count], tab[1][:].indirect(listed(first, count)))

        def times_table(acc, operands, passes):
            order = [(a, i) for a in passes for i in range(len(operands))]
            for a, i in order:
                codes, planes, cols = operands[i]
                nc.tensor.matmul_mx(
                    acc[:, i, :],
                    lhsT=codes[a].bitcast(E4M3),
                    lhsT_scale=planes[a],
                    rhs=v_codes[a][:, cols].bitcast(E4M3),
                    rhs_scale=v_plane[TAB_PLANE_ROW + 4 * a :, cols],
                    start=(a, i) == order[0],
                    stop=(a, i) == order[-1],
                )

        pre, act, h_rows, h_grouped, h_codes, h_plane = {}, {}, {}, {}, {}, {}
        d_acc, y_acc, linear, nonlinear, drift, picked, fresh = {}, {}, {}, {}, {}, {}, {}

        def w1_operand(b, t, cols):
            u, i = divmod(t, 2)
            return (
                [w1_codes[b, a, u][:, i * P : (i + 1) * P] for a in range(PASSES)],
                [w1_plane[b, a, u][:, i * P : (i + 1) * P] for a in range(PASSES)],
                cols,
            )

        def passes_of(s):
            return range(PASSES) if s == 0 else range(PASSES - 1, -1, -1)

        def sums_by_rows(s, b, halves=(0, 1)):
            for u in halves:
                pre[s, b, u] = bank("pre", 2)
                times_table(pre[s, b, u], [w1_operand(b, 2 * u + i, columns(s)) for i in range(2)], passes_of(s))

        def sums_by_columns(s, b):
            for c in range(2):
                pre[s, b, c] = bank("pre", PACK)
                times_table(pre[s, b, c], [w1_operand(b, t, columns(s, c * P, P)) for t in range(PACK)], passes_of(s))

        def linear_sums(s, pair):
            d_acc[s, pair] = bank("d_acc", 2)
            times_table(
                d_acc[s, pair],
                [
                    (
                        [w3_codes[pair][:, a, i * P : (i + 1) * P] for a in range(PASSES)],
                        [w3_plane[W3_PLANE_ROW:, a, (2 * pair + i) * P : (2 * pair + i + 1) * P] for a in range(PASSES)],
                        columns(s),
                    )
                    for i in range(2)
                ],
                range(PASSES),
            )

        def nonlinear_sums(s, rows):
            acc = bank("y_acc", 2)
            order = [(b, n) for b in range(PASSES) for n in rows]
            for b, n in order:
                nc.tensor.matmul_mx(
                    acc[:, n - rows[0], :],
                    lhsT=w2_codes[n // 2][:, b, 2 * (n % 2) * P : 2 * (n % 2 + 1) * P].bitcast(E2M1),
                    lhsT_scale=w2_plane[:, b, n * P : (n + 1) * P],
                    rhs=h_codes[s, b].bitcast(E4M3),
                    rhs_scale=h_plane[s, b][:],
                    start=(b, n) == order[0],
                    stop=(b, n) == order[-1],
                )
            y_acc[s, rows] = acc

        def squash(s, b, halves=(0, 1)):
            for u in halves:
                act[s, b, u] = from_scalar([P, 2, WIDTH], F32, "act")
                nc.scalar.activation(act[s, b, u][:], pre[s, b, u][:], TANH)

        def squash_interleaved(s, b):
            act[s, b] = from_scalar([P, WIDTH, PACK], F32, "act")
            for c in range(2):
                nc.scalar.activation(
                    act[s, b][:, c * P : (c + 1) * P, :], pre[s, b, c][:].rearrange("p t c -> p c t"), TANH
                )

        def apply_gains(s, b, tile=from_scalar):
            h_rows[s, b] = tile([P, PACK, WIDTH], BF16, "h_rows")
            for t in range(PACK):
                nc.scalar.activation(
                    h_rows[s, b][:, t, :], act[s, b, t // 2][:, t % 2, :], COPY, scale=gains[:, b, t : t + 1]
                )

        def interleave(s, b, tile=from_scalar):
            grouped = tile([P, WIDTH * PACK], BF16, "h_grouped")
            h_grouped[s, b] = [grouped[:]]
            nc.scalar.copy(
                grouped[:].rearrange("p (c i t) -> p c t i", i=4, t=PACK),
                h_rows[s, b][:].rearrange("p t (c i) -> p c t i", i=4),
            )

        def copy_linear(s, pair, tile=from_scalar):
            both = tile([P, 2, WIDTH], F32, "linear")
            nc.scalar.copy(both[:], d_acc[s, pair][:])
            linear[s, (2 * pair, 2 * pair + 1)] = both[:]
            for i in range(2):
                linear[s, (2 * pair + i,)] = both[:, i : i + 1, :]

        def copy_nonlinear(s, rows, tile=from_scalar):
            copy = tile([P, len(rows), WIDTH], F32, "nonlinear")
            nc.scalar.copy(copy[:], y_acc[s, rows][:, : len(rows), :])
            nonlinear[s, rows] = copy[:]
            for i, n in enumerate(rows):
                nonlinear[s, (n,)] = copy[:, i : i + 1, :]

        def gains_and_round(s, b, tile, first=0, count=WIDTH):
            grouped = tile([P, count * PACK], BF16, "h_grouped")
            h_grouped.setdefault((s, b), []).append(grouped[:])
            nc.gpsimd.tensor_tensor(
                grouped[:].rearrange("p (c t) -> p c t", t=PACK),
                act[s, b][:, first : first + count, :],
                gains[:, b : b + 1, :].to_broadcast([P, count, PACK]),
                MULT,
            )

        def multiply(s, rows, tile=from_gpsimd):
            drift[s, rows] = tile([P, len(rows), WIDTH], F32, "drift")[:]
            nc.gpsimd.tensor_tensor(drift[s, rows], nonlinear[s, rows], linear[s, rows], MULT)

        def add_state(s, rows, into):
            nc.gpsimd.tensor_tensor(into, drift[s, rows], picked[s, rows], ADD)
            for i, n in enumerate(rows):
                fresh[s, n] = into[:, i, :]

        def fresh_tile(rows, tile=from_gpsimd):
            return tile([P, len(rows), WIDTH], F32, "fresh")[:]

        def pick(n, into, first_slice, start=0, stop=None):
            part = into[:, n % 2, start:stop]
            nc.vector.tensor_copy(part, state[n][:].indirect(listed(first_slice * WIDTH + start, part.shape[1])))

        def picked_tile(rows, first_slice, slices, tile):
            both = tile([P, 2, slices * WIDTH], F32, "picked")
            for s in range(slices):
                picked[first_slice + s, rows] = both[:, :, columns(s)]
                for i, n in enumerate(rows):
                    picked[first_slice + s, (n,)] = both[:, i : i + 1, columns(s)]
            return both

        def quantise_h(s, blocks, tile):
            codes = tile([P, len(blocks) * WIDTH], U32, "h_codes")
            for i, b in enumerate(blocks):
                h_codes[s, b] = codes[:, i * WIDTH : (i + 1) * WIDTH]
                h_plane[s, b] = keep.tile([P, WIDTH], U8, name="h_plane%d_%d" % (s, b), align_bytes=64)
                first = 0
                for piece in h_grouped[s, b]:
                    cols = slice(first, first + piece.shape[1] // PACK)
                    nc.vector.quantize_mx(h_codes[s, b][:, cols].bitcast(E4M3), h_plane[s, b][:, cols], piece)
                    first = cols.stop

        def multiply_from_bank(s, rows):
            drift[s, rows] = from_vector([P, len(rows), WIDTH], F32, "drift")[:]
            nc.vector.tensor_tensor(drift[s, rows], y_acc[s, rows][:, : len(rows), :], linear[s, rows], MULT)

        def scatter(n, first, values):
            nc.vector.tensor_copy(state[n][:].indirect(listed(first, values.shape[1])), values)

        def put_back(s, n):
            scatter(n, s * WIDTH, fresh[s, n])

        def over_rows(s):
            return over(h_rows[s, 1][:].rearrange("p t c -> p (t c)"))

        low, high = (0, 1), (2, 3)
        in_turn = handed("in_turn")

        first_h = handed("first_h")
        sums_by_columns(0, 0)
        sums_by_rows(1, 0)
        sums_by_columns(2, 0)
        sums_by_rows(3, 0, (0,))
        squash_interleaved(0, 0)
        gains_and_round(0, 0, first_h)
        squash(1, 0)
        apply_gains(1, 0)
        squash(3, 0, (0,))
        interleave(1, 0)
        scalar_cast(1, 1, 1)
        squash_interleaved(2, 0)

        high_all = picked_tile(high, 0, SLICES, handed("high_all"))
        pick(2, high_all, 0)
        vector_cast(1, 0, 0)
        vector_cast(1, 0, 1)
        quantise_w1(1, 0, 0)
        vector_cast(1, 1, 0, lambda shape, dtype, name: high_all[:, 1, :PASS].bitcast(dtype))
        quantise_w1(1, 0, 1)
        quantise_w1(1, 1, 0)
        quantise_w1(1, 1, 1)
        quantise_h(0, (0,), from_vector)
        quantise_h(1, (0,), from_vector)
        gains_and_round(2, 0, over(h_grouped[1, 0][0]), 0, P)

        sums_by_columns(0, 1)
        sums_by_rows(1, 1)
        squash_interleaved(0, 1)
        gains_and_round(0, 1, first_h)
        pick(3, high_all, 0)
        low_middle = picked_tile(low, 1, 2, from_vector)
        low_last = picked_tile(low, 3, 1, from_vector)
        pick(1, low_middle, 1)
        pick(1, low_last, 3)
        quantise_h(0, (1,), from_vector)
        gains_and_round(2, 0, first_h, P, P)
        low_first = picked_tile(low, 0, 1, handed("low_first"))
        pick(1, low_first, 0)

        sums_by_rows(2, 1)
        linear_sums(0, 0)
        nonlinear_sums(0, low)
        linear_sums(1, 0)
        sums_by_rows(3, 0, (1,))
        linear_sums(0, 1)
        nonlinear_sums(0, high)
        linear_sums(1, 1)
        squash(1, 1)
        apply_gains(1, 1)
        squash(2, 1)
        copy_linear(0, 0)
        interleave(1, 1)
        copy_linear(0, 1)
        copy_nonlinear(0, high)
        apply_gains(2, 1)

        multiply_from_bank(0, low)
        pick(0, low_first, 0)
        pick(0, low_middle, 1)
        pick(0, low_last, 3)
        add_state(0, low, fresh_tile(low, over_rows(1)))
        quantise_h(1, (1,), handed("low_first"))
        nonlinear_sums(1, low)
        nonlinear_sums(1, high)
        copy_linear(1, 0)
        copy_nonlinear(1, low)
        interleave(2, 1)
        copy_linear(1, 1)
        copy_nonlinear(1, high)
        multiply(0, high, over(h_grouped[1, 1][0]))
        add_state(0, high, fresh_tile(high))
        for n in range(ROW_TILES):
            put_back(0, n)
        multiply(1, low, in_turn)
        add_state(1, low, fresh_tile(low, over_rows(2)))

        quantise_h(2, (0, 1), in_turn)
        multiply(1, high, over(h_grouped[2, 1][0]))
        add_state(1, high, fresh_tile(high))
        for n in range(ROW_TILES):
            put_back(1, n)
        linear_sums(2, 0)
        sums_by_rows(3, 1)
        linear_sums(2, 1)
        nonlinear_sums(2, low)
        nonlinear_sums(2, high)
        linear_sums(3, 0)
        linear_sums(3, 1)
        squash(3, 0, (1,))
        apply_gains(3, 0)
        copy_linear(2, 0)
        interleave(3, 0)
        squash(3, 1)
        copy_nonlinear(2, low)
        apply_gains(3, 1)
        copy_linear(2, 1)
        interleave(3, 1)
        copy_nonlinear(2, high)
        copy_linear(3, 0)
        copy_linear(3, 1)
        multiply(2, low, handed("next_turn"))
        add_state(2, low, fresh_tile(low, over_rows(3)))

        quantise_h(3, (0, 1), handed("next_turn"))
        multiply(2, (2,), over(h_grouped[3, 1][0]))
        add_state(2, (2,), fresh_tile((2,)))
        for n in range(ROW_TILES - 1):
            put_back(2, n)
        for rows in (low, high):
            nonlinear_sums(3, rows)
            copy_nonlinear(3, rows)
        multiply(3, low)
        for n in low:
            drift[3, (n,)] = drift[3, low][:, n : n + 1, :]
            add_state(3, (n,), fresh_tile((n,)))
            put_back(3, n)
        wide = from_gpsimd([P, 2, 2 * WIDTH], F32, "drift")
        nc.gpsimd.tensor_tensor(wide[:, :, WIDTH:], nonlinear[3, high], linear[3, high], MULT)
        nc.gpsimd.tensor_tensor(wide[:, 1:, :WIDTH], nonlinear[2, (3,)], linear[2, (3,)], MULT)
        for n, first in ((2, 3 * WIDTH), (3, 2 * WIDTH)):
            nc.vector.tensor_tensor(
                state[n][:].indirect(listed(first, S - first)),
                high_all[:, n % 2, first:],
                wide[:, n % 2, first - 2 * WIDTH :],
                ADD,
            )

        for n in range(ROW_TILES - 1):
            nc.sync.dma_start(out[n * P : (n + 1) * P, :], state[n][:])
        n = ROW_TILES - 1
        nc.sync.dma_start(out[n * P :, : T // 2], state[n][:, : T // 2])
        nc.scalar.dma_start(out[n * P :, T // 2 :], state[n][:, T // 2 :])
